import numpy as np, ml_dtypes
CORES = [51,54,179,182]
N = 4
BF = ml_dtypes.bfloat16
W, L, S, H, CP = 3072, 1024, 4, 2, 64
def parts(rng):
    x = np.minimum((128 * rng.random((N, 8, 16, W), dtype=np.float32) * (0.25 + 0.75 * rng.random((N, 8, 1, W), dtype=np.float32))).astype(np.int64), 127)
    share = np.zeros((N, 8, W)) + rng.choice(np.array([0.01, 0.03, 0.06]), (N, 8, 1))
    for t in range(S):
        B = W - 256 * (t + 1)
        share[:, :, B:B + 256] = rng.choice(np.array([0.3, 0.6, 0.9]) if t == 0 else np.array([0.1, 0.3, 0.5]), (N, 8, 1))
    mk = (rng.random((N, 8, W)) < share).astype(np.int64)
    return x, mk, rng.integers(0, 4096, (N, 8, 16, L)), rng.integers(0, 4096, (N, 8, S * 256)), rng.integers(0, 256, (N, 8, 16)), rng.choice(np.array([1, 8, 20, 40, 80]), (N, 8))
def pack(x, mk, oc, dl, wt, th):
    return {"xc": x.reshape(N, 128, W).astype(np.float32).astype(BF), "mk": mk.astype(np.float32).astype(BF), "oc": oc.reshape(N, 128, L).astype(np.int32),
            "dl": dl.astype(np.int32), "wt": wt.reshape(N, 128, 1).astype(np.int32), "th": th.reshape(N, 8, 1).astype(np.int32)}
def setup_inputs(rng):
    return pack(*parts(rng))
def setup_inputs_spread(rng):
    x, mk, oc, dl, wt, th = parts(rng)
    x = np.minimum((np.exp2(8 * rng.random((N, 8, 1, W))) * rng.random((N, 8, 16, W))).astype(np.int64), 127)
    mk = (rng.random((N, 8, W)) < np.exp2(-6 * rng.random((N, 8, 1)))).astype(np.int64)
    oc = np.minimum((4096 * rng.random((N, 8, 16, L)) ** 3).astype(np.int64), 4095)
    flip = rng.integers(0, 2, (N, 8, 1, 1)); oc = np.where(flip == 1, 4095 - oc, oc)
    wt = np.minimum((np.exp2(8 * rng.random((N, 8, 16))) - 1).astype(np.int64), 255)
    th = np.minimum(np.exp2(11 * rng.random((N, 8))).astype(np.int64), 2032)
    th[:, rng.integers(0, 8)] = 1
    return pack(x, mk, oc, dl, wt, th)
def setup_inputs_ends(rng):
    x, mk, oc, dl, wt, th = parts(rng)
    kind = rng.integers(0, 3, (N, 8, 1, W)); x = 127 * np.where(kind == 2, rng.integers(0, 2, (N, 8, 16, W)), kind)
    mk = rng.integers(0, 2, (N, 8, W))
    E = np.array([0] + [W - 256 * (t + 1) - 1 for t in range(S)])
    c = rng.integers(0, 3, (N, 8)); c[:, 0] = 2; c[N - 1, 7] = 1; c[N - 2, 7] = 0; c[0, 5] = 2
    for q in range(N):
        for g in range(8):
            x[q, g][:, E] = 127 * rng.integers(0, 2, (16, len(E))) if c[q, g] == 2 else 127 * c[q, g]
    x[:, :, :, W - 1] = 127; mk[:, :, W - 1] = 1; mk[N - 1, 7, E] = 1
    oc = 4095 * rng.integers(0, 2, (N, 8, 16, L)); oc[:, :, :15, ::7] = 0; oc[:, :, 15, ::7] = 4095; oc[:, :, :, L - 1] = 4095
    dl = 4095 * rng.integers(0, 2, dl.shape)
    wt = 255 * rng.integers(0, 2, wt.shape); wt[N - 1, 7] = 255; wt[0, 5] = 0; wt[:, 2, 0] = 0; wt[:, 2, 15] = 255
    th = np.where(rng.integers(0, 2, (N, 8)) == 1, 2032, 1); th[:, 0] = 1; th[:, 1] = 2032; th[N - 2, 7] = 2032
    return pack(x, mk, oc, dl, wt, th)
def setup_inputs_corners(rng):
    x, mk, oc, dl, wt, th = parts(rng); B = W - 256
    u = np.arange(4096); lv = ((u * u >> 5) + 37 * u) & (L - 1); top = int(np.argmax(lv)); place = int(lv[top])
    for q in range(N):
        for g in range(8):
            n = int((0, 1, CP - 1, CP, CP + 1, 256)[int(rng.integers(0, 6))])
            if q == 0: n = (CP, CP + 1, 256, CP, CP + 1, 256, CP, CP)[g]
            if q == 1: n = 0
            if q == 2: n = 63 if g == 7 else 0
            if q == 3: n = (CP - 1, 1, 0, CP, CP + 1, 256, CP - 1, CP)[g]
            o = rng.permutation(256); e = B + o[:n]; rest = B + o[n:]; T = (1, 127)[int(rng.integers(0, 2))]; th[q, g] = T
            xg = x[q, g]; xg[15, :B] = 0; xg[15, e] = 127; xg[:15, e[::2]] = 0; xg[:, rest] = 0
            if T == 127: xg[15, rest[::2]] = 126
            if g == 4: mk[q, g, :B] = 0
            if g == 6: mk[q, g, :B] = 1
            mk[q, g, e] = 1; mk[q, g, rest] = rng.integers(0, 2, 256 - n)
            if g == 0: wt[q, g] = 0
            if g == 1: wt[q, g] = 255
            if g == 2: oc[q, g] = 4095 * rng.integers(0, 2, (16, L))
            if g == 5: oc[q, g] = oc[q, g, :1].copy()
            if g % 4 == 3:
                wt[q, g] = 0; wt[q, g, 0] = 1; wt[q, g, 1] = 128
                xg[0, e[1::2]] = top & 127; xg[1, e[1::2]] = top >> 7
                oc[q, g, :, place] = 4095 * rng.integers(0, 2, 16); oc[q, g, :, 0] = 4095 * rng.integers(0, 2, 16)
    return pack(x, mk, oc, dl, wt, th)
def setup_inputs_crowd(rng):
    x, mk, oc, dl, wt, th = parts(rng); s = int(rng.integers(0, 8)); low = W - 256 * S
    for q in range(N):
        for g in range(8):
            kind = (g + s) % 8; xg = x[q, g]; odd = [W - 256 * (t + 1) + int(rng.integers(0, 256)) for t in range(S)]
            if kind == 7: continue
            mk[q, g, low:] = 1; th[q, g] = 1
            if kind in (0, 1, 4):
                keep = xg[:, odd].copy(); xg[:, low:] = xg[:, W - 1:W].copy()
                if kind == 1: xg[:, odd] = keep
                if kind == 4: mk[q, g, odd] = 0
            if kind == 2:
                three = xg[:, W - 3:].copy(); xg[:, low:] = three[:, rng.integers(0, 3, 256 * S)]
            if kind == 3: oc[q, g] = int(rng.integers(0, 4096))
            if kind in (5, 6): wt[q, g] = 0
            if kind == 6:
                wt[q, g, 15] = 1; xg[15, :] = 0; xg[15, odd] = 64
    return pack(x, mk, oc, dl, wt, th)
def setup_inputs_edges(rng):
    x, mk, oc, dl, wt, th = parts(rng); B = W - 256; low = W - 256 * S
    p = [int(a) for a in rng.permutation(8)]; z = p[0]; e = int(rng.integers(0, N)); s = (e + 1) % N
    u = np.arange(4096); lv = ((u * u >> 5) + 37 * u) & (L - 1); pl, first = np.unique(lv, return_index=True); first = first[pl >= 64]
    x[:, z, :, low:] = rng.integers(64, 128, (N, 16, 256 * S)); x[:, z, :, 0] = 0; x[:, z, :, W // 8:W // 2] = 0
    mk[:, z, W // 8:W // 2] = 0; oc[:, z, :, :64] = 0; wt[:, z] = 0
    for t in range(S):
        Bt = W - 256 * (t + 1); c = W // 2 - 1 - t
        x[:, z, :, c] = 127; dl[:, z, t * 256:(t + 1) * 256] = -((-c * 4096) // Bt); mk[:, z, Bt + 255] = 1
    for q in range(N):
        for g, pair in ((p[1], (257, 385)), (p[2], (513, 1001))):
            T = pair[int(rng.integers(0, 2))]; th[q, g] = T
            x[q, g, 4:, :B] = 0; x[q, g, :, B:] = 0; mk[q, g, B:] = rng.integers(0, 2, 256)
            o = B + rng.permutation(256)[:40]; tot = T - (np.arange(40) & 1); dv = rng.integers(-20, 21, (6, 40))
            v = np.concatenate([dv, -dv]) + tot // 12; v[11] += tot % 12
            x[q, g][4:, o] = v; mk[q, g, o] = 1
        g = p[3]; two = [int(a) for a in rng.permutation(low)[:2]]
        for k, c in ((0, two[0]), (int(rng.integers(1, 16)), two[1])):
            oc[q, g, k] = -((-c * 4096) // B); x[q, g, :, c] = 127; mk[q, g, c] = 1
        x[q, g, int(rng.integers(0, 16)), two[0]] = 126 * int(rng.integers(0, 2)); x[q, g, :, B::2] = 127; mk[q, g, B::2] = 1
        g = p[4]; us = rng.permutation(first)[:256]
        wt[q, g] = 0; wt[q, g, 0] = 1; wt[q, g, 1] = 128; x[q, g, :2, :B] = 0
        x[q, g, 0, B:] = us & 127; x[q, g, 1, B:] = us >> 7; mk[q, g, B:] = 1
        oc[q, g] = oc[q, g] & 4094; dl[q, g, :256] = dl[q, g, :256] | 1
    mk[s, p[:1] + p[3:], B:] = 0
    x[e, :, :, W - 512:W - 256] = 0
    return pack(x, mk, oc, dl, wt, th)
def check_inputs(d):
    bad = []
    for k, lo, hi in (("xc", 0, 127), ("mk", 0, 1), ("oc", 0, 4095), ("dl", 0, 4095), ("wt", 0, 255), ("th", 1, 2032)):
        v = np.asarray(d[k]).astype(np.float64)
        if not (np.min(v) >= lo and np.max(v) <= hi): bad.append("range of " + k)
        elif np.any(v != np.floor(v)): bad.append("whole numbers of " + k)
    return bad
def hop(y, x, m, o, w, A, B):
    n = y.shape[2]
    u = np.add.reduce(w[:, :, None] * y, axis=1) & 4095
    l = ((u * u >> 5) + 37 * u + A) & (L - 1)
    c = (np.take_along_axis(o, l[:, None, :], 2) * B) >> 12
    cc = c.reshape(8, 16 * n)
    v = np.take_along_axis(x, cc[:, None, :], 2).reshape(8, 16, 16, n)
    s = np.add.reduce(np.minimum(v, y[:, :, None, :]), axis=1) + 256 * np.take_along_axis(m, cc, 1).reshape(8, 16, n)
    k = np.argmax(s, axis=1)
    return l, s, np.take_along_axis(c, k[:, None, :], 1)[:, 0]
def reference(xc, mk, oc, dl, wt, th):
    x = xc.astype(np.float32).astype(np.int64).reshape(N, 8, 16, W); m = mk.astype(np.float32).astype(np.int64).reshape(N, 8, W)
    o = oc.astype(np.int64).reshape(N, 8, 16, L); w = wt.astype(np.int64).reshape(N, 8, 16); d = dl.astype(np.int64); lim = th.astype(np.int64).reshape(N, 8, 1)
    A = [0] * N; ya = np.full((N, 8, S, H, 256), -1, np.int64)
    for t in range(S):
        B = W - 256 * (t + 1)
        box = np.zeros((N, 8, 16, CP), np.int64); full = np.zeros((N, 8, CP), bool)
        for r in range(N):
            y = x[r, :, :, B:B + 256]; live = m[r, :, B:B + 256] == 1
            for h in range(H):
                l, s, a = hop(y, x[r], m[r], o[r], w[r], A[r], B)
                ya[r, :, t, h] = np.where(live, a, -1)
                for g in range(8): m[r, g, a[g][live[g]]] = 1
                y = np.maximum(y - np.take_along_axis(x[r], a[:, None, :], 2), 0)
            k = np.argmin(s, axis=1)
            go = live & (np.add.reduce(y, axis=1) >= lim[r])
            for g in range(8):
                i = np.flatnonzero(live[g]); i = i[np.unique(l[g, i], return_index=True)[1]]
                o[r, g, k[g, i], l[g, i]] = d[r, g, t * 256 + i]
                j = np.flatnonzero(go[g])[:CP]
                box[r, g, :, :len(j)] = y[g][:, j]; full[r, g, :len(j)] = True
        for r in range(N):
            q = (r - 1 - t % (N - 1)) % N
            l, s, a = hop(box[q], x[r], m[r], o[r], w[r], A[r], B)
            for g in range(8): m[r, g, a[g][full[q, g]]] = 1
            A[r] = int(np.count_nonzero(full[q])) & 63
    return {"ya": ya.reshape(N, 8, S * H * 256).astype(np.float32), "ym": m.astype(np.float32).astype(BF), "yo": o.reshape(N, 128, L).astype(np.float32)}

@@ -1,0 +1,652 @@
+import numpy as np
+from concourse.mybir import AluOpType, ActivationFunctionType
+
+W, L, NS = 3072, 1024, 4
+BF, F32, I32, U16 = "bfloat16", "float32", "int32", "uint16"
+_SB = {
+    "x": (W, BF), "oci": (L, I32), "tab": (L + 16, F32), "win": (W + 16, F32), "dgw": (L, BF),
+    "vm": (4096, BF), "mg": (4096, BF), "yr0": (4096, BF), "yr1": (4096, BF), "yrh": (4096, BF),
+    "vmr": (1024, BF), "mgr": (1024, BF), "yrr": (1024, BF),
+    "c0": (256, U16), "c1": (256, U16), "cr": (64, U16),
+    "pi": (2, I32), "cols": (40, F32), "wti": (1, I32), "thi": (1, I32), "thf": (1, F32), "thc": (1, F32),
+    "colf": (256, F32), "rr": (256, F32), "hi4": (256, F32), "lo64": (256, F32), "hi16": (128, F32), "comb": (256, BF),
+    "mkb": (W, BF), "m8": (128, BF), "ymb": (2064, BF), "ones": (16, BF),
+    "biasb": (12, F32), "slotc": (64, F32),
+    "zf": (144, BF), "zm": (144, BF), "zw": (144, BF), "zd": (144, BF), "zl": (144, BF), "zs": (144, BF), "zv": (144, BF),
+    "bo": (128, BF), "bd": (128, BF), "bl": (128, BF), "bz": (128, BF), "by": (128, BF), "bn": (128, BF), "bt": (128, BF),
+    "tri": (128, BF), "idn": (128, BF), "idp": (128, BF), "e0": (128, BF), "g8": (128, F32), "zero": (128, BF),
+    "kl0": (128, BF), "kl1": (128, BF), "klr": (128, BF), "kr": (256, BF),
+    "kseg": (256, BF), "kdg": (256, BF), "kne": (256, BF), "rbig": (256, BF), "rmin": (256, BF),
+    "lp": (16, U16), "qp": (16, F32), "y0p": (256, BF), "lf": (16, U16), "l2": (16, U16), "lr": (16, U16), "ct": (16, BF), "oh": (16, F32), "idf": (128, F32), "idg": (128, F32),
+    "dli": (64, I32), "dlc": (64, F32), "dl8": (L, F32), "dln": (256, F32), "dlp": (256, F32),
+    "base": (64, I32), "ui": (64, I32), "uu": (64, I32), "sq": (64, I32), "t32": (64, I32), "zz": (64, I32), "li": (64, I32),
+    "l0": (16, U16), "l1": (32, U16), "lv": (4, U16), "zb": (16, I32), "lb": (16, I32),
+    "ai": (2, I32), "ac": (8, F32),
+    "rs": (256, F32), "ji": (16, I32), "ja": (16, I32), "j16": (16, U16), "jr": (4, U16),
+    "rm": (256, F32), "ki": (16, I32), "ka": (16, I32), "k16": (16, U16),
+    "y0f": (256, BF), "y1n": (256, BF), "y1p": (256, BF), "y1r": (256, BF), "y2n": (256, BF), "lvn": (256, BF), "val": (64, BF),
+    "ad": (256, BF), "adf": (256, F32), "ld": (256, BF), "nn": (256, F32), "t1": (256, F32), "t2": (256, F32),
+    "adr": (64, BF), "adfr": (64, F32),
+    "propa": (256, F32), "eqa": (256, BF), "cna": (256, BF), "vva": (16, F32), "offa": (32, U16),
+    "propn": (256, F32), "eqn": (256, BF), "cnn": (256, BF), "vvn": (16, F32), "offn": (32, U16),
+    "zr": (256, F32), "yab": (2048, F32),
+    "rdy": (16, BF), "pre": (16, BF), "rp": (16, BF), "slot": (16, U16),
+    "snd0": (528, BF), "snd1": (528, BF), "snd2": (528, BF), "snd3": (528, BF),
+    "land0": (80, BF), "land1": (80, BF), "land2": (80, BF), "land3": (80, BF),
+}
+_PS = ["pk", "pr", "pa", "pb", "pu", "psm", "prk", "pz"]
+_AT, _END = {}, {}
+for _k, (_n, _d) in _SB.items():
+    _b = "pool_" + _d if _n <= 144 else _k
+    _AT[_k] = (_b, _END.get(_b, (0, _d))[0])
+    _END[_b] = (_AT[_k][1] + -(-_n // 16) * 16, _d)
+SCRATCH = {k: ("sbuf", [128, v[0]], v[1]) for k, v in _END.items()}
+SCRATCH.update({k: ("psum", [128, 512], F32) for k in _PS})
+NDMA = 20
+SEMAPHORES = ["sV", "sS", "sP", "sG", "sent"] + ["arr%d" % t for t in range(NS)] + ["d%d" % i for i in range(NDMA)]
+
+SILU_ONE = 1.2784645427610738
+CENTER = 32 * 148 * 1024
+NENG = 8
+CFG = dict(
+    f0=(2, 2, 2, 2, 2, 2, 2, 1, 1), m0=(2, 2, 1, 2, 1, 1, 1, 2, 1, 1, -2), m00=(2, 2, 2, 2, 2, 2, 2, 1, 1),
+    f1=(2, 3, 2, 1, 3, 2, 2, 1), m1=(2, 3, 1, 2, 3, -1, 3, 1), rch=(8, 4, 4),
+    yh=("GGGGGGGGSSSSVVVV", "GGGGGGSSVVVVVVVV"), yrr="VVVVSSSSSSSSSSSS", y00="VVVVVVVVVGGGSSSS",
+    gather=1.56, scatter=3.8, pe=0.5, wake=90.0, dma=2000.0, remote=2800.0, look=0.3, waw=True, passes=300, seed=1, shift=300.0, share=0.05,
+)
+
+
+def rank_program(g, core, T, topo):
+    rank = T.rank_of(core)
+    if rank is None:
+        return
+    A_ = AluOpType
+    AF = ActivationFunctionType
+    nrank = len(T.cores)
+    ops = []
+
+    def a(name, c0=0, c1=None, st=1, p=None):
+        n = 512 if name in _PS else _SB[name][0]
+        c1 = n if c1 is None else c1
+        ps = slice(0, 128) if p is None else p
+        b, o = (name, 0) if name in _PS else _AT[name]
+        ap = T[b][ps, o + c0:o + c1] if st == 1 else T[b][ps, o + c0:o + c1:st]
+        return (ap, [(name, c0, c1, st)])
+
+    def ind(w, o):
+        return (w[0].indirect(o[0]), w[1], o[1])
+
+    def val(s):
+        return s[0] if isinstance(s, tuple) else s
+
+    def num(s):
+        f = s[-1][0]
+        return len(range(f[1], f[2], f[3])) * (16 if len(s) == 3 else 1)
+
+    def narrow(*aps):
+        return all(s[1][0][0] not in _PS and _SB[s[1][0][0]][1] in (BF, U16) for s in aps)
+
+    def span(o, i, per):
+        if len(o) == 3:
+            return 55 + num(o) * CFG["scatter"]
+        if len(i) == 3:
+            return 55 + num(i) * CFG["gather"]
+        return max(64, num(o) * per)
+
+    def rec(q, fn, outs, ins, cost, kind="c", lat=0.0):
+        rd, wr = [], []
+        for o in outs:
+            wr += o[1]
+            if len(o) == 3:
+                rd += o[2]
+        for s in ins:
+            if isinstance(s, tuple):
+                rd += s[1]
+                if len(s) == 3:
+                    rd += s[2]
+        ops.append([q, fn, rd, wr, kind, cost, lat])
+
+    def ts(o, i, s1, s2, o0, o1=None):
+        c = span(o, i, 0.5 if narrow(o, i) else 1)
+        if o1 is None:
+            rec("V", lambda: g.vector.tensor_scalar(o[0], i[0], val(s1), None, o0), [o], [i, s1], c)
+        else:
+            rec("V", lambda: g.vector.tensor_scalar(o[0], i[0], val(s1), val(s2), o0, o1), [o], [i, s1, s2], c)
+
+    def tt(o, i0, i1, op):
+        c = span(o, i0, 1 if i0[1][0][0] in _PS or i1[1][0][0] in _PS else 2)
+        rec("V", lambda: g.vector.tensor_tensor(o[0], i0[0], i1[0], op), [o], [i0, i1], c)
+
+    def cp(o, i):
+        rec("V", lambda: g.vector.tensor_copy(o[0], i[0]), [o], [i], span(o, i, 0.5 if narrow(o, i) else 1))
+
+    def scan(o, d0, d1, o0, o1):
+        rec("V", lambda: g.vector.tensor_tensor_scan(o[0], d0[0], d1[0], 0.0, o0, o1), [o], [d0, d1],
+            span(o, d0, 0.5 if narrow(o, d0, d1) else 1))
+
+    def fill(o, c):
+        rec("V", lambda: g.vector.memset(o[0], c), [o], [], 64)
+
+    def act(o, i, f=AF.Identity, bias=0.0, scale=1.0):
+        if f == AF.Silu:
+            rec("S", lambda: g.scalar.activation(o[0], i[0], f), [o], [i], span(o, i, 1))
+        else:
+            rec("S", lambda: g.scalar.activation(o[0], i[0], f, bias=val(bias), scale=val(scale)), [o], [i, bias, scale], span(o, i, 1))
+
+    def wide(pairs, p=None):
+        for b in range(0, 256, 64):
+            for n, (l, r, at) in enumerate(pairs):
+                mm(a("pu", 256 + b, 320 + b), a(l, p=p), a(r, at + b, at + b + 64, p=p), n == 0, n == len(pairs) - 1)
+
+    def mm(o, l, r, start, stop):
+        c = max(64, num(r)) * CFG["pe"] * (1 if narrow(l) else 4)
+        rec("P", lambda last: g.tensor.matmul(o[0], l[0], r[0], start, last), [o], [l, r], c)
+        ops[-1].append(start)
+
+    def iota(o, pat, base=0, cm=0, flag=True):
+        if flag:
+            rec("G", lambda: g.iota(o[0], pat, base, cm, allow_small_or_imprecise_dtypes=True), [o], [], 130 + 2 * num(o))
+        else:
+            rec("G", lambda: g.iota(o[0], pat, base, cm), [o], [], 130 + 2 * num(o))
+
+    def asel(o, i, pat, cmp, fl, base, cm):
+        rec("G", lambda: g.affine_select(o[0], i[0], pat, cmp, fl, base, cm), [o], [i], 170 + 2 * num(o))
+
+    QO = {"V": g.vector, "S": g.scalar, "P": g.tensor, "G": g, "Y": g.sync}
+
+    def dma(q, o, i, kb):
+        rec(q, lambda: QO[q].dma_start(o[0], i[0]), [o], [i], 1000 if q == "G" else 100, "d", CFG["dma"] + kb * 7)
+
+    def ext(ap):
+        return (ap, [])
+
+    def sel(fam, r):
+        return a(fam, 15 - r, 143 - r)
+
+    g16, k3, p8 = slice(0, 128, 16), slice(0, 3), slice(0, 8)
+    col = lambda j: a("cols", j, j + 1)
+
+    dma("Y", a("x", 2048, W), ext(T.xc[:, 2048:W]), 256)
+    dma("S", a("oci"), ext(T.oc[:]), 512)
+    dma("Y", a("wti"), ext(T.wt[:]), 1)
+    dma("Y", a("mkb", p=p8), ext(T.mk[:]), 48)
+    dma("Y", a("x", 0, 1024), ext(T.xc[:, 0:1024]), 512)
+    dma("S", a("x", 1024, 2048), ext(T.xc[:, 1024:2048]), 512)
+    dma("Y", a("dli"), ext(T.dl[:]), 32)
+    dma("Y", a("thi", p=p8), ext(T.th[:]), 1)
+
+    iota(a("pi", 0, 1), [[0, 1]], 0, 1, False)
+    iota(a("hi4"), [[1, 4], [0, 64]], 128)
+    iota(a("lo64"), [[0, 4], [1, 64]], 128)
+    iota(a("colf"), [[1, 256]])
+    iota(a("rr"), [[0, 16], [1, 16]])
+    iota(a("hi16"), [[16, 8], [0, 16]])
+    iota(a("slotc"), [[1, 4], [4, 16]])
+    P_, R_, G_, G15, IS0, IS1, IS2, DIG, DIG4, WN, R16, RREV, R15, R240, N1, DM, DN = range(17)
+    KA, KB, KC, KD, MW, LW, VW, YW, SC, BI, P16, TA, R8, DY = range(17, 31)
+    ts(a("pi", 1, 2), a("pi", 0, 1), 15, None, A_.bitwise_and)
+    cp(col(P_), a("pi", 0, 1))
+    cp(col(R_), a("pi", 1, 2))
+    for j, v in ((IS0, 0.0), (IS1, 1.0), (IS2, 2.0)):
+        ts(col(j), col(R_), v, None, A_.is_equal)
+    for j, v in ((KA, 128.0), (MW, -1048576.0), (LW, -12416.0 / 4096), (YW, 8192.0), (VW, 4096.0), (BI, SILU_ONE), (KB, -256.0), (KD, 64.0)):
+        ts(col(j), col(R_), 0.0, v, A_.is_equal, A_.mult)
+    for j, m, v in ((R16, 16.0, 0.0), (RREV, -16.0, 240.0), (R15, -1.0, 15.0), (DM, 1.0, float(W)), (DN, 1.0, float(L)), (R240, 1.0, 240.0), (DY, 1.0, 2048.0)):
+        ts(col(j), col(R_), m, v, A_.mult, A_.add)
+    ts(col(SC), col(R_), 0.0, None, A_.not_equal)
+    ts(col(N1), col(R_), 1.0, None, A_.not_equal)
+    tt(col(G_), col(P_), col(R_), A_.subtract)
+    ts(col(G15), col(G_), 15.0, None, A_.add)
+    ts(col(P16), col(P_), 16.0, None, A_.mult)
+    ts(col(TA), col(IS2), 4096.0 * 2304, col(IS1), A_.mult, A_.add)
+    ts(col(KC), col(IS0), 3840.0, col(TA), A_.mult, A_.add)
+    ts(col(DIG4), col(IS1), 64.0, col(IS2), A_.mult, A_.add)
+    ts(col(DIG), col(DIG4), 1.0 / 4096, None, A_.mult)
+    ts(col(WN), a("wti"), -1.0, None, A_.mult)
+    ts(a("hi4"), a("hi4"), col(IS1), None, A_.mult)
+    ts(a("lo64"), a("lo64"), col(IS2), None, A_.mult)
+    ts(a("biasb"), a("colf", 0, 12), col(IS1), 4.0, A_.mult, A_.mult)
+    tt(a("comb"), a("hi4"), a("lo64"), A_.add)
+    fill(a("win", W, W + 16), 0.0)
+    ts(a("m8"), a("colf", 0, 128), col(P16), None, A_.is_equal)
+    ts(a("idp"), a("colf", 0, 128), col(P_), None, A_.is_equal)
+    for b in range(12):
+        o = a(("pa", "pb", "pz", "psm", "pk", "pr")[b % 6], 0, 256)
+        mm(o, a("idp"), a("comb"), True, False)
+        mm(o, a("m8", p=p8), a("mkb", 256 * b, 256 * b + 256, p=p8), False, True)
+        act(a("win", 256 * b, 256 * b + 256), o, AF.Identity, a("biasb", b, b + 1))
+    for b in range(4):
+        act(a("dgw", 256 * b, 256 * b + 256), a("comb"), AF.Identity, a("biasb", b, b + 1))
+    for fam, w in (("zf", -4096.0), ("zm", col(MW)), ("zw", col(WN)), ("zd", col(DIG)), ("zl", col(LW)), ("zs", -1.0), ("zv", col(VW))):
+        ts(a(fam), a("colf", 0, 144), col(G15), w, A_.is_equal, A_.mult)
+    for fam, w in (("bd", col(DIG)), ("bl", col(LW)), ("bz", col(DIG4)), ("by", col(YW)), ("bo", 1.0), ("bn", -1.0)):
+        ts(a(fam), a("hi16"), col(G_), w, A_.is_equal, A_.mult)
+    for fam, s1, s2 in (("kl0", KA, TA), ("kl1", KB, KC), ("klr", KD, TA)):
+        ts(a(fam), a("rr", 0, 128), col(s1), col(s2), A_.mult, A_.add)
+    ts(a("kr"), a("colf"), col(IS1), col(N1), A_.mult, A_.add)
+    ts(a("rbig"), a("rr"), 0.0, 33554432.0, A_.is_equal, A_.mult)
+    ts(a("rmin"), a("rbig"), -1.0, 2.0, A_.mult, A_.add)
+    ts(a("kseg"), a("rr"), 0.0, None, A_.not_equal)
+    ts(a("kne"), a("rr"), col(R_), None, A_.not_equal)
+    tt(a("kdg"), a("kseg"), a("kne"), A_.mult)
+    ts(a("lf"), a("colf", 0, 16), col(R16), None, A_.add)
+    ts(a("lr"), a("colf", 0, 16), col(RREV), None, A_.add)
+    iota(a("qp"), [[8, 2], [32, 8]])
+    ts(col(R8), col(R_), 8.0, 8.0, A_.is_ge, A_.mult)
+    ts(a("lp"), a("qp"), col(R8), col(R_), A_.add, A_.add)
+    ts(a("l2"), a("colf", 0, 16), 16.0, col(R15), A_.mult, A_.add)
+    ts(a("ct"), a("colf", 0, 16), -16.0, col(R240), A_.mult, A_.add)
+    ts(a("oh"), a("colf", 0, 16), col(R15), None, A_.is_equal)
+    ts(a("idf"), a("colf", 0, 128), col(P_), None, A_.is_equal)
+    ts(a("idg"), a("colf", 0, 128), col(P_), -1.0, A_.is_equal, A_.mult)
+    ts(a("idn"), a("colf", 0, 128), col(P_), -1.0, A_.is_equal, A_.mult)
+    ts(a("e0"), a("colf", 0, 128), 0.0, col(IS0), A_.mult, A_.add)
+    ts(a("g8"), a("hi16"), col(P16), None, A_.is_equal)
+    fill(a("zero"), 0.0)
+    fill(a("ones"), 1.0)
+    fill(a("ymb", 2048, 2064), 0.0)
+    fill(a("tab", L, L + 16), 0.0)
+    for t in range(NS):
+        fill(a("snd%d" % t, 0, 80), 0.0)
+    asel(a("bt"), a("bn"), [[1, 128]], A_.is_ge, 0.0, 0, -1)
+    asel(a("tri"), a("bt"), [[1, 128]], A_.not_equal, -256.0, 0, -1)
+    cp(a("tab", 0, L), a("oci"))
+    cp(a("dlc"), a("dli"))
+    dma("Y", a("dl8", p=p8), a("dlc"), 32)
+    cp(a("thf", p=p8), a("thi", p=p8))
+    mm(a("prk", 48, 49), a("g8", p=p8), a("thf", p=p8), True, True)
+    act(a("thc"), a("prk", 48, 49), AF.Identity, 4096.0)
+    for h in range(2):
+        for r in range(16):
+            mm(a("pu", 32 * h, 32 * h + 32), sel("zw", r), a("x", 2048 + 8 * h + r + 8 * (r >> 3), W, 32), r == 0, r == 15)
+    ts(a("ui"), a("pu", 0, 64), -1.0, None, A_.mult)
+    ts(a("uu"), a("ui"), 4095, None, A_.bitwise_and)
+    tt(a("sq"), a("uu"), a("uu"), A_.mult)
+    ts(a("t32"), a("uu"), 1184.0, -float(CENTER), A_.mult, A_.add)
+    tt(a("base"), a("sq"), a("t32"), A_.add)
+
+    def yrep(dst, who, src, neg, n=256, at=0, pos=None):
+        for k, eng in enumerate(who):
+            o = a(dst, 16 * at + k, 16 * (at + n), 16)
+            if eng == "V" and neg:
+                ts(o, src, -1.0, None, A_.mult)
+            elif eng == "V":
+                cp(o, src)
+            elif eng == "S":
+                act(o, src, AF.Identity, 0.0, -1.0 if neg else 1.0)
+            elif eng == "s":
+                f = src[1][0]
+                for b in range(0, n, 64):
+                    act(a(dst, 16 * (at + b) + k, 16 * (at + b + 64), 16), a(f[0], f[1] + b, f[1] + b + 64), AF.Identity, 0.0, -1.0)
+            else:
+                asel(o, pos or src, [[0, n]], A_.is_ge, 0.0, 0, 0)
+
+    def ycols(t):
+        return a("x", W - 256 * (t + 1), W - 256 * t)
+
+    def names(dst, lst, t, first=False):
+        ts(dst, ind(a("oci") if first else a("tab", 0, L), lst), (11 - t) / 16.0, -15.0 / 32, A_.mult, A_.add)
+
+    def main(c, yr, rev, fch, mch):
+        u = 0
+        for w in fch:
+            tt(a("vm", 256 * u, 256 * (u + w)), ind(a("x"), a(c, 16 * u, 16 * (u + w))), a(yr, 256 * u, 256 * (u + w)), A_.min)
+            u += w
+        u = 0
+        for w in mch:
+            o, i = a("mg", 256 * u, 256 * (u + abs(w))), ind(a("win"), a(c, 16 * u, 16 * (u + abs(w))))
+            act(o, i) if w > 0 else cp(o, i)
+            u += abs(w)
+        if rev:
+            mm(a("pk", 0, 256), a("kl1", p=k3), a("kr", p=k3), True, False)
+            for u in range(16):
+                for buf, fam in (("vm", "zf"), ("mg", "zm")):
+                    mm(a("pk", 0, 256), sel(fam, 15 - u), a(buf, 256 * u, 256 * u + 256), False, False)
+            return
+        for h, bank in enumerate(("pr", "pk")):
+            mm(a(bank, 0, 128), a("kl0", p=k3), a("kr", 0, 128, p=k3), True, False)
+            for u in range(16):
+                for buf, fam in (("vm", "zf"), ("mg", "zm")):
+                    mm(a(bank, 0, 128), sel(fam, u), a(buf, 2048 * h + 128 * u, 2048 * h + 128 * u + 128), False, False)
+
+    def live(order, r):
+        if order in (10, 11):
+            return a("lvn", 16 * r + 8 * (order - 10), 16 * r + 8 * (order - 9))
+        return a("lvn", 15 - r, 256, 16) if order == 2 else a("val", r, 64, 16)
+
+    def distinct(bank, order, dig, n, s, dummy, at=0):
+        q, e = n // 16, at // 16
+        mm(a(bank, 0, 512), a("zero", p=slice(0, 1)), a("x", 2048, 2560, p=slice(0, 1)), True, False)
+        for r in range(16):
+            mm(a(bank, r, n, 16), sel("zl", r), live(order, r), False, False)
+        if order >= 10:
+            for r in range(8):
+                mm(a(bank, 256 + 16 * r, 272 + 16 * r), a("bl"), a("lvn", 8 * (order - 10) + r, 256, 16), False, False)
+        elif order:
+            for r in range(16):
+                mm(a(bank, 256 + r, 256 + n, 16), a("bl"), live(order, r), False, False)
+        else:
+            mm(a(bank, 256, 256 + n), a("bl"), a("val"), False, False)
+        for r in range(16):
+            mm(a(bank, r, n, 16), sel("zd", r), a(dig, at + r, at + n, 16), False, False)
+        mm(a(bank, 256, 256 + n), a("bd"), a(dig, at, at + n), False, True)
+        scan(a("prop" + s, 0, n), a("kdg", 0, n), a(bank, 0, n), A_.mult, A_.add)
+        tt(a("eq" + s, 0, n), a("prop" + s, 0, n), a(bank, 256, 256 + n), A_.is_equal)
+        scan(a("cn" + s, 0, n), a("kseg", 0, n), a("eq" + s, 0, n), A_.mult, A_.add)
+        tt(a("vv" + s, 0, q), a("prop" + s, 15, n, 16), a("cn" + s, 15, n, 16), A_.add)
+        ts(a("off" + s, 2 * e, 2 * (e + q), 2), a("vv" + s, 0, q), 4096.0, col(dummy), A_.mult, A_.min)
+
+    def best(bank, n, dst):
+        q = n // 16
+        scan(a("rs", 0, n), a("rbig", 0, n), a(bank, 0, n), A_.add, A_.min)
+        cp(a("ji", 0, q), a("rs", 15, n, 16))
+        ts(a("ja", 0, q), a("ji", 0, q), 4095, None, A_.bitwise_and)
+        cp(dst, a("ja", 0, q))
+
+    def place(b, n, dst, t):
+        acol = -float(CENTER) if t == 0 else a("ac", 2 * t + 1, 2 * t + 2)
+        cp(a("ui", b, n), a("pu", b, n))
+        ts(a("uu", b, n), a("ui", b, n), 4095, None, A_.bitwise_and)
+        tt(a("sq", b, n), a("uu", b, n), a("uu", b, n), A_.mult)
+        ts(a("t32", b, n), a("uu", b, n), 1184.0, acol, A_.mult, A_.add)
+        tt(a("zz", b, n), a("sq", b, n), a("t32", b, n), A_.add)
+        ts(a("li", b, n), a("zz", b, n), 5, 1023, A_.arith_shift_right, A_.bitwise_and)
+        cp(a(dst, b, n), a("li", b, n))
+
+    def mark(src, lst, order, n, at=0):
+        ad, adf = ("ad", "adf") if order else ("adr", "adfr")
+        act(a(ad, at, at + n), ind(src, lst))
+        act(a(adf, at, at + n), a(ad, at, at + n), AF.Identity, col(BI), col(SC))
+        distinct("pb" if order == 11 else "pa", order, ad, n, "a", DM, at)
+        for q in range(at // 16, (at + n) // 16):
+            act(ind(a("win"), a("offa", 2 * q, 2 * q + 1)), a(adf, 16 * q, 16 * q + 16), AF.Silu)
+
+    def ya_out(t, h):
+        mm(a("pz", 0, 256), a("by"), a("lvn"), True, False)
+        for r in range(16):
+            if h:
+                mm(a("pz", 15 - r, 256, 16), a("bz"), a("ad", r, 256, 16), False, False)
+            else:
+                mm(a("pz", r, 256, 16), a("bz"), a("ad", 16 * r, 16 * r + 16), False, False)
+        act(a("zr"), a("pz", 0, 256), AF.Relu, -16511.0)
+        act(a("yab", 256 * (2 * t + h), 256 * (2 * t + h + 1)), a("zr"), AF.Identity, -1.0)
+
+    yrbuf = ["yr0", "yr1"]
+
+    def first_y(t, who):
+        act(a("y0p"), ind(ycols(t), a("lp")))
+        yrep(yrbuf[t % 2], who, a("y0p"), False)
+
+    first_y(0, CFG["y00"])
+    first_y(1, "G" * 16)
+    for h in range(2):
+        ts(a("lb", 8 * h, 8 * h + 8), a("base", 32 * h + 24, 32 * h + 32), 5, 1023, A_.arith_shift_right, A_.bitwise_and)
+
+    for t in range(NS):
+        B = W - 256 * (t + 1)
+        cp(a("l0"), a("lb"))
+        names(a("c0"), a("l0"), t, t == 0)
+        asel(a("lvn"), a("win", B, B + 256), [[0, 256]], A_.is_ge, 0.0, 0, 0)
+        act(a("y0f"), ind(ycols(t), a("lf")))
+        wide([("g8", "dl8", 256 * t)], p8)
+        act(a("dln"), a("pu", 256, 512))
+        act(a("dlp"), ind(a("dln"), a("l2")))
+        main("c0", yrbuf[t % 2], False, CFG["f0"], CFG["m0"] if t else CFG["m00"])
+        if t + 2 < NS:
+            first_y(t + 2, "G" * 16)
+        for h, bank in enumerate(("pr", "pk")):
+            j, b = a("j16", 8 * h, 8 * h + 8), 128 * h
+            best(bank, 128, j)
+            tt(a("y1n", b, b + 128), ind(a("vm", 16 * b, 16 * b + 2048), j), a("y0f", b, b + 128), A_.subtract)
+            if "G" in CFG["yh"][h]:
+                act(a("y1p", b, b + 128), a("y1n", b, b + 128), AF.Identity, 0.0, -1.0)
+            yrep("yrh", CFG["yh"][h], a("y1n", b, b + 128), True, 128, b, a("y1p", b, b + 128))
+            mark(a("mg", 16 * b, 16 * b + 2048), j, 10 + h, 128, b)
+            for r in range(16):
+                mm(a("pu", 8 * h, 8 * h + 8), sel("zw", r), a("y1n", b + r, b + 128, 16), r == 0, r == 15)
+            if h:
+                for r in range(16):
+                    mm(a("pu", 16, 32), sel("zw", 15 - r), a("y1n", 16 * r, 16 * r + 16), r == 0, r == 15)
+            place(8 * h, 32 if h else 8, "l1", t)
+            names(a("c1", b, b + 128), a("l1", 8 * h, 8 * h + 8), t)
+        ya_out(t, 0)
+        act(a("y1r"), ind(a("y1n"), a("lr")), AF.Identity, 0.0, -1.0)
+        act(a("nn"), ind(a("tab"), a("l1", 16, 32)))
+        wide([("idf", "dlp", 0), ("idg", "nn", 0)])
+        act(a("t2"), a("pu", 256, 512))
+        main("c1", "yrh", True, CFG["f1"], CFG["m1"])
+        act(a("ld"), ind(a("dgw"), a("l1", 16, 32)))
+        distinct("pb", 2, "ld", 256, "n", DN)
+        best("pk", 256, a("j16"))
+        tt(a("y2n"), ind(a("vm"), a("j16")), a("y1r"), A_.subtract)
+        for r in range(16):
+            mm(a("psm", 0, 16), sel("zv", r), live(2, r), r == 0, False)
+        for r in range(16):
+            mm(a("psm", 0, 16), sel("zs", r), a("y2n", r, 256, 16), False, r == 15)
+        ts(a("rdy"), a("psm", 0, 16), a("thc"), None, A_.is_ge)
+        scan(a("pre"), a("kseg", 0, 16), a("rdy"), A_.mult, A_.add)
+        tt(a("rp"), a("rdy"), a("ct"), A_.mult)
+        mm(a("prk", 0, 16), a("idp"), a("ct"), True, False)
+        mm(a("prk", 0, 16), a("tri"), a("rdy"), False, False)
+        mm(a("prk", 0, 16), a("bo"), a("pre"), False, False)
+        mm(a("prk", 0, 16), a("idn"), a("rp"), False, True)
+        mm(a("prk", 16, 17), a("bo"), a("pre", 15, 16), True, True)
+        snd, land = "snd%d" % t, "land%d" % t
+        ts(a("slot"), a("prk", 0, 16), 255.0, None, A_.add)
+        ts(a(snd, 0, 1), a("prk", 16, 17), 64.0, None, A_.min)
+        cp(ind(a(snd, 16, 528), a("slot")), a("y2n"))
+        dst = T.cores[(rank + 1 + t % (nrank - 1)) % nrank]
+        rid, pid = topo.addr(dst, core)
+        mask = sum(1 << e for e in topo.engines(core, dst)[:NENG])
+        rec("G", lambda t=t, rid=rid, pid=pid, mask=mask: g.remote_dma(
+            a("land%d" % t)[0], a("snd%d" % t, 0, 80)[0], T.sem["arr%d" % t], T.sem.sent, pid, rid, mask),
+            [], [a(snd, 0, 80)], 300, "r")
+        ops.append(["A", None, [], [(land, 0, 80, 1)], ("a", t, len(ops) - 1), 0, CFG["remote"]])
+        scan(a("rm"), a("rmin"), a("pk", 0, 256), A_.add, A_.max)
+        ts(a("ki"), a("rm", 15, 256, 16), 1.0, None, A_.add)
+        ts(a("ka"), a("ki"), 15, None, A_.bitwise_and)
+        cp(a("k16"), a("ka"))
+        mark(a("mg"), a("j16"), 2, 256)
+        ya_out(t, 1)
+        if t == NS - 1:
+            dma("Y", ext(T.ya[:]), a("yab", p=g16), 64)
+        tt(a("t1"), ind(a("oh"), a("k16")), a("t2"), A_.mult)
+        for q in range(15, -1, -1):
+            tt(ind(a("tab"), a("offn", 2 * q, 2 * q + 1)), a("t1", 16 * q, 16 * q + 16), a("nn", 16 * q, 16 * q + 16), A_.add)
+        if t == NS - 1:
+            dma("Y", ext(T.yo[:]), a("tab", 0, L), 512)
+        for r in range(16):
+            mm(a("pu", 0, 4), sel("zw", r), a(land, 16 + r, 80, 16), r == 0, r == 15)
+        yrep("yrr", CFG["yrr"], a(land, 16, 80), True, 64)
+        ts(a("val"), a("slotc"), a(land, 0, 1), None, A_.is_lt)
+        place(0, 4, "lv", t)
+        names(a("cr"), a("lv"), t)
+        if t + 1 < NS:
+            u = t + 1
+            mm(a("prk", 32, 33), a("e0"), a(land, 0, 1), True, True)
+            cp(a("ai", 0, 1), a("prk", 32, 33))
+            ts(a("ai", 1, 2), a("ai", 0, 1), 63, None, A_.bitwise_and)
+            ts(a("ac", 2 * u, 2 * u + 1), a("ai", 1, 2), 32.0, None, A_.mult)
+            ts(a("ac", 2 * u + 1, 2 * u + 2), a("ai", 1, 2), 32.0, -float(CENTER), A_.mult, A_.add)
+            for h in range(2):
+                b = 32 * h + 8 * (3 - u)
+                ts(a("zb", 8 * h, 8 * h + 8), a("base", b, b + 8), a("ac", 2 * u, 2 * u + 1), None, A_.add)
+            ts(a("lb"), a("zb"), 5, 1023, A_.arith_shift_right, A_.bitwise_and)
+        mm(a("pr", 0, 64), a("klr", p=k3), a("kr", 0, 64, p=k3), True, False)
+        u = 0
+        for w in CFG["rch"]:
+            c = a("cr", 4 * u, 4 * (u + w))
+            tt(a("vmr", 64 * u, 64 * (u + w)), ind(a("x"), c), a("yrr", 64 * u, 64 * (u + w)), A_.min)
+            act(a("mgr", 64 * u, 64 * (u + w)), ind(a("win"), c))
+            for r in range(u, u + w):
+                mm(a("pr", 0, 64), sel("zf", r), a("vmr", 64 * r, 64 * r + 64), False, False)
+                mm(a("pr", 0, 64), sel("zm", r), a("mgr", 64 * r, 64 * r + 64), False, r == 15)
+            u += w
+        best("pr", 64, a("jr"))
+        if t + 1 < NS:
+            mark(a("mgr"), a("jr"), 0, 64)
+        if t == NS - 2:
+            dma("G", ext(T.ym[:, 2048:W]), a("win", 2048, W, p=g16), 16)
+        if t == NS - 1:
+            for b in range(0, 2048, 256):
+                cp(a("ymb", b, b + 256), a("win", b, b + 256))
+            act(a("adr"), ind(a("mgr"), a("jr")))
+            distinct("pa", 0, "adr", 64, "a", DY)
+            for q in range(4):
+                cp(ind(a("ymb"), a("offa", 2 * q, 2 * q + 1)), a("ones"))
+            dma("Y", ext(T.ym[:, 0:2048]), a("ymb", 0, 2048, p=g16), 32)
+
+    emit(g, T, ops, QO)
+
+
+def emit(g, T, ops, QO):
+    n = len(ops)
+    width = {k: v[0] for k, v in _SB.items()}
+    width.update({k: 1 for k in _PS})
+    writer = {k: np.full(w, -1) for k, w in width.items()}
+    reader = {k: [] for k in width}
+    semof, deps, soft, nd = [], [], [], 0
+
+    def cols(f):
+        return slice(0, 1) if f[0] in _PS else slice(f[1], f[2], f[3])
+
+    member = {k: [] for k in _PS}
+    group, last = {}, {}
+    for i, (q, fn, rd, wr, kind, cost, lat) in enumerate(o[:7] for o in ops):
+        if kind == "d":
+            semof.append("d%d" % nd)
+            nd += 1
+        else:
+            semof.append("sent" if kind == "r" else "s" + q if kind == "c" else "arr%d" % kind[1])
+        me = semof[i]
+        need, order = set(), set()
+        for f in rd:
+            need.update(int(w) for w in np.unique(writer[f[0]][cols(f)]) if w >= 0)
+            if f[0] in _PS:
+                need.update(r for r, m in reader[f[0]] if semof[r] != me)
+                need.update(member[f[0]])
+        for f in wr:
+            if q == "P":
+                if ops[i][7]:
+                    order.update(member[f[0]])
+                    member[f[0]] = []
+                member[f[0]].append(i)
+                group[i] = member[f[0]][0]
+                order.add(group[i])
+                order.discard(i)
+            else:
+                for w in np.unique(writer[f[0]][cols(f)]):
+                    if w >= 0:
+                        (order if semof[w] == me and kind == "c" and not CFG["waw"] else need).add(int(w))
+            keep = []
+            for r, m in reader[f[0]]:
+                if m[cols(f)].any():
+                    need.add(r)
+                    m[cols(f)] = False
+                if m.any():
+                    keep.append((r, m))
+            reader[f[0]] = keep
+        for f in wr:
+            writer[f[0]][cols(f)] = i
+        for f in rd:
+            m = np.zeros(width[f[0]], bool)
+            m[cols(f)] = True
+            reader[f[0]].append((i, m))
+        need.discard(i)
+        if fn is None:
+            order.add(kind[2])
+        if wr and wr[0][0] in ("vm", "mg", "vmr", "mgr"):
+            if (q, wr[0][0]) in last:
+                order.add(last[q, wr[0][0]])
+            last[q, wr[0][0]] = i
+        deps.append(need)
+        soft.append(order - need)
+    wake = CFG["wake"]
+    rank_, succ = [0.0] * n, [[] for _ in range(n)]
+    for i in range(n):
+        for d in deps[i]:
+            succ[d].append((i, wake + ops[d][6]))
+        for d in soft[i]:
+            succ[d].append((i, 0.0))
+    for i in range(n - 1, -1, -1):
+        rank_[i] = ops[i][5] + max([ops[i][6]] + [w + rank_[j] for j, w in succ[i]])
+    pred = [[] for _ in range(n)]
+    for i in range(n):
+        for j, w in succ[i]:
+            pred[j].append((i, w))
+
+    def schedule(prio, nxt, prv):
+        left = [len(p) for p in prv]
+        ready, end = [0.0] * n, [0.0] * n
+        pool = {q: [] for q in list(QO) + ["A"]}
+        for i in range(n):
+            if not left[i]:
+                pool[ops[i][0]].append(i)
+        free = {q: 0.0 for q in pool}
+        seq = []
+        while len(seq) < n:
+            now, q = min((max(free[q], min(ready[i] for i in pool[q])), q) for q in pool if pool[q])
+            i = max((i for i in pool[q] if ready[i] <= now), key=lambda i: (prio[i], -i))
+            soon = [j for j in pool[q] if now < ready[j] <= now + CFG["look"] * ops[i][5] and prio[j] > prio[i]]
+            if soon:
+                i = max(soon, key=lambda j: prio[j])
+                now = ready[i]
+            pool[q].remove(i)
+            seq.append(i)
+            end[i] = free[q] = now + ops[i][5]
+            for j, w in nxt[i]:
+                ready[j] = max(ready[j], free[q] + w)
+                left[j] -= 1
+                if not left[j]:
+                    pool[ops[j][0]].append(j)
+        return seq, end, max(end[i] + ops[i][6] for i in range(n))
+
+    seq, end, length = schedule(rank_, succ, pred)
+    CFG["path"] = max(rank_)
+    rng = np.random.RandomState(CFG["seed"])
+    prio = np.array(rank_)
+    for _ in range(0 if "seq" in CFG else CFG["passes"]):
+        trial = prio + rng.normal(0.0, CFG["shift"], n) * (rng.rand(n) < CFG["share"])
+        s2, end, l2 = schedule(trial.tolist(), succ, pred)
+        if l2 < length:
+            seq, length, prio = s2, l2, trial
+    seq = CFG.setdefault("seq", seq)
+    CFG["span"] = length
+    wanted = set()
+    for d in deps:
+        wanted |= d
+    count, value = {}, {}
+    for i in seq:
+        kind = ops[i][4]
+        step = 16 if kind == "d" else (1 if i in wanted else 0) if kind == "c" else NENG
+        count[semof[i]] = count.get(semof[i], 0) + step
+        value[i] = count[semof[i]]
+    final = {group[i]: i for i in seq if i in group}
+    known = {q: {} for q in QO}
+    after = {}
+    for i in seq:
+        q, fn, kind = ops[i][0], ops[i][1], ops[i][4]
+        if fn is None:
+            after[i] = {semof[i]: value[i]}
+            continue
+        kn = known[q]
+        top = {}
+        for d in deps[i]:
+            if semof[d] not in top or value[d] > value[top[semof[d]]]:
+                top[semof[d]] = d
+        for d in sorted(top.values(), key=lambda d: -len(after[d])):
+            if kn.get(semof[d], 0) < value[d]:
+                QO[q].wait_ge(T.sem[semof[d]], value[d])
+                for s, v in after[d].items():
+                    kn[s] = max(kn.get(s, 0), v)
+        ins = fn(final[group[i]] == i) if q == "P" else fn()
+        if kind == "d":
+            ins.then_inc(T.sem[semof[i]], 16)
+        elif kind == "c" and i in wanted:
+            ins.then_inc(T.sem[semof[i]], 1)
+        done = dict(kn)
+        done[semof[i]] = max(done.get(semof[i], 0), value[i])
+        after[i] = done
+    for s, v in count.items():
+        if v and known["G"].get(s, 0) < v:
+            g.wait_ge(T.sem[s], v)

@@ -2,34 +2,36 @@ import numpy as np
 from concourse.mybir import AluOpType, ActivationFunctionType
 
 W, L, NS = 3072, 1024, 4
-BF, F32, I32, U16 = "bfloat16", "float32", "int32", "uint16"
+PAD = 128
+MIR = 64
+BF, F32, I32, U16, F16 = "bfloat16", "float32", "int32", "uint16", "float16"
 _SB = {
-    "x": (W, BF), "oci": (L, I32), "tab": (L + 16, F32), "win": (W + 16, F32), "dgw": (L, BF),
-    "vm": (4096, BF), "mg": (4096, BF), "yr0": (4096, BF), "yr1": (4096, BF), "yrh": (4096, BF),
-    "vmr": (1024, BF), "mgr": (1024, BF), "yrr": (1024, BF),
+    "x": (W, BF), "oci": (L, I32), "tab": (L + MIR + 32, F32), "win": (PAD + W + 16, F32),
+    "vm": (4128, BF), "mg": (4128, BF), "yr0": (4096, BF), "yr1": (4096, BF), "yrh": (4096, BF),
+    "vmr": (1040, BF), "mgr": (1040, BF), "yrr": (1024, BF),
     "c0": (256, U16), "c1": (256, U16), "cr": (64, U16),
-    "pi": (2, I32), "cols": (40, F32), "wti": (1, I32), "thi": (1, I32), "thf": (1, F32), "thc": (1, F32),
-    "colf": (256, F32), "rr": (256, F32), "hi4": (256, F32), "lo64": (256, F32), "hi16": (128, F32), "comb": (256, BF),
-    "mkb": (W, BF), "m8": (128, BF), "ymb": (2064, BF), "ones": (16, BF),
-    "biasb": (12, F32), "slotc": (64, F32),
-    "zf": (144, BF), "zm": (144, BF), "zw": (144, BF), "zd": (144, BF), "zl": (144, BF), "zs": (144, BF), "zv": (144, BF),
-    "bo": (128, BF), "bd": (128, BF), "bl": (128, BF), "bz": (128, BF), "by": (128, BF), "bn": (128, BF), "bt": (128, BF),
-    "tri": (128, BF), "idn": (128, BF), "idp": (128, BF), "e0": (128, BF), "g8": (128, F32), "zero": (128, BF),
-    "kl0": (128, BF), "kl1": (128, BF), "klr": (128, BF), "kr": (256, BF),
-    "kseg": (256, BF), "kdg": (256, BF), "kne": (256, BF), "rbig": (256, BF), "rmin": (256, BF),
-    "lp": (16, U16), "qp": (16, F32), "y0p": (256, BF), "lf": (16, U16), "l2": (16, U16), "lr": (16, U16), "ct": (16, BF), "oh": (16, F32), "idf": (128, F32), "idg": (128, F32),
-    "dli": (64, I32), "dlc": (64, F32), "dl8": (L, F32), "dln": (256, F32), "dlp": (256, F32),
+    "pi": (2, I32), "pj": (2, I32), "cols": (40, F32), "wti": (1, I32), "thi": (1, I32), "thf": (1, F32), "thc": (1, F32),
+    "colf": (256, F32), "rr": (256, BF), "hi4": (256, BF), "lo64": (256, BF), "hi16": (128, F32), "comb": (256, BF),
+    "mkb": (W, BF), "m8": (128, BF), "m8a": (128, BF), "ymb": (PAD + 2064, BF), "ones": (16, BF),
+    "biasb": (12, F32), "rslot": (4, F32),
+    "z1": (144, BF), "zf": (144, BF), "zm": (144, BF), "zw": (144, BF), "zl": (144, BF), "zv": (144, BF),
+    "bo": (128, BF), "bd": (128, BF), "bw": (128, BF), "bn": (128, BF), "bt": (128, BF),
+    "tri": (128, BF), "idn": (128, BF), "idp": (128, BF), "e0": (128, BF), "g8": (128, F32), "idg": (128, F32),
+    "c17": (128, BF), "cq": (128, BF), "c256": (256, BF), "kseg": (256, BF), "rb": (256, BF), "rw": (256, BF),
+    "dm": (384, BF), "nsel": (2048, F16), "dg": (64, BF), "sp16": (16, F16),
+    "lp": (16, U16), "qp": (16, F32), "y0p": (256, BF), "lf": (16, U16), "ct": (16, BF), "oh": (16, F32),
+    "dli": (64, I32), "dlc": (64, F32), "dl8": (L, F32),
     "base": (64, I32), "ui": (64, I32), "uu": (64, I32), "sq": (64, I32), "t32": (64, I32), "zz": (64, I32), "li": (64, I32),
-    "l0": (16, U16), "l1": (32, U16), "lv": (4, U16), "zb": (16, I32), "lb": (16, I32),
-    "ai": (2, I32), "ac": (8, F32),
-    "rs": (256, F32), "ji": (16, I32), "ja": (16, I32), "j16": (16, U16), "jr": (4, U16),
+    "l0": (16, U16), "l1": (32, U16), "lv": (4, U16), "ai": (1, I32), "ac": (4, F32), "us": (64, F32),
+    "rs": (256, F32), "ji": (16, I32), "ja": (16, I32), "jm": (16, I32), "j16": (16, U16), "jr": (4, U16),
+    "thr": (16, F32), "dd": (16, I32), "idh": (128, F16), "bnh": (128, F16),
     "rm": (256, F32), "ki": (16, I32), "ka": (16, I32), "k16": (16, U16),
-    "y0f": (256, BF), "y1n": (256, BF), "y1p": (256, BF), "y1r": (256, BF), "y2n": (256, BF), "lvn": (256, BF), "val": (64, BF),
-    "ad": (256, BF), "adf": (256, F32), "ld": (256, BF), "nn": (256, F32), "t1": (256, F32), "t2": (256, F32),
+    "y0f": (256, BF), "y1n": (256, BF), "y1p": (256, BF), "y1r": (256, BF), "y2n": (256, BF), "lvn": (256, BF), "inv": (4, BF),
+    "ad": (256, BF), "adf": (256, F32), "nn": (256, F32), "t1": (256, F32), "t2": (256, F32),
     "adr": (64, BF), "adfr": (64, F32),
-    "propa": (256, F32), "eqa": (256, BF), "cna": (256, BF), "vva": (16, F32), "offa": (32, U16),
-    "propn": (256, F32), "eqn": (256, BF), "cnn": (256, BF), "vvn": (16, F32), "offn": (32, U16),
-    "zr": (256, F32), "yab": (2048, F32),
+    "prop": (256, F32), "eqa": (256, BF), "cna": (256, F32), "ndg": (512, BF), "rup": (256, BF), "offa": (32, U16),
+    "lw": (16, F16), "eqn": (384, BF), "offn": (32, U16),
+    "yab": (2048, F32),
     "rdy": (16, BF), "pre": (16, BF), "rp": (16, BF), "slot": (16, U16),
     "snd0": (528, BF), "snd1": (528, BF), "snd2": (528, BF), "snd3": (528, BF),
     "land0": (80, BF), "land1": (80, BF), "land2": (80, BF), "land3": (80, BF),
@@ -46,13 +48,15 @@ NDMA = 20
 SEMAPHORES = ["sV", "sS", "sP", "sG", "sent"] + ["arr%d" % t for t in range(NS)] + ["d%d" % i for i in range(NDMA)]
 
 SILU_ONE = 1.2784645427610738
-CENTER = 32 * 148 * 1024
 NENG = 8
+U18 = 2.0 ** -18
 CFG = dict(
-    f0=(2, 2, 2, 2, 2, 2, 2, 1, 1), m0=(2, 2, 1, 2, 1, 1, 1, 2, 1, 1, -2), m00=(2, 2, 2, 2, 2, 2, 2, 1, 1),
-    f1=(2, 3, 2, 1, 3, 2, 2, 1), m1=(2, 3, 1, 2, 3, -1, 3, 1), rch=(8, 4, 4),
-    yh=("GGGGGGGGSSSSVVVV", "GGGGGGSSVVVVVVVV"), yrr="VVVVSSSSSSSSSSSS", y00="VVVVVVVVVGGGSSSS",
-    gather=1.56, scatter=3.8, pe=0.5, wake=90.0, dma=2000.0, remote=2800.0, look=0.3, waw=True, passes=300, seed=1, shift=300.0, share=0.05,
+    f0=(2, 2, 2, 2, 4, 2, 1, 1), m0=(2, 2, 3, 1, 1, 1, 2, 1, 1, -2), m00=(2, 1, 1, 2, 2, 2, 2, 1, 2, 1),
+    f1=(2, 5, 1, 5, 2, 1), m1=(2, 3, 1, 2, 3, -1, 3, 1), rch=(8, 4, 4),
+    yh=("GGGGGGGGVVVVVVVV", "GGGGGGSSVVVVVVVV"), yrr="SSSSSSSSSSSSVVVV", y00=("VVVVVVVVVVVVVVVV", "GGGGGGVVVVVVSSSS"),
+    pair=True, uscan=True, look=0.5, turns=4, mix=0.6, passes=150, seed=1, shift=300.0, share=0.05,
+    models=((1.0, 1.56, 3.8, 0.0, 0.5, 90.0, 2000.0, 2800.0), (0.92, 1.56, 3.8, 0.0, 0.46, 190.0, 2000.0, 2800.0),
+            (0.95, 1.56, 3.8, 2.0, 0.5, 130.0, 2000.0, 2800.0)),
 )
 
 
@@ -84,16 +88,16 @@ def rank_program(g, core, T, topo):
         return len(range(f[1], f[2], f[3])) * (16 if len(s) == 3 else 1)
 
     def narrow(*aps):
-        return all(s[1][0][0] not in _PS and _SB[s[1][0][0]][1] in (BF, U16) for s in aps)
+        return all(s[1][0][0] not in _PS and _SB[s[1][0][0]][1] in (BF, U16, F16) for s in aps)
 
-    def span(o, i, per):
+    def span(o, i, per, fused=False):
         if len(o) == 3:
-            return 55 + num(o) * CFG["scatter"]
+            return ("s", num(o))
         if len(i) == 3:
-            return 55 + num(i) * CFG["gather"]
-        return max(64, num(o) * per)
+            return ("f" if fused else "g", num(i))
+        return ("c", max(64, num(o) * per))
 
-    def rec(q, fn, outs, ins, cost, kind="c", lat=0.0):
+    def rec(q, fn, outs, ins, cost, kind="c", lat=("n", 0.0)):
         rd, wr = [], []
         for o in outs:
             wr += o[1]
@@ -114,7 +118,7 @@ def rank_program(g, core, T, topo):
             rec("V", lambda: g.vector.tensor_scalar(o[0], i[0], val(s1), val(s2), o0, o1), [o], [i, s1, s2], c)
 
     def tt(o, i0, i1, op):
-        c = span(o, i0, 1 if i0[1][0][0] in _PS or i1[1][0][0] in _PS else 2)
+        c = span(o, i0, 1 if i0[1][0][0] in _PS or i1[1][0][0] in _PS else 2, True)
         rec("V", lambda: g.vector.tensor_tensor(o[0], i0[0], i1[0], op), [o], [i0, i1], c)
 
     def cp(o, i):
@@ -125,7 +129,7 @@ def rank_program(g, core, T, topo):
             span(o, d0, 0.5 if narrow(o, d0, d1) else 1))
 
     def fill(o, c):
-        rec("V", lambda: g.vector.memset(o[0], c), [o], [], 64)
+        rec("V", lambda: g.vector.memset(o[0], c), [o], [], span(o, o, 0.5 if narrow(o) else 1))
 
     def act(o, i, f=AF.Identity, bias=0.0, scale=1.0):
         if f == AF.Silu:
@@ -133,29 +137,24 @@ def rank_program(g, core, T, topo):
         else:
             rec("S", lambda: g.scalar.activation(o[0], i[0], f, bias=val(bias), scale=val(scale)), [o], [i, bias, scale], span(o, i, 1))
 
-    def wide(pairs, p=None):
-        for b in range(0, 256, 64):
-            for n, (l, r, at) in enumerate(pairs):
-                mm(a("pu", 256 + b, 320 + b), a(l, p=p), a(r, at + b, at + b + 64, p=p), n == 0, n == len(pairs) - 1)
-
-    def mm(o, l, r, start, stop):
-        c = max(64, num(r)) * CFG["pe"] * (1 if narrow(l) else 4)
-        rec("P", lambda last: g.tensor.matmul(o[0], l[0], r[0], start, last), [o], [l, r], c)
+    def mm(o, l, r, start=False):
+        c = max(64, num(r)) * (4 if _SB[l[1][0][0]][1] == F32 else 1)
+        rec("P", lambda last: g.tensor.matmul(o[0], l[0], r[0], start, last), [o], [l, r], ("p", c))
         ops[-1].append(start)
 
     def iota(o, pat, base=0, cm=0, flag=True):
         if flag:
-            rec("G", lambda: g.iota(o[0], pat, base, cm, allow_small_or_imprecise_dtypes=True), [o], [], 130 + 2 * num(o))
+            rec("G", lambda: g.iota(o[0], pat, base, cm, allow_small_or_imprecise_dtypes=True), [o], [], ("c", 130 + 2 * num(o)))
         else:
-            rec("G", lambda: g.iota(o[0], pat, base, cm), [o], [], 130 + 2 * num(o))
+            rec("G", lambda: g.iota(o[0], pat, base, cm), [o], [], ("c", 130 + 2 * num(o)))
 
     def asel(o, i, pat, cmp, fl, base, cm):
-        rec("G", lambda: g.affine_select(o[0], i[0], pat, cmp, fl, base, cm), [o], [i], 170 + 2 * num(o))
+        rec("G", lambda: g.affine_select(o[0], i[0], pat, cmp, fl, base, cm), [o], [i], ("c", 170 + 2 * num(o)))
 
     QO = {"V": g.vector, "S": g.scalar, "P": g.tensor, "G": g, "Y": g.sync}
 
     def dma(q, o, i, kb):
-        rec(q, lambda: QO[q].dma_start(o[0], i[0]), [o], [i], 1000 if q == "G" else 100, "d", CFG["dma"] + kb * 7)
+        rec(q, lambda: QO[q].dma_start(o[0], i[0]), [o], [i], ("n", 1000 if q == "G" else 100), "d", ("d", kb))
 
     def ext(ap):
         return (ap, [])
@@ -163,107 +162,139 @@ def rank_program(g, core, T, topo):
     def sel(fam, r):
         return a(fam, 15 - r, 143 - r)
 
-    g16, k3, p8 = slice(0, 128, 16), slice(0, 3), slice(0, 8)
+    g16, p1, p8 = slice(0, 128, 16), slice(0, 1), slice(0, 8)
     col = lambda j: a("cols", j, j + 1)
+    top = W - 256
 
-    dma("Y", a("x", 2048, W), ext(T.xc[:, 2048:W]), 256)
+    dma("Y", a("x", top, W), ext(T.xc[:, top:W]), 64)
     dma("S", a("oci"), ext(T.oc[:]), 512)
     dma("Y", a("wti"), ext(T.wt[:]), 1)
     dma("Y", a("mkb", p=p8), ext(T.mk[:]), 48)
-    dma("Y", a("x", 0, 1024), ext(T.xc[:, 0:1024]), 512)
-    dma("S", a("x", 1024, 2048), ext(T.xc[:, 1024:2048]), 512)
+    dma("Y", a("x", 0, 1408), ext(T.xc[:, 0:1408]), 400)
+    dma("S", a("x", 1408, top), ext(T.xc[:, 1408:top]), 400)
     dma("Y", a("dli"), ext(T.dl[:]), 32)
     dma("Y", a("thi", p=p8), ext(T.th[:]), 1)
 
-    iota(a("pi", 0, 1), [[0, 1]], 0, 1, False)
+    iota(a("pi"), [[2, 2]], 0, 1, False)
+    iota(a("colf"), [[1, 256]])
     iota(a("hi4"), [[1, 4], [0, 64]], 128)
     iota(a("lo64"), [[0, 4], [1, 64]], 128)
-    iota(a("colf"), [[1, 256]])
     iota(a("rr"), [[0, 16], [1, 16]])
     iota(a("hi16"), [[16, 8], [0, 16]])
-    iota(a("slotc"), [[1, 4], [4, 16]])
-    P_, R_, G_, G15, IS0, IS1, IS2, DIG, DIG4, WN, R16, RREV, R15, R240, N1, DM, DN = range(17)
-    KA, KB, KC, KD, MW, LW, VW, YW, SC, BI, P16, TA, R8, DY = range(17, 31)
-    ts(a("pi", 1, 2), a("pi", 0, 1), 15, None, A_.bitwise_and)
+    iota(a("qp"), [[8, 2], [32, 8]])
+    (P_, R_, K2, G_, G15, IS0, IS1, IS2, IS3, IS4, DIG, WN, R16, R255, DM, DN0, DN1, MW, LW, VW, SC, BI, P16, P3, R8, DY,
+     J0, J1, JR, TA, TB, DEAD) = range(32)
+    ts(a("pj"), a("pi"), 15, None, A_.bitwise_and)
     cp(col(P_), a("pi", 0, 1))
-    cp(col(R_), a("pi", 1, 2))
-    for j, v in ((IS0, 0.0), (IS1, 1.0), (IS2, 2.0)):
-        ts(col(j), col(R_), v, None, A_.is_equal)
-    for j, v in ((KA, 128.0), (MW, -1048576.0), (LW, -12416.0 / 4096), (YW, 8192.0), (VW, 4096.0), (BI, SILU_ONE), (KB, -256.0), (KD, 64.0)):
-        ts(col(j), col(R_), 0.0, v, A_.is_equal, A_.mult)
-    for j, m, v in ((R16, 16.0, 0.0), (RREV, -16.0, 240.0), (R15, -1.0, 15.0), (DM, 1.0, float(W)), (DN, 1.0, float(L)), (R240, 1.0, 240.0), (DY, 1.0, 2048.0)):
-        ts(col(j), col(R_), m, v, A_.mult, A_.add)
-    ts(col(SC), col(R_), 0.0, None, A_.not_equal)
-    ts(col(N1), col(R_), 1.0, None, A_.not_equal)
-    tt(col(G_), col(P_), col(R_), A_.subtract)
-    ts(col(G15), col(G_), 15.0, None, A_.add)
+    cp(a("cols", R_, R_ + 2), a("pj"))
+    ts(a("cols", IS0, IS0 + 5), a("colf", 0, 5), col(R_), None, A_.is_equal)
+    for j, m, v in ((R16, 16.0, 0.0), (R255, -1.0, 255.0), (DM, 1.0, PAD + W), (DN0, 1.0, L + MIR), (DN1, 1.0, L + MIR + 16),
+                    (DY, 1.0, PAD + 2048), (J0, 128.0, -240 - (1 << 21)), (JR, 64.0, -240 - (1 << 21))):
+        ts(col(j), col(R_), m, float(v), A_.mult, A_.add)
+    ts(col(G15), col(P_), col(R_), 15.0, A_.subtract, A_.add)
+    ts(col(G_), col(P_), col(R_), None, A_.subtract)
     ts(col(P16), col(P_), 16.0, None, A_.mult)
-    ts(col(TA), col(IS2), 4096.0 * 2304, col(IS1), A_.mult, A_.add)
-    ts(col(KC), col(IS0), 3840.0, col(TA), A_.mult, A_.add)
-    ts(col(DIG4), col(IS1), 64.0, col(IS2), A_.mult, A_.add)
-    ts(col(DIG), col(DIG4), 1.0 / 4096, None, A_.mult)
+    ts(col(P3), col(P_), 16.0, 3.0, A_.mult, A_.add)
     ts(col(WN), a("wti"), -1.0, None, A_.mult)
-    ts(a("hi4"), a("hi4"), col(IS1), None, A_.mult)
+    ts(col(LW), col(IS0), -16.0, None, A_.mult)
+    ts(col(VW), col(IS0), -4096.0, None, A_.mult)
+    ts(col(MW), col(IS3), -U18, col(IS0), A_.mult, A_.add)
+    ts(col(TA), col(IS0), col(IS3), None, A_.add)
+    ts(col(BI), col(TA), SILU_ONE, None, A_.mult)
+    ts(col(SC), col(TA), -1.0, 1.0, A_.mult, A_.add)
+    ts(col(TA), col(IS1), 64.0, col(IS2), A_.mult, A_.add)
+    ts(col(TB), col(IS4), -64.0, col(TA), A_.mult, A_.add)
+    ts(col(DIG), col(TB), 1.0 / 4096, None, A_.mult)
+    ts(col(R8), col(R_), 8.0, 8.0, A_.is_ge, A_.mult)
+    ts(col(TA), col(R8), 2.0, -240.0 - (1 << 21), A_.mult, A_.add)
+    ts(col(J1), col(R_), 256.0, col(TA), A_.mult, A_.add)
+    ts(col(TA), col(IS1), col(IS4), 128.0, A_.add, A_.mult)
+    ts(col(DEAD), col(IS2), 127.0, col(TA), A_.mult, A_.add)
+    ts(col(TB), col(IS4), 128.0, None, A_.mult)
+    ts(a("hi4"), a("hi4"), col(IS1), col(TB), A_.mult, A_.add)
     ts(a("lo64"), a("lo64"), col(IS2), None, A_.mult)
     ts(a("biasb"), a("colf", 0, 12), col(IS1), 4.0, A_.mult, A_.mult)
-    tt(a("comb"), a("hi4"), a("lo64"), A_.add)
-    fill(a("win", W, W + 16), 0.0)
-    ts(a("m8"), a("colf", 0, 128), col(P16), None, A_.is_equal)
+    ts(a("m8a"), a("colf", 0, 128), col(P16), None, A_.is_equal)
+    ts(a("m8"), a("colf", 0, 128), col(P3), None, A_.is_equal)
+    tt(a("m8"), a("m8"), a("m8a"), A_.add)
     ts(a("idp"), a("colf", 0, 128), col(P_), None, A_.is_equal)
-    for b in range(12):
+    tt(a("comb"), a("hi4"), a("lo64"), A_.add)
+    for b in range(11, -1, -1):
         o = a(("pa", "pb", "pz", "psm", "pk", "pr")[b % 6], 0, 256)
-        mm(o, a("idp"), a("comb"), True, False)
-        mm(o, a("m8", p=p8), a("mkb", 256 * b, 256 * b + 256, p=p8), False, True)
-        act(a("win", 256 * b, 256 * b + 256), o, AF.Identity, a("biasb", b, b + 1))
-    for b in range(4):
-        act(a("dgw", 256 * b, 256 * b + 256), a("comb"), AF.Identity, a("biasb", b, b + 1))
-    for fam, w in (("zf", -4096.0), ("zm", col(MW)), ("zw", col(WN)), ("zd", col(DIG)), ("zl", col(LW)), ("zs", -1.0), ("zv", col(VW))):
-        ts(a(fam), a("colf", 0, 144), col(G15), w, A_.is_equal, A_.mult)
-    for fam, w in (("bd", col(DIG)), ("bl", col(LW)), ("bz", col(DIG4)), ("by", col(YW)), ("bo", 1.0), ("bn", -1.0)):
-        ts(a(fam), a("hi16"), col(G_), w, A_.is_equal, A_.mult)
-    for fam, s1, s2 in (("kl0", KA, TA), ("kl1", KB, KC), ("klr", KD, TA)):
-        ts(a(fam), a("rr", 0, 128), col(s1), col(s2), A_.mult, A_.add)
-    ts(a("kr"), a("colf"), col(IS1), col(N1), A_.mult, A_.add)
-    ts(a("rbig"), a("rr"), 0.0, 33554432.0, A_.is_equal, A_.mult)
-    ts(a("rmin"), a("rbig"), -1.0, 2.0, A_.mult, A_.add)
+        mm(o, a("idp"), a("comb"), True)
+        mm(o, a("m8", p=p8), a("mkb", 256 * b, 256 * b + 256, p=p8))
+        act(a("win", PAD + 256 * b, PAD + 256 * b + 256), o, AF.Identity, a("biasb", b, b + 1))
+    ts(a("zw"), a("colf", 0, 144), col(G15), col(WN), A_.is_equal, A_.mult)
+    ts(a("z1"), a("colf", 0, 144), col(G15), None, A_.is_equal)
+    for fam, w in (("zf", 1.0 / 256), ("zm", col(MW)), ("zl", col(LW)), ("zv", col(VW))):
+        ts(a(fam), a("z1"), w, None, A_.mult)
+    ts(a("bo"), a("hi16"), col(G_), None, A_.is_equal)
+    for fam, w in (("bd", col(DIG)), ("bw", col(WN)), ("bn", -1.0)):
+        ts(a(fam), a("bo"), w, None, A_.mult)
+    fill(a("c17"), 2 * U18)
+    fill(a("cq"), -0.25)
+    act(a("c256"), a("colf"), AF.Identity, 256.0, -1.0)
     ts(a("kseg"), a("rr"), 0.0, None, A_.not_equal)
-    ts(a("kne"), a("rr"), col(R_), None, A_.not_equal)
-    tt(a("kdg"), a("kseg"), a("kne"), A_.mult)
+    ts(a("rb"), a("kseg"), 64.0, -64.0, A_.mult, A_.add)
+    ts(a("rw"), a("rb"), -1.0, -4 * U18, A_.mult, A_.add)
+    ts(a("dm", 0, 256), a("rr"), col(R_), 2048.0, A_.is_ge, A_.mult)
+    fill(a("dm", 256, 384), 0.0)
+    ts(a("ndg", 0, 256), a("rr"), col(R_), None, A_.not_equal)
+    fill(a("ndg", 256, 512), 0.0)
+    ts(a("rup"), a("rb"), -1.0, None, A_.mult)
+    ts(a("dg"), a("rr", 0, 64), col(R_), 1048576.0, A_.is_equal, A_.mult)
     ts(a("lf"), a("colf", 0, 16), col(R16), None, A_.add)
-    ts(a("lr"), a("colf", 0, 16), col(RREV), None, A_.add)
-    iota(a("qp"), [[8, 2], [32, 8]])
-    ts(col(R8), col(R_), 8.0, 8.0, A_.is_ge, A_.mult)
     ts(a("lp"), a("qp"), col(R8), col(R_), A_.add, A_.add)
-    ts(a("l2"), a("colf", 0, 16), 16.0, col(R15), A_.mult, A_.add)
-    ts(a("ct"), a("colf", 0, 16), -16.0, col(R240), A_.mult, A_.add)
-    ts(a("oh"), a("colf", 0, 16), col(R15), None, A_.is_equal)
-    ts(a("idf"), a("colf", 0, 128), col(P_), None, A_.is_equal)
-    ts(a("idg"), a("colf", 0, 128), col(P_), -1.0, A_.is_equal, A_.mult)
-    ts(a("idn"), a("colf", 0, 128), col(P_), -1.0, A_.is_equal, A_.mult)
-    ts(a("e0"), a("colf", 0, 128), 0.0, col(IS0), A_.mult, A_.add)
+    ts(a("ct"), a("colf", 0, 16), -16.0, col(R255), A_.mult, A_.add)
+    ts(a("oh"), a("colf", 0, 16), col(K2), None, A_.is_equal)
+    ts(col(TA), col(R_), -4.0, 64.0, A_.mult, A_.add)
+    ts(a("rslot"), a("colf", 0, 4), -1.0, col(TA), A_.mult, A_.add)
+    for e, c in enumerate((DN0, DN1 if CFG["pair"] else DN0)):
+        ts(a("sp16", e, 16, 2), a("colf", 0, 8), 0.0, col(c), A_.mult, A_.add)
+    act(a("idg"), a("idp"), AF.Identity, 0.0, -1.0)
+    ts(a("idn"), a("idp"), -1.0, None, A_.mult)
+    ts(col(TA), col(IS0), 32.0, None, A_.mult)
+    ts(a("e0"), a("idp"), 0.0, col(TA), A_.mult, A_.add)
     ts(a("g8"), a("hi16"), col(P16), None, A_.is_equal)
-    fill(a("zero"), 0.0)
     fill(a("ones"), 1.0)
-    fill(a("ymb", 2048, 2064), 0.0)
-    fill(a("tab", L, L + 16), 0.0)
+    fill(a("tab", L, L + MIR + 32), 0.0)
+    for b in (0, 2064):
+        fill(a("vm", b, b + 16), 0.0)
+    for o in (a("mg", 0, 16), a("mg", 2064, 2080), a("mgr", 0, 16)):
+        ts(o, a("rr", 0, 16), 0.0, col(DEAD), A_.mult, A_.add)
     for t in range(NS):
         fill(a("snd%d" % t, 0, 80), 0.0)
-    asel(a("bt"), a("bn"), [[1, 128]], A_.is_ge, 0.0, 0, -1)
+    asel(a("bt"), a("bn"), [[-1, 128]], A_.is_ge, 0.0, 0, 1)
     asel(a("tri"), a("bt"), [[1, 128]], A_.not_equal, -256.0, 0, -1)
+    cp(a("idh"), a("idp"))
+    cp(a("bnh"), a("bn"))
+    for r in range(16):
+        asel(a("nsel", 128 * r, 128 * r + 128), a("bnh"), [[-16, 8], [0, 16]], A_.is_equal, 0.0, -r, 1)
     cp(a("tab", 0, L), a("oci"))
     cp(a("dlc"), a("dli"))
     dma("Y", a("dl8", p=p8), a("dlc"), 32)
     cp(a("thf", p=p8), a("thi", p=p8))
-    mm(a("prk", 48, 49), a("g8", p=p8), a("thf", p=p8), True, True)
-    act(a("thc"), a("prk", 48, 49), AF.Identity, 4096.0)
-    for h in range(2):
-        for r in range(16):
-            mm(a("pu", 32 * h, 32 * h + 32), sel("zw", r), a("x", 2048 + 8 * h + r + 8 * (r >> 3), W, 32), r == 0, r == 15)
-    ts(a("ui"), a("pu", 0, 64), -1.0, None, A_.mult)
-    ts(a("uu"), a("ui"), 4095, None, A_.bitwise_and)
-    tt(a("sq"), a("uu"), a("uu"), A_.mult)
-    ts(a("t32"), a("uu"), 1184.0, -float(CENTER), A_.mult, A_.add)
-    tt(a("base"), a("sq"), a("t32"), A_.add)
+    mm(a("prk", 48, 49), a("g8", p=p8), a("thf", p=p8), True)
+    act(a("thc"), a("prk", 48, 49), AF.Identity, -129.0 / 256, 1.0 / 256)
+
+    def first_places(n, x0, x1, at):
+        for h in range(2):
+            for r in range(16):
+                mm(a("pu", n * h, n * h + n), sel("zw", r), a("x", x0 + 8 * h + r + 8 * (r >> 3), x1, 32), r == 0)
+        n *= 2
+        ts(a("ui", 0, n), a("pu", 0, n), -1.0, None, A_.mult)
+        ts(a("uu", 0, n), a("ui", 0, n), 4095, None, A_.bitwise_and)
+        tt(a("sq", 0, n), a("uu", 0, n), a("uu", 0, n), A_.mult)
+        ts(a("t32", 0, n), a("uu", 0, n), 1184.0, None, A_.mult)
+        tt(a("zz", 0, n), a("sq", 0, n), a("t32", 0, n), A_.add)
+        if at:
+            ts(a("base", at, at + n), a("zz", 0, n), 32736, None, A_.bitwise_and)
+        else:
+            ts(a("li", 0, n), a("zz", 0, n), 5, 1023, A_.arith_shift_right, A_.bitwise_and)
+            cp(a("l0"), a("li", 0, n))
+
+    first_places(8, top, W, 0)
+    first_places(24, 2048, top, 16)
 
     def yrep(dst, who, src, neg, n=256, at=0, pos=None):
         for k, eng in enumerate(who):
@@ -274,229 +305,257 @@ def rank_program(g, core, T, topo):
                 cp(o, src)
             elif eng == "S":
                 act(o, src, AF.Identity, 0.0, -1.0 if neg else 1.0)
-            elif eng == "s":
-                f = src[1][0]
-                for b in range(0, n, 64):
-                    act(a(dst, 16 * (at + b) + k, 16 * (at + b + 64), 16), a(f[0], f[1] + b, f[1] + b + 64), AF.Identity, 0.0, -1.0)
             else:
                 asel(o, pos or src, [[0, n]], A_.is_ge, 0.0, 0, 0)
 
     def ycols(t):
         return a("x", W - 256 * (t + 1), W - 256 * t)
 
-    def names(dst, lst, t, first=False):
-        ts(dst, ind(a("oci") if first else a("tab", 0, L), lst), (11 - t) / 16.0, -15.0 / 32, A_.mult, A_.add)
+    def names(dst, tab, lst, t):
+        ts(dst, ind(tab, lst), (11 - t) / 16.0, -15.0 / 32, A_.mult, A_.add)
 
-    def main(c, yr, rev, fch, mch):
+    def at16(j):
+        return 16 + j + 16 * (j >= 2048)
+
+    def opened(bank, n, dead=True):
+        mm(a(bank, 0, n), a("c17", p=p1), a("c256", 0, n, p=p1), True)
+        if dead:
+            mm(a(bank, 0, n), a("cq", p=p1), a("rb", 0, n, p=p1))
+
+    marks = a("win", PAD, PAD + W)
+
+    def main(c, yr, hop, fch, mch):
         u = 0
         for w in fch:
-            tt(a("vm", 256 * u, 256 * (u + w)), ind(a("x"), a(c, 16 * u, 16 * (u + w))), a(yr, 256 * u, 256 * (u + w)), A_.min)
+            o = at16(256 * u)
+            tt(a("vm", o, o + 256 * w), ind(a("x"), a(c, 16 * u, 16 * (u + w))), a(yr, 256 * u, 256 * (u + w)), A_.min)
             u += w
         u = 0
         for w in mch:
-            o, i = a("mg", 256 * u, 256 * (u + abs(w))), ind(a("win"), a(c, 16 * u, 16 * (u + abs(w))))
+            o = at16(256 * u)
+            o, i = a("mg", o, o + 256 * abs(w)), ind(marks, a(c, 16 * u, 16 * (u + abs(w))))
             act(o, i) if w > 0 else cp(o, i)
             u += abs(w)
-        if rev:
-            mm(a("pk", 0, 256), a("kl1", p=k3), a("kr", p=k3), True, False)
+        for h, bank in enumerate(("pk",) if hop else ("pr", "pk")):
+            n = 256 if hop else 128
+            opened(bank, n)
             for u in range(16):
+                mm(a(bank, 0, n, 16), sel("zl", u), a("lvn", u, 256, 16) if hop else a("lvn", 16 * u + 8 * h, 16 * u + 8 * h + 8))
                 for buf, fam in (("vm", "zf"), ("mg", "zm")):
-                    mm(a("pk", 0, 256), sel(fam, 15 - u), a(buf, 256 * u, 256 * u + 256), False, False)
-            return
-        for h, bank in enumerate(("pr", "pk")):
-            mm(a(bank, 0, 128), a("kl0", p=k3), a("kr", 0, 128, p=k3), True, False)
-            for u in range(16):
-                for buf, fam in (("vm", "zf"), ("mg", "zm")):
-                    mm(a(bank, 0, 128), sel(fam, u), a(buf, 2048 * h + 128 * u, 2048 * h + 128 * u + 128), False, False)
+                    o = at16(2048 * h + n * u)
+                    mm(a(bank, 0, n), sel(fam, u), a(buf, o, o + n))
 
-    def live(order, r):
-        if order in (10, 11):
-            return a("lvn", 16 * r + 8 * (order - 10), 16 * r + 8 * (order - 9))
-        return a("lvn", 15 - r, 256, 16) if order == 2 else a("val", r, 64, 16)
-
-    def distinct(bank, order, dig, n, s, dummy, at=0):
+    def distinct(bank, dig, n, dummy, at=0):
         q, e = n // 16, at // 16
-        mm(a(bank, 0, 512), a("zero", p=slice(0, 1)), a("x", 2048, 2560, p=slice(0, 1)), True, False)
-        for r in range(16):
-            mm(a(bank, r, n, 16), sel("zl", r), live(order, r), False, False)
-        if order >= 10:
-            for r in range(8):
-                mm(a(bank, 256 + 16 * r, 272 + 16 * r), a("bl"), a("lvn", 8 * (order - 10) + r, 256, 16), False, False)
-        elif order:
-            for r in range(16):
-                mm(a(bank, 256 + r, 256 + n, 16), a("bl"), live(order, r), False, False)
-        else:
-            mm(a(bank, 256, 256 + n), a("bl"), a("val"), False, False)
-        for r in range(16):
-            mm(a(bank, r, n, 16), sel("zd", r), a(dig, at + r, at + n, 16), False, False)
-        mm(a(bank, 256, 256 + n), a("bd"), a(dig, at, at + n), False, True)
-        scan(a("prop" + s, 0, n), a("kdg", 0, n), a(bank, 0, n), A_.mult, A_.add)
-        tt(a("eq" + s, 0, n), a("prop" + s, 0, n), a(bank, 256, 256 + n), A_.is_equal)
-        scan(a("cn" + s, 0, n), a("kseg", 0, n), a("eq" + s, 0, n), A_.mult, A_.add)
-        tt(a("vv" + s, 0, q), a("prop" + s, 15, n, 16), a("cn" + s, 15, n, 16), A_.add)
-        ts(a("off" + s, 2 * e, 2 * (e + q), 2), a("vv" + s, 0, q), 4096.0, col(dummy), A_.mult, A_.min)
+        mm(a(bank, 0, 256 + n), a("idp"), a("ndg", 0, 256 + n), True)
+        mm(a(bank, 0, n), a("bd"), a(dig, at, at + n))
+        mm(a(bank, 256, 256 + n), a("bd"), a(dig, at, at + n))
+        scan(a("prop", 0, n), a("rup", 0, n), a(bank, 0, n), A_.add, A_.min)
+        tt(a("eqa", 0, n), a("prop", 0, n), a(bank, 256, 256 + n), A_.is_equal)
+        scan(a("cna", 0, n), a("eqa", 0, n), a(bank, 0, n), A_.add, A_.min)
+        ts(a("offa", 2 * e, 2 * (e + q), 2), a("cna", 15, n, 16), 4096.0, col(dummy), A_.mult, A_.min)
 
-    def best(bank, n, dst):
+    def best(bank, n, dst, first):
         q = n // 16
-        scan(a("rs", 0, n), a("rbig", 0, n), a(bank, 0, n), A_.add, A_.min)
-        cp(a("ji", 0, q), a("rs", 15, n, 16))
-        ts(a("ja", 0, q), a("ji", 0, q), 4095, None, A_.bitwise_and)
-        cp(dst, a("ja", 0, q))
+        scan(a("rs", 0, n), a("kseg", 0, n), a(bank, 0, n), A_.mult, A_.max)
+        ts(a("ji", 0, q), a("rs", 15, n, 16), -1 / U18, None, A_.mult)
+        ts(a("ja", 0, q), a("ji", 0, q), 1, 511 + (1 << 21), A_.arith_shift_right, A_.bitwise_and)
+        ts(dst, a("ja", 0, q), col(first), 0.0, A_.add, A_.max)
 
-    def place(b, n, dst, t):
-        acol = -float(CENTER) if t == 0 else a("ac", 2 * t + 1, 2 * t + 2)
-        cp(a("ui", b, n), a("pu", b, n))
+    def place(src, b, n, dst, t):
+        cp(a("ui", b, n), src)
         ts(a("uu", b, n), a("ui", b, n), 4095, None, A_.bitwise_and)
         tt(a("sq", b, n), a("uu", b, n), a("uu", b, n), A_.mult)
-        ts(a("t32", b, n), a("uu", b, n), 1184.0, acol, A_.mult, A_.add)
+        ts(a("t32", b, n), a("uu", b, n), 1184.0, a("ac", t, t + 1) if t else 0.0, A_.mult, A_.add)
         tt(a("zz", b, n), a("sq", b, n), a("t32", b, n), A_.add)
         ts(a("li", b, n), a("zz", b, n), 5, 1023, A_.arith_shift_right, A_.bitwise_and)
         cp(a(dst, b, n), a("li", b, n))
 
-    def mark(src, lst, order, n, at=0):
-        ad, adf = ("ad", "adf") if order else ("adr", "adfr")
+    def mark(src, lst, bank, n, at=0, names_=("ad", "adf")):
+        ad, adf = names_
         act(a(ad, at, at + n), ind(src, lst))
         act(a(adf, at, at + n), a(ad, at, at + n), AF.Identity, col(BI), col(SC))
-        distinct("pb" if order == 11 else "pa", order, ad, n, "a", DM, at)
+        distinct(bank, ad, n, DM, at)
         for q in range(at // 16, (at + n) // 16):
             act(ind(a("win"), a("offa", 2 * q, 2 * q + 1)), a(adf, 16 * q, 16 * q + 16), AF.Silu)
 
     def ya_out(t, h):
-        mm(a("pz", 0, 256), a("by"), a("lvn"), True, False)
+        if h:
+            mm(a("pz", 0, 256), a("bd"), a("ad"), True)
+        for r in range(0 if h else 16):
+            mm(a("pz", r, 256, 16), a("bd"), a("ad", 16 * r, 16 * r + 16), True)
+        act(a("yab", 256 * (2 * t + h), 256 * (2 * t + h + 1)), a("pz", 0, 256), AF.Identity, -float(PAD), 4096.0)
+
+    def name_offsets():
         for r in range(16):
-            if h:
-                mm(a("pz", 15 - r, 256, 16), a("bz"), a("ad", r, 256, 16), False, False)
-            else:
-                mm(a("pz", r, 256, 16), a("bz"), a("ad", 16 * r, 16 * r + 16), False, False)
-        act(a("zr"), a("pz", 0, 256), AF.Relu, -16511.0)
-        act(a("yab", 256 * (2 * t + h), 256 * (2 * t + h + 1)), a("zr"), AF.Identity, -1.0)
+            mm(a("psm", 0, 16), sel("zv", r), a("lvn", r, 256, 16), r == 0)
+        mm(a("psm", 0, 16), a("idh"), a("sp16"))
+        tt(a("lw"), a("li", 16, 32), a("psm", 0, 16), A_.max)
+        n = 384 if CFG["pair"] else 256
+        mm(a("pb", 0, n), a("idp"), a("dm", 0, n), True)
+        for r in range(16):
+            ns = a("nsel", 128 * r, 128 * r + 128)
+            mm(a("pb", r, 256, 16), a("idh"), a("lw"))
+            mm(a("pb", r, 256, 16), ns, a("lw"))
+            if CFG["pair"]:
+                mm(a("pb", 256 + r, 384, 16), a("idh"), a("lw", 1, 16, 2))
+                mm(a("pb", 256 + r, 384, 16), ns, a("lw", 0, 16, 2))
+        ts(a("eqn", 0, n), a("pb", 0, n), 0.0, 2048.0, A_.is_equal, A_.mult)
+        mm(a("psm", 0, 16), a("idh"), a("lw"), True)
+        for r in range(16):
+            mm(a("psm", 0, 16), a("idp"), a("eqn", r, 256, 16))
+            if CFG["pair"]:
+                mm(a("psm", 1, 16, 2), a("idp"), a("eqn", 256 + r, 384, 16))
+        if CFG["pair"]:
+            for e, c in enumerate((DN0, DN1)):
+                ts(a("offn", e, 16, 2), a("psm", e, 16, 2), col(c), None, A_.min)
+        else:
+            ts(a("offn", 0, 32, 2), a("psm", 0, 16), col(DN0), None, A_.min)
 
     yrbuf = ["yr0", "yr1"]
-
-    def first_y(t, who):
-        act(a("y0p"), ind(ycols(t), a("lp")))
-        yrep(yrbuf[t % 2], who, a("y0p"), False)
-
-    first_y(0, CFG["y00"])
-    first_y(1, "G" * 16)
+    act(a("y0p"), ind(ycols(0), a("lp")))
     for h in range(2):
-        ts(a("lb", 8 * h, 8 * h + 8), a("base", 32 * h + 24, 32 * h + 32), 5, 1023, A_.arith_shift_right, A_.bitwise_and)
+        yrep("yr0", CFG["y00"][h], a("y0p", 128 * h, 128 * h + 128), False, 128, 128 * h)
+
+    def first_y(t):
+        act(a("y0p"), ind(ycols(t), a("lp")))
+        yrep(yrbuf[t % 2], "G" * 16, a("y0p"), False)
+
+    first_y(1)
+    fill(a("win", 0, PAD), 0.0)
+    fill(a("win", PAD + W, PAD + W + 16), 0.0)
+    fill(a("ymb", PAD + 2048, PAD + 2064), 0.0)
+    fill(a("ymb", 0, PAD), 0.0)
 
     for t in range(NS):
         B = W - 256 * (t + 1)
-        cp(a("l0"), a("lb"))
-        names(a("c0"), a("l0"), t, t == 0)
-        asel(a("lvn"), a("win", B, B + 256), [[0, 256]], A_.is_ge, 0.0, 0, 0)
+        table = a("tab", 0, L)
+        for h in range(2):
+            names(a("c0", 128 * h, 128 * h + 128), a("tab", 0, L + MIR) if t else a("oci"), a("l0", 8 * h, 8 * h + 8), t)
+        asel(a("lvn"), a("win", PAD + B, PAD + B + 256), [[0, 256]], A_.is_ge, 0.0, 0, 0)
         act(a("y0f"), ind(ycols(t), a("lf")))
-        wide([("g8", "dl8", 256 * t)], p8)
-        act(a("dln"), a("pu", 256, 512))
-        act(a("dlp"), ind(a("dln"), a("l2")))
-        main("c0", yrbuf[t % 2], False, CFG["f0"], CFG["m0"] if t else CFG["m00"])
+        main("c0", yrbuf[t % 2], 0, CFG["f0"], CFG["m0"] if t else CFG["m00"])
         if t + 2 < NS:
-            first_y(t + 2, "G" * 16)
+            first_y(t + 2)
         for h, bank in enumerate(("pr", "pk")):
             j, b = a("j16", 8 * h, 8 * h + 8), 128 * h
-            best(bank, 128, j)
-            tt(a("y1n", b, b + 128), ind(a("vm", 16 * b, 16 * b + 2048), j), a("y0f", b, b + 128), A_.subtract)
+            best(bank, 128, j, J0)
+            tt(a("y1n", b, b + 128), ind(a("vm", 2064 * h, 2064 * h + 2064), j), a("y0f", b, b + 128), A_.subtract)
             if "G" in CFG["yh"][h]:
                 act(a("y1p", b, b + 128), a("y1n", b, b + 128), AF.Identity, 0.0, -1.0)
             yrep("yrh", CFG["yh"][h], a("y1n", b, b + 128), True, 128, b, a("y1p", b, b + 128))
-            mark(a("mg", 16 * b, 16 * b + 2048), j, 10 + h, 128, b)
+            mark(a("mg", 2064 * h, 2064 * h + 2064), j, ("pa", "pb")[h], 128, b)
             for r in range(16):
-                mm(a("pu", 8 * h, 8 * h + 8), sel("zw", r), a("y1n", b + r, b + 128, 16), r == 0, r == 15)
+                mm(a("pu", 8 * h, 8 * h + 8), sel("zw", r), a("y1n", b + r, b + 128, 16), r == 0)
             if h:
                 for r in range(16):
-                    mm(a("pu", 16, 32), sel("zw", 15 - r), a("y1n", 16 * r, 16 * r + 16), r == 0, r == 15)
-            place(8 * h, 32 if h else 8, "l1", t)
-            names(a("c1", b, b + 128), a("l1", 8 * h, 8 * h + 8), t)
+                    mm(a("pu", 16, 32), sel("zw", r), a("y1n", 16 * r, 16 * r + 16), r == 0)
+            place(a("pu", 8 * h, 32 if h else 8), 8 * h, 32 if h else 8, "l1", t)
+            names(a("c1", b, b + 128), table, a("l1", 8 * h, 8 * h + 8), t)
         ya_out(t, 0)
-        act(a("y1r"), ind(a("y1n"), a("lr")), AF.Identity, 0.0, -1.0)
-        act(a("nn"), ind(a("tab"), a("l1", 16, 32)))
-        wide([("idf", "dlp", 0), ("idg", "nn", 0)])
-        act(a("t2"), a("pu", 256, 512))
-        main("c1", "yrh", True, CFG["f1"], CFG["m1"])
-        act(a("ld"), ind(a("dgw"), a("l1", 16, 32)))
-        distinct("pb", 2, "ld", 256, "n", DN)
-        best("pk", 256, a("j16"))
+        act(a("y1r"), ind(a("y1n"), a("lf")), AF.Identity, 0.0, -1.0)
+        act(a("nn"), ind(table, a("l1", 16, 32)))
+        for b in range(0, 256, 64):
+            mm(a("pz", 256 + b, 320 + b), a("g8", p=p8), a("dl8", 256 * t + b, 256 * t + b + 64, p=p8), True)
+            mm(a("pz", 256 + b, 320 + b), a("idg"), a("nn", b, b + 64))
+        act(a("t2"), a("pz", 256, 512))
+        for r in range(16):
+            mm(a("prk", 64, 80), sel("zf", r), a("y1n", 16 * r, 16 * r + 16), r == 0)
+        act(a("thr"), a("prk", 64, 80), AF.Identity, a("thc"))
+        main("c1", "yrh", 1, CFG["f1"], CFG["m1"])
+        name_offsets()
+        best("pk", 256, a("j16"), J1)
         tt(a("y2n"), ind(a("vm"), a("j16")), a("y1r"), A_.subtract)
-        for r in range(16):
-            mm(a("psm", 0, 16), sel("zv", r), live(2, r), r == 0, False)
-        for r in range(16):
-            mm(a("psm", 0, 16), sel("zs", r), a("y2n", r, 256, 16), False, r == 15)
-        ts(a("rdy"), a("psm", 0, 16), a("thc"), None, A_.is_ge)
+        tt(a("dd"), a("rs", 15, 256, 16), a("thr"), A_.add)
+        ts(a("jm"), a("ji"), 1, None, A_.bitwise_and)
+        tt(a("rdy"), a("jm"), a("dd"), A_.is_gt)
         scan(a("pre"), a("kseg", 0, 16), a("rdy"), A_.mult, A_.add)
         tt(a("rp"), a("rdy"), a("ct"), A_.mult)
-        mm(a("prk", 0, 16), a("idp"), a("ct"), True, False)
-        mm(a("prk", 0, 16), a("tri"), a("rdy"), False, False)
-        mm(a("prk", 0, 16), a("bo"), a("pre"), False, False)
-        mm(a("prk", 0, 16), a("idn"), a("rp"), False, True)
-        mm(a("prk", 16, 17), a("bo"), a("pre", 15, 16), True, True)
+        mm(a("prk", 0, 16), a("idp"), a("ct"), True)
+        mm(a("prk", 0, 16), a("tri"), a("rdy"))
+        mm(a("prk", 0, 16), a("bo"), a("pre"))
+        mm(a("prk", 0, 16), a("idn"), a("rp"))
+        mm(a("pu", 64, 65), a("bo"), a("pre", 15, 16), True)
         snd, land = "snd%d" % t, "land%d" % t
         ts(a("slot"), a("prk", 0, 16), 255.0, None, A_.add)
-        ts(a(snd, 0, 1), a("prk", 16, 17), 64.0, None, A_.min)
+        act(a(snd, 0, 1), a("pu", 64, 65), AF.Relu, 64.0, -1.0)
         cp(ind(a(snd, 16, 528), a("slot")), a("y2n"))
         dst = T.cores[(rank + 1 + t % (nrank - 1)) % nrank]
         rid, pid = topo.addr(dst, core)
         mask = sum(1 << e for e in topo.engines(core, dst)[:NENG])
         rec("G", lambda t=t, rid=rid, pid=pid, mask=mask: g.remote_dma(
             a("land%d" % t)[0], a("snd%d" % t, 0, 80)[0], T.sem["arr%d" % t], T.sem.sent, pid, rid, mask),
-            [], [a(snd, 0, 80)], 300, "r")
-        ops.append(["A", None, [], [(land, 0, 80, 1)], ("a", t, len(ops) - 1), 0, CFG["remote"]])
-        scan(a("rm"), a("rmin"), a("pk", 0, 256), A_.add, A_.max)
-        ts(a("ki"), a("rm", 15, 256, 16), 1.0, None, A_.add)
-        ts(a("ka"), a("ki"), 15, None, A_.bitwise_and)
+            [], [a(snd, 0, 80)], ("n", 300), "r")
+        ops.append(["A", None, [], [(land, 0, 80, 1)], ("a", t, len(ops) - 1), ("n", 0), ("r", 0)])
+        scan(a("rm"), a("rw"), a("pk", 0, 256), A_.add, A_.min)
+        ts(a("ki"), a("rm", 15, 256, 16), 1 / U18, 1.0, A_.mult, A_.add)
+        ts(a("ka"), a("ki"), 1, 15, A_.arith_shift_right, A_.bitwise_and)
         cp(a("k16"), a("ka"))
-        mark(a("mg"), a("j16"), 2, 256)
+        mark(a("mg"), a("j16"), "pa", 256)
         ya_out(t, 1)
         if t == NS - 1:
             dma("Y", ext(T.ya[:]), a("yab", p=g16), 64)
         tt(a("t1"), ind(a("oh"), a("k16")), a("t2"), A_.mult)
-        for q in range(15, -1, -1):
-            tt(ind(a("tab"), a("offn", 2 * q, 2 * q + 1)), a("t1", 16 * q, 16 * q + 16), a("nn", 16 * q, 16 * q + 16), A_.add)
+        step = 32 if CFG["pair"] else 16
+        for q in range(256 // step - 1, -1, -1):
+            tt(ind(a("tab"), a("offn", 2 * q, 2 * q + step // 16)), a("t1", step * q, step * q + step), a("nn", step * q, step * q + step), A_.add)
         if t == NS - 1:
-            dma("Y", ext(T.yo[:]), a("tab", 0, L), 512)
-        for r in range(16):
-            mm(a("pu", 0, 4), sel("zw", r), a(land, 16 + r, 80, 16), r == 0, r == 15)
+            dma("Y", ext(T.yo[:]), table, 512)
+        else:
+            act(a("tab", L, L + MIR), a("tab", 0, MIR))
+        if CFG["uscan"]:
+            mm(a("pu", 0, 64), a("idp"), a("dg"), True)
+            mm(a("pu", 0, 64), a("bw"), a(land, 16, 80))
+            scan(a("us"), a("kseg", 0, 64), a("pu", 0, 64), A_.mult, A_.max)
+            place(a("us", 15, 64, 16), 0, 4, "lv", t)
+        else:
+            for r in range(16):
+                mm(a("pu", 0, 4), sel("zw", r), a(land, 16 + r, 80, 16), r == 0)
+            place(a("pu", 0, 4), 0, 4, "lv", t)
         yrep("yrr", CFG["yrr"], a(land, 16, 80), True, 64)
-        ts(a("val"), a("slotc"), a(land, 0, 1), None, A_.is_lt)
-        place(0, 4, "lv", t)
-        names(a("cr"), a("lv"), t)
+        ts(a("inv"), a("rslot"), a(land, 0, 1), 16.0, A_.is_le, A_.mult)
+        names(a("cr"), table, a("lv"), t)
         if t + 1 < NS:
             u = t + 1
-            mm(a("prk", 32, 33), a("e0"), a(land, 0, 1), True, True)
-            cp(a("ai", 0, 1), a("prk", 32, 33))
-            ts(a("ai", 1, 2), a("ai", 0, 1), 63, None, A_.bitwise_and)
-            ts(a("ac", 2 * u, 2 * u + 1), a("ai", 1, 2), 32.0, None, A_.mult)
-            ts(a("ac", 2 * u + 1, 2 * u + 2), a("ai", 1, 2), 32.0, -float(CENTER), A_.mult, A_.add)
+            mm(a("prk", 32, 33), a("e0"), a(land, 0, 1), True)
+            ts(a("ai"), a("prk", 32, 33), -1.0 / 2048, -31.5 / 64, A_.mult, A_.add)
+            ts(a("ac", u, u + 1), a("ai"), -2048.0, a("prk", 32, 33), A_.mult, A_.subtract)
             for h in range(2):
-                b = 32 * h + 8 * (3 - u)
-                ts(a("zb", 8 * h, 8 * h + 8), a("base", b, b + 8), a("ac", 2 * u, 2 * u + 1), None, A_.add)
-            ts(a("lb"), a("zb"), 5, 1023, A_.arith_shift_right, A_.bitwise_and)
-        mm(a("pr", 0, 64), a("klr", p=k3), a("kr", 0, 64, p=k3), True, False)
+                b = 16 + 24 * h + 8 * (3 - u)
+                ts(a("l0", 8 * h, 8 * h + 8), a("base", b, b + 8), a("ac", u, u + 1), 1.0 / 32, A_.add, A_.mult)
+        opened("pr", 64, False)
+        mm(a("pr", 0, 64, 16), a("idp"), a("inv"))
         u = 0
         for w in CFG["rch"]:
             c = a("cr", 4 * u, 4 * (u + w))
-            tt(a("vmr", 64 * u, 64 * (u + w)), ind(a("x"), c), a("yrr", 64 * u, 64 * (u + w)), A_.min)
-            act(a("mgr", 64 * u, 64 * (u + w)), ind(a("win"), c))
+            tt(a("vmr", 16 + 64 * u, 16 + 64 * (u + w)), ind(a("x"), c), a("yrr", 64 * u, 64 * (u + w)), A_.min)
+            act(a("mgr", 16 + 64 * u, 16 + 64 * (u + w)), ind(marks, c))
             for r in range(u, u + w):
-                mm(a("pr", 0, 64), sel("zf", r), a("vmr", 64 * r, 64 * r + 64), False, False)
-                mm(a("pr", 0, 64), sel("zm", r), a("mgr", 64 * r, 64 * r + 64), False, r == 15)
+                mm(a("pr", 0, 64), sel("zf", r), a("vmr", 16 + 64 * r, 80 + 64 * r))
+                mm(a("pr", 0, 64), sel("zm", r), a("mgr", 16 + 64 * r, 80 + 64 * r))
             u += w
-        best("pr", 64, a("jr"))
+        best("pr", 64, a("jr"), JR)
         if t + 1 < NS:
-            mark(a("mgr"), a("jr"), 0, 64)
+            mark(a("mgr"), a("jr"), "pa", 64, 0, ("adr", "adfr"))
         if t == NS - 2:
-            dma("G", ext(T.ym[:, 2048:W]), a("win", 2048, W, p=g16), 16)
+            dma("G", ext(T.ym[:, 2048:W]), a("win", PAD + 2048, PAD + W, p=g16), 16)
         if t == NS - 1:
-            for b in range(0, 2048, 256):
-                cp(a("ymb", b, b + 256), a("win", b, b + 256))
+            for b in range(PAD, PAD + 2048, 256):
+                act(a("ymb", b, b + 256), a("win", b, b + 256))
             act(a("adr"), ind(a("mgr"), a("jr")))
-            distinct("pa", 0, "adr", 64, "a", DY)
+            distinct("pa", "adr", 64, DY)
             for q in range(4):
                 cp(ind(a("ymb"), a("offa", 2 * q, 2 * q + 1)), a("ones"))
-            dma("Y", ext(T.ym[:, 0:2048]), a("ymb", 0, 2048, p=g16), 32)
+            dma("Y", ext(T.ym[:, 0:2048]), a("ymb", PAD, PAD + 2048, p=g16), 32)
 
     emit(g, T, ops, QO)
+
+
+def price(c, m):
+    cyc, gather, scatter, fused, pe, wake, dma, remote = m
+    k, n = c
+    return {"c": n * cyc, "g": 55 + n * gather * cyc, "f": 55 + n * max(gather, fused) * cyc, "s": 55 + n * scatter * cyc,
+            "p": n * pe, "n": n, "d": dma + 7 * n, "r": remote}[k]
 
 
 def emit(g, T, ops, QO):
@@ -511,6 +570,7 @@ def emit(g, T, ops, QO):
         return slice(0, 1) if f[0] in _PS else slice(f[1], f[2], f[3])
 
     member = {k: [] for k in _PS}
+    opener = {}
     group, last = {}, {}
     for i, (q, fn, rd, wr, kind, cost, lat) in enumerate(o[:7] for o in ops):
         if kind == "d":
@@ -530,14 +590,13 @@ def emit(g, T, ops, QO):
                 if ops[i][7]:
                     order.update(member[f[0]])
                     member[f[0]] = []
+                    opener[f[0]] = i
                 member[f[0]].append(i)
-                group[i] = member[f[0]][0]
+                group[i] = opener[f[0]]
                 order.add(group[i])
                 order.discard(i)
             else:
-                for w in np.unique(writer[f[0]][cols(f)]):
-                    if w >= 0:
-                        (order if semof[w] == me and kind == "c" and not CFG["waw"] else need).add(int(w))
+                need.update(int(w) for w in np.unique(writer[f[0]][cols(f)]) if w >= 0)
             keep = []
             for r, m in reader[f[0]]:
                 if m[cols(f)].any():
@@ -555,63 +614,15 @@ def emit(g, T, ops, QO):
         need.discard(i)
         if fn is None:
             order.add(kind[2])
-        if wr and wr[0][0] in ("vm", "mg", "vmr", "mgr"):
+        if wr and wr[0][0] in ("vm", "mg", "vmr", "mgr") and cost[0] in "fg":
             if (q, wr[0][0]) in last:
                 order.add(last[q, wr[0][0]])
             last[q, wr[0][0]] = i
         deps.append(need)
         soft.append(order - need)
-    wake = CFG["wake"]
-    rank_, succ = [0.0] * n, [[] for _ in range(n)]
-    for i in range(n):
-        for d in deps[i]:
-            succ[d].append((i, wake + ops[d][6]))
-        for d in soft[i]:
-            succ[d].append((i, 0.0))
-    for i in range(n - 1, -1, -1):
-        rank_[i] = ops[i][5] + max([ops[i][6]] + [w + rank_[j] for j, w in succ[i]])
-    pred = [[] for _ in range(n)]
-    for i in range(n):
-        for j, w in succ[i]:
-            pred[j].append((i, w))
-
-    def schedule(prio, nxt, prv):
-        left = [len(p) for p in prv]
-        ready, end = [0.0] * n, [0.0] * n
-        pool = {q: [] for q in list(QO) + ["A"]}
-        for i in range(n):
-            if not left[i]:
-                pool[ops[i][0]].append(i)
-        free = {q: 0.0 for q in pool}
-        seq = []
-        while len(seq) < n:
-            now, q = min((max(free[q], min(ready[i] for i in pool[q])), q) for q in pool if pool[q])
-            i = max((i for i in pool[q] if ready[i] <= now), key=lambda i: (prio[i], -i))
-            soon = [j for j in pool[q] if now < ready[j] <= now + CFG["look"] * ops[i][5] and prio[j] > prio[i]]
-            if soon:
-                i = max(soon, key=lambda j: prio[j])
-                now = ready[i]
-            pool[q].remove(i)
-            seq.append(i)
-            end[i] = free[q] = now + ops[i][5]
-            for j, w in nxt[i]:
-                ready[j] = max(ready[j], free[q] + w)
-                left[j] -= 1
-                if not left[j]:
-                    pool[ops[j][0]].append(j)
-        return seq, end, max(end[i] + ops[i][6] for i in range(n))
-
-    seq, end, length = schedule(rank_, succ, pred)
-    CFG["path"] = max(rank_)
-    rng = np.random.RandomState(CFG["seed"])
-    prio = np.array(rank_)
-    for _ in range(0 if "seq" in CFG else CFG["passes"]):
-        trial = prio + rng.normal(0.0, CFG["shift"], n) * (rng.rand(n) < CFG["share"])
-        s2, end, l2 = schedule(trial.tolist(), succ, pred)
-        if l2 < length:
-            seq, length, prio = s2, l2, trial
-    seq = CFG.setdefault("seq", seq)
-    CFG["span"] = length
+    if "seq" not in CFG:
+        CFG["seq"] = arrange(ops, deps, soft, list(QO) + ["A"])
+    seq = CFG["seq"]
     wanted = set()
     for d in deps:
         wanted |= d
@@ -650,3 +661,92 @@ def emit(g, T, ops, QO):
     for s, v in count.items():
         if v and known["G"].get(s, 0) < v:
             g.wait_ge(T.sem[s], v)
+
+
+def arrange(ops, deps, soft, queues):
+    n = len(ops)
+    models = CFG["models"]
+    mean = [sum(m[k] for m in models) / len(models) for k in range(len(models[0]))]
+    qof = [o[0] for o in ops]
+
+    def tables(m):
+        cost = [price(o[5], m) for o in ops]
+        lat = [price(o[6], m) for o in ops]
+        prv = [[(d, m[5] + lat[d]) for d in deps[i]] + [(d, 0.0) for d in soft[i]] for i in range(n)]
+        return cost, lat, prv
+
+    cost, lat, prv = tables(mean)
+    nxt = [[] for _ in range(n)]
+    for i in range(n):
+        for d, w in prv[i]:
+            nxt[d].append((i, w))
+    rank_ = [0.0] * n
+    for i in range(n - 1, -1, -1):
+        rank_[i] = cost[i] + max([lat[i]] + [w + rank_[j] for j, w in nxt[i]])
+    each = [tables(m) for m in models]
+
+    def length(seq):
+        total = []
+        for c, la, pv in each:
+            end, free, top = [0.0] * n, {q: 0.0 for q in queues}, 0.0
+            for i in seq:
+                s = free[qof[i]]
+                for d, w in pv[i]:
+                    if end[d] + w > s:
+                        s = end[d] + w
+                end[i] = free[qof[i]] = s + c[i]
+                if end[i] + la[i] > top:
+                    top = end[i] + la[i]
+            total.append(top)
+        return total
+
+    def schedule(prio, prv=prv, nxt=nxt, end=None):
+        left = [len(p) for p in prv]
+        ready = [0.0] * n
+        pool = {q: [] for q in queues}
+        for i in range(n):
+            if not left[i]:
+                pool[qof[i]].append(i)
+        free = {q: 0.0 for q in pool}
+        seq = []
+        while len(seq) < n:
+            now, q = min((max(free[q], min(ready[i] for i in pool[q])), q) for q in pool if pool[q])
+            i = max((i for i in pool[q] if ready[i] <= now), key=lambda i: (prio[i], -i))
+            soon = [j for j in pool[q] if now < ready[j] <= now + CFG["look"] * cost[i] and prio[j] > prio[i]]
+            if soon:
+                i = max(soon, key=lambda j: prio[j])
+                now = ready[i]
+            pool[q].remove(i)
+            seq.append(i)
+            free[q] = now + cost[i]
+            if end is not None:
+                end[i] = free[q]
+            for j, w in nxt[i]:
+                ready[j] = max(ready[j], free[q] + w)
+                left[j] -= 1
+                if not left[j]:
+                    pool[qof[j]].append(j)
+        return seq
+
+    seq = schedule(rank_)
+    span = length(seq)
+    rng = np.random.RandomState(CFG["seed"])
+    prio = np.array(rank_)
+    back = rank_
+    for _ in range(CFG["turns"]):
+        fwd, bwd = [0.0] * n, [0.0] * n
+        schedule(back, end=fwd)
+        schedule(fwd, nxt, prv, bwd)
+        back = [CFG["mix"] * b + (1 - CFG["mix"]) * o for b, o in zip(bwd, back)]
+        s2 = schedule(back)
+        l2 = length(s2)
+        if sum(l2) < sum(span):
+            seq, span, prio = s2, l2, np.array(back)
+    for _ in range(CFG["passes"]):
+        trial = prio + rng.normal(0.0, CFG["shift"], n) * (rng.rand(n) < CFG["share"])
+        s2 = schedule(trial.tolist())
+        l2 = length(s2)
+        if sum(l2) < sum(span):
+            seq, span, prio = s2, l2, trial
+    CFG["span"], CFG["path"] = span, max(rank_)
+    return seq

@@ -6,21 +6,21 @@ PAD = 128
 MIR = 64
 BF, F32, I32, U16, F16 = "bfloat16", "float32", "int32", "uint16", "float16"
 _SB = {
-    "x": (W, BF), "oci": (L, I32), "tab": (L + MIR + 32, F32), "win": (PAD + W + 16, F32),
+    "x": (W, BF), "oci": (L, I32), "tab": (L + MIR + 32, F32), "win": (PAD + W + 32, F32),
     "vm": (4128, BF), "mg": (4128, BF), "yr0": (4096, BF), "yr1": (4096, BF), "yrh": (4096, BF),
     "vmr": (1040, BF), "mgr": (1040, BF), "yrr": (1024, BF),
     "c0": (256, U16), "c1": (256, U16), "cr": (64, U16),
-    "pi": (2, I32), "pj": (2, I32), "cols": (40, F32), "wti": (1, I32), "thi": (1, I32), "thf": (1, F32), "thc": (1, F32),
-    "colf": (256, F32), "rr": (256, BF), "hi4": (256, BF), "lo64": (256, BF), "hi16": (128, F32), "comb": (256, BF),
-    "mkb": (W, BF), "m8": (128, BF), "m8a": (128, BF), "ymb": (PAD + 2064, BF), "ones": (16, BF),
-    "biasb": (12, F32), "rslot": (4, F32),
-    "z1": (144, BF), "zf": (144, BF), "zm": (144, BF), "zw": (144, BF), "zl": (144, BF), "zv": (144, BF),
+    "pi": (2, I32), "pj": (2, I32), "cols": (48, F32), "wti": (1, I32), "thi": (1, I32), "thf": (1, F16), "thc": (1, F32),
+    "colf": (256, F32), "rr": (256, BF), "hi4": (64, BF), "lo64": (64, BF), "hi16": (128, F32),
+    "mkb": (W, BF), "m8": (128, BF), "m8a": (128, BF), "ymb": (PAD + 2080, BF), "ymh": (W - 2048, BF), "ones": (32, BF),
+    "rslot": (4, F32),
+    "z1": (144, BF), "zf": (144, BF), "zm": (144, BF), "zw": (144, BF), "zl": (144, BF), "zn": (144, BF), "zp": (144, BF), "raw": (2048, BF),
     "bo": (128, BF), "bd": (128, BF), "bw": (128, BF), "bn": (128, BF), "bt": (128, BF),
-    "tri": (128, BF), "idn": (128, BF), "idp": (128, BF), "e0": (128, BF), "g8": (128, F32), "idg": (128, F32),
+    "tri": (128, BF), "idn": (128, BF), "idp": (128, BF), "e0": (128, BF), "g8": (128, F16), "idg": (128, F32),
     "c17": (128, BF), "cq": (128, BF), "c256": (256, BF), "kseg": (256, BF), "rb": (256, BF), "rw": (256, BF),
     "dm": (384, BF), "nsel": (2048, F16), "dg": (64, BF), "sp16": (16, F16),
     "lp": (16, U16), "qp": (16, F32), "y0p": (256, BF), "lf": (16, U16), "ct": (16, BF), "oh": (16, F32),
-    "dli": (64, I32), "dlc": (64, F32), "dl8": (L, F32),
+    "dli": (64, I32), "dlc": (64, F16), "dl8": (L, F16),
     "base": (64, I32), "ui": (64, I32), "uu": (64, I32), "sq": (64, I32), "t32": (64, I32), "zz": (64, I32), "li": (64, I32),
     "l0": (16, U16), "l1": (32, U16), "lv": (4, U16), "ai": (1, I32), "ac": (4, F32), "us": (64, F32),
     "rs": (256, F32), "ji": (16, I32), "ja": (16, I32), "jm": (16, I32), "j16": (16, U16), "jr": (4, U16),
@@ -29,8 +29,8 @@ _SB = {
     "y0f": (256, BF), "y1n": (256, BF), "y1p": (256, BF), "y1r": (256, BF), "y2n": (256, BF), "lvn": (256, BF), "inv": (4, BF),
     "ad": (256, BF), "adf": (256, F32), "nn": (256, F32), "t1": (256, F32), "t2": (256, F32),
     "adr": (64, BF), "adfr": (64, F32),
-    "prop": (256, F32), "eqa": (256, BF), "cna": (256, F32), "ndg": (512, BF), "rup": (256, BF), "offa": (32, U16),
-    "lw": (16, F16), "eqn": (384, BF), "offn": (32, U16),
+    "prop": (512, F32), "eqa": (512, BF), "cna": (512, F32), "nd2": (512, BF), "ru2": (512, BF), "r32": (256, BF), "ndg": (256, BF), "lvw": (16, BF), "id16": (128, BF), "rup": (256, BF), "offa": (32, U16),
+    "lw": (16, F16), "eqn": (384, BF), "eqm": (384, BF), "cz": (256, F32), "offn": (32, U16),
     "yab": (2048, F32),
     "rdy": (16, BF), "pre": (16, BF), "rp": (16, BF), "slot": (16, U16),
     "snd0": (528, BF), "snd1": (528, BF), "snd2": (528, BF), "snd3": (528, BF),
@@ -42,6 +42,8 @@ for _k, (_n, _d) in _SB.items():
     _b = "pool_" + _d if _n <= 144 else _k
     _AT[_k] = (_b, _END.get(_b, (0, _d))[0])
     _END[_b] = (_AT[_k][1] + -(-_n // 16) * 16, _d)
+for _k in ("mk8", "mk9"):
+    _SB[_k], _AT[_k] = _SB["mkb"], _AT["mkb"]
 SCRATCH = {k: ("sbuf", [128, v[0]], v[1]) for k, v in _END.items()}
 SCRATCH.update({k: ("psum", [128, 512], F32) for k in _PS})
 NDMA = 20
@@ -51,12 +53,18 @@ SILU_ONE = 1.2784645427610738
 NENG = 8
 U18 = 2.0 ** -18
 CFG = dict(
-    f0=(2, 2, 2, 2, 4, 2, 1, 1), m0=(2, 2, 3, 1, 1, 1, 2, 1, 1, -2), m00=(2, 1, 1, 2, 2, 2, 2, 1, 2, 1),
-    f1=(2, 5, 1, 5, 2, 1), m1=(2, 3, 1, 2, 3, -1, 3, 1), rch=(8, 4, 4),
-    yh=("GGGGGGGGVVVVVVVV", "GGGGGGSSVVVVVVVV"), yrr="SSSSSSSSSSSSVVVV", y00=("VVVVVVVVVVVVVVVV", "GGGGGGVVVVVVSSSS"),
-    pair=True, uscan=True, look=0.5, turns=4, mix=0.6, passes=150, seed=1, shift=300.0, share=0.05,
-    models=((1.0, 1.56, 3.8, 0.0, 0.5, 90.0, 2000.0, 2800.0), (0.92, 1.56, 3.8, 0.0, 0.46, 190.0, 2000.0, 2800.0),
-            (0.95, 1.56, 3.8, 2.0, 0.5, 130.0, 2000.0, 2800.0)),
+    f0=(2, 2, 3, 1, 4, 4, 4, 8, 2, 2), f00=(4, 4, 4, 4, 7, 5, 2, 2), m0=(12, 4, 8, 2, -6), m00=(4, 2, 2, 4, 4, 4, 4, 2, 6),
+    f1=(1, 3, 8, 1, 1, 2, 7, 7, 2), m1=(12, 4, 8, 2, 2, 2, -2), rch=(8, 6, 2),
+    bias={"V:c<cz": 2300, "P:pu<zw": 2000, "V:l<li": 2000, "V:rs<kseg": 2000, "V:lw<li": 3000, "P:pz<idn": -2000,
+          "P:pk<cq": -300, "S:vm<pb": 300, "S:cz<tab": -300, "S:yrr<land": 800, "V:vm<x": -800},
+    wait={"S:yab<pz": 1.2, "V:vmr<x": 0.5, "S:nn<tab": 0.5},
+    yh=("GGGGGGGGVVVVVVVV", "GGGGGGGGGGSVVVVV"), yrr="SSSSSSSSVVVVVVVV", y00=("VVVVVVVVVVVVVVVV", "GGGGGGVVVVVVSSSS"),
+    two="2222", sr=(1, 1, 2, 2), we="SSSSSV", ce="SSVVVSSS", early=0.0, cs="SSSVSS", pair=True, uscan=True, look=0.35,
+    order={"G": ("pi hi4 lo64 rr qp hi16 yr*6 lvn r32 bt tri nsel*16 yrh*16 yr*11 send yr*5", "yr-*9 y0f lvn yr-*7 yrh*16 send"),
+           "S": ("oci x", "")},
+    pg=16, settle=(), tries=0, model=2, far=400.0, warm=200.0, moves=0, heat=0.0, turns=2, mix=0.05, passes=800, seed=1, shift=300.0, share=0.03,
+    models=((0.9, 1.56, 3.8, 0.0, 0.42, 215.0, 2000.0, 2800.0, 0.0), (0.85, 1.35, 3.2, 0.0, 0.45, 190.0, 2000.0, 3500.0, 30.0),
+            (1.05, 1.7, 4.2, 0.0, 0.5, 230.0, 2000.0, 3200.0, 0.0), (1.0, 1.56, 3.8, 0.0, 0.47, 150.0, 2000.0, 3000.0, 20.0)),
 )
 
 
@@ -108,7 +116,7 @@ def rank_program(g, core, T, topo):
                 rd += s[1]
                 if len(s) == 3:
                     rd += s[2]
-        ops.append([q, fn, rd, wr, kind, cost, lat])
+        ops.append([q, fn, rd, wr, kind, ("a", cost[1]) if q == "S" and cost[0] == "c" else cost, lat])
 
     def ts(o, i, s1, s2, o0, o1=None):
         c = span(o, i, 0.5 if narrow(o, i) else 1)
@@ -124,8 +132,8 @@ def rank_program(g, core, T, topo):
     def cp(o, i):
         rec("V", lambda: g.vector.tensor_copy(o[0], i[0]), [o], [i], span(o, i, 0.5 if narrow(o, i) else 1))
 
-    def scan(o, d0, d1, o0, o1):
-        rec("V", lambda: g.vector.tensor_tensor_scan(o[0], d0[0], d1[0], 0.0, o0, o1), [o], [d0, d1],
+    def scan(o, d0, d1, o0, o1, first=0.0):
+        rec("V", lambda: g.vector.tensor_tensor_scan(o[0], d0[0], d1[0], first, o0, o1), [o], [d0, d1],
             span(o, d0, 0.5 if narrow(o, d0, d1) else 1))
 
     def fill(o, c):
@@ -136,6 +144,12 @@ def rank_program(g, core, T, topo):
             rec("S", lambda: g.scalar.activation(o[0], i[0], f), [o], [i], span(o, i, 1))
         else:
             rec("S", lambda: g.scalar.activation(o[0], i[0], f, bias=val(bias), scale=val(scale)), [o], [i, bias, scale], span(o, i, 1))
+
+    def aff(o, i, m, b=0.0, eng=None):
+        if (eng or CFG["ce"][6]) == "S":
+            act(o, i, AF.Identity, b, m)
+        else:
+            ts(o, i, m, b, A_.mult, A_.add)
 
     def mm(o, l, r, start=False):
         c = max(64, num(r)) * (4 if _SB[l[1][0][0]][1] == F32 else 1)
@@ -167,101 +181,99 @@ def rank_program(g, core, T, topo):
     top = W - 256
 
     dma("Y", a("x", top, W), ext(T.xc[:, top:W]), 64)
-    dma("S", a("oci"), ext(T.oc[:]), 512)
+    dma("S", a("oci"), ext(T.oc[:]), 400)
     dma("Y", a("wti"), ext(T.wt[:]), 1)
     dma("Y", a("mkb", p=p8), ext(T.mk[:]), 48)
-    dma("Y", a("x", 0, 1408), ext(T.xc[:, 0:1408]), 400)
-    dma("S", a("x", 1408, top), ext(T.xc[:, 1408:top]), 400)
+    dma("S", a("x", 0, top), ext(T.xc[:, 0:top]), 750)
     dma("Y", a("dli"), ext(T.dl[:]), 32)
     dma("Y", a("thi", p=p8), ext(T.th[:]), 1)
 
     iota(a("pi"), [[2, 2]], 0, 1, False)
-    iota(a("colf"), [[1, 256]])
-    iota(a("hi4"), [[1, 4], [0, 64]], 128)
-    iota(a("lo64"), [[0, 4], [1, 64]], 128)
+    p48 = slice(0, W // 64)
+    for row, tile, step in ((8, "hi4", 0), (9, "lo64", 1)):
+        iota(a(tile, p=p48), [[step, 64]], 0, 1 - step)
+        dma("Y", a("mk%d" % row, p=slice(row, row + 1)), a(tile, p=p48), 6)
+    fill(a("c256"), 1.0)
+    scan(a("colf"), a("c256"), a("c256"), A_.mult, A_.add, -1.0)
     iota(a("rr"), [[0, 16], [1, 16]])
     iota(a("hi16"), [[16, 8], [0, 16]])
     iota(a("qp"), [[8, 2], [32, 8]])
-    (P_, R_, K2, G_, G15, IS0, IS1, IS2, IS3, IS4, DIG, WN, R16, R255, DM, DN0, DN1, MW, LW, VW, SC, BI, P16, P3, R8, DY,
-     J0, J1, JR, TA, TB, DEAD) = range(32)
+    (P_, R_, K2, G_, G15, IS0, IS1, IS2, IS3, IS4, DIG, WN, R16, R255, DM, DM1, DN0, DN1, MW, LW, SC, BI, P16, P3, R8, DY, DY1,
+     J0, J1, JR, DEAD, T0, T1, T2, T3, T4, T5, T6, T7, T8, T9) = range(41)
     ts(a("pj"), a("pi"), 15, None, A_.bitwise_and)
     cp(col(P_), a("pi", 0, 1))
     cp(a("cols", R_, R_ + 2), a("pj"))
     ts(a("cols", IS0, IS0 + 5), a("colf", 0, 5), col(R_), None, A_.is_equal)
     for j, m, v in ((R16, 16.0, 0.0), (R255, -1.0, 255.0), (DM, 1.0, PAD + W), (DN0, 1.0, L + MIR), (DN1, 1.0, L + MIR + 16),
-                    (DY, 1.0, PAD + 2048), (J0, 128.0, -240 - (1 << 21)), (JR, 64.0, -240 - (1 << 21))):
-        ts(col(j), col(R_), m, float(v), A_.mult, A_.add)
+                    (DY, 1.0, PAD + 2048), (DY1, 1.0, PAD + 2064), (DM1, 1.0, PAD + W + 16), (J0, 128.0, -240 - (1 << 21)), (JR, 64.0, -240 - (1 << 21))):
+        aff(col(j), col(R_), m, float(v), CFG["ce"][5])
     ts(col(G15), col(P_), col(R_), 15.0, A_.subtract, A_.add)
     ts(col(G_), col(P_), col(R_), None, A_.subtract)
-    ts(col(P16), col(P_), 16.0, None, A_.mult)
-    ts(col(P3), col(P_), 16.0, 3.0, A_.mult, A_.add)
     ts(col(WN), a("wti"), -1.0, None, A_.mult)
-    ts(col(LW), col(IS0), -16.0, None, A_.mult)
-    ts(col(VW), col(IS0), -4096.0, None, A_.mult)
-    ts(col(MW), col(IS3), -U18, col(IS0), A_.mult, A_.add)
-    ts(col(TA), col(IS0), col(IS3), None, A_.add)
-    ts(col(BI), col(TA), SILU_ONE, None, A_.mult)
-    ts(col(SC), col(TA), -1.0, 1.0, A_.mult, A_.add)
-    ts(col(TA), col(IS1), 64.0, col(IS2), A_.mult, A_.add)
-    ts(col(TB), col(IS4), -64.0, col(TA), A_.mult, A_.add)
-    ts(col(DIG), col(TB), 1.0 / 4096, None, A_.mult)
     ts(col(R8), col(R_), 8.0, 8.0, A_.is_ge, A_.mult)
-    ts(col(TA), col(R8), 2.0, -240.0 - (1 << 21), A_.mult, A_.add)
-    ts(col(J1), col(R_), 256.0, col(TA), A_.mult, A_.add)
-    ts(col(TA), col(IS1), col(IS4), 128.0, A_.add, A_.mult)
-    ts(col(DEAD), col(IS2), 127.0, col(TA), A_.mult, A_.add)
-    ts(col(TB), col(IS4), 128.0, None, A_.mult)
-    ts(a("hi4"), a("hi4"), col(IS1), col(TB), A_.mult, A_.add)
-    ts(a("lo64"), a("lo64"), col(IS2), None, A_.mult)
-    ts(a("biasb"), a("colf", 0, 12), col(IS1), 4.0, A_.mult, A_.mult)
-    ts(a("m8a"), a("colf", 0, 128), col(P16), None, A_.is_equal)
-    ts(a("m8"), a("colf", 0, 128), col(P3), None, A_.is_equal)
+    for j, i, m, v in ((P16, P_, 16.0, 0.0), (P3, P_, 16.0, 1.5), (LW, IS0, -16.0, 0.0),
+                       (MW, IS3, -U18, col(IS0)), (T0, IS0, 1.0, col(IS3)), (BI, T0, SILU_ONE, 0.0), (SC, T0, -1.0, 1.0),
+                       (T1, IS1, 64.0, col(IS2)), (T2, IS4, -64.0, col(T1)), (DIG, T2, 1.0 / 4096, 0.0),
+                       (T3, R8, 2.0, -240.0 - (1 << 21)), (J1, R_, 256.0, col(T3)), (T4, IS4, 128.0, 0.0),
+                       (T5, IS1, 128.0, col(T4)), (DEAD, IS2, 127.0, col(T5)), (T6, R_, -4.0, 64.0), (T7, IS0, 32.0, 0.0),
+                       (T9, IS2, 128.0, col(T5))):
+        aff(col(j), col(i), m, v, CFG["ce"][7])
+    act(a("m8a"), a("colf", 0, 128), AF.Abs, col(P3), -1.0)
+    ts(a("m8"), a("m8a"), 1.5, None, A_.is_equal)
+    ts(col(T8), col(P_), 8.0, 64.0, A_.is_lt, A_.mult)
+    ts(a("m8a"), a("rr", 0, 128), col(T8), 7.0, A_.add, A_.add)
+    ts(a("m8a"), a("m8a"), col(P_), None, A_.is_equal)
     tt(a("m8"), a("m8"), a("m8a"), A_.add)
     ts(a("idp"), a("colf", 0, 128), col(P_), None, A_.is_equal)
-    tt(a("comb"), a("hi4"), a("lo64"), A_.add)
-    for b in range(11, -1, -1):
-        o = a(("pa", "pb", "pz", "psm", "pk", "pr")[b % 6], 0, 256)
-        mm(o, a("idp"), a("comb"), True)
-        mm(o, a("m8", p=p8), a("mkb", 256 * b, 256 * b + 256, p=p8))
-        act(a("win", PAD + 256 * b, PAD + 256 * b + 256), o, AF.Identity, a("biasb", b, b + 1))
+    p10 = slice(0, 10)
+    for b, eng in zip(range(5, -1, -1), CFG["we"]):
+        o = a(("pa", "pb", "pz", "psm", "pk", "pr")[b], 0, 512)
+        rows = a("mkb", 512 * b, 512 * b + 512, p=p10)
+        mm(o, a("m8", p=p10), (rows[0], rows[1] + a("mk8")[1] + a("mk9")[1]), True)
+        aff(a("win", PAD + 512 * b, PAD + 512 * b + 512), o, 1.0, col(T9), eng)
     ts(a("zw"), a("colf", 0, 144), col(G15), col(WN), A_.is_equal, A_.mult)
     ts(a("z1"), a("colf", 0, 144), col(G15), None, A_.is_equal)
-    for fam, w in (("zf", 1.0 / 256), ("zm", col(MW)), ("zl", col(LW)), ("zv", col(VW))):
-        ts(a(fam), a("z1"), w, None, A_.mult)
+    for fam, w in (("zf", 1.0 / 256), ("zm", col(MW)), ("zl", col(LW))):
+        aff(a(fam), a("z1"), w, eng=CFG["ce"][0])
+    if CFG["sr"]:
+        aff(a("zn"), a("zf"), -1.0)
+        aff(a("zp"), a("zw"), -1.0)
     ts(a("bo"), a("hi16"), col(G_), None, A_.is_equal)
     for fam, w in (("bd", col(DIG)), ("bw", col(WN)), ("bn", -1.0)):
-        ts(a(fam), a("bo"), w, None, A_.mult)
+        aff(a(fam), a("bo"), w, eng=CFG["ce"][1])
     fill(a("c17"), 2 * U18)
     fill(a("cq"), -0.25)
-    act(a("c256"), a("colf"), AF.Identity, 256.0, -1.0)
+    aff(a("c256"), a("colf"), -1.0, 256.0)
     ts(a("kseg"), a("rr"), 0.0, None, A_.not_equal)
-    ts(a("rb"), a("kseg"), 64.0, -64.0, A_.mult, A_.add)
-    ts(a("rw"), a("rb"), -1.0, -4 * U18, A_.mult, A_.add)
+    aff(a("rb"), a("kseg"), 64.0, -64.0, CFG["ce"][2])
+    aff(a("rw"), a("rb"), -1.0, -4 * U18, CFG["ce"][3])
+    aff(a("rup"), a("rb"), -1.0, 0.0, CFG["ce"][3])
     ts(a("dm", 0, 256), a("rr"), col(R_), 2048.0, A_.is_ge, A_.mult)
     fill(a("dm", 256, 384), 0.0)
-    ts(a("ndg", 0, 256), a("rr"), col(R_), None, A_.not_equal)
-    fill(a("ndg", 256, 512), 0.0)
-    ts(a("rup"), a("rb"), -1.0, None, A_.mult)
-    ts(a("dg"), a("rr", 0, 64), col(R_), 1048576.0, A_.is_equal, A_.mult)
+    ts(a("ndg"), a("rr"), col(R_), None, A_.not_equal)
+    iota(a("r32"), [[0, 8], [1, 32]])
+    for k in range(2):
+        ts(a("nd2", 256 * k, 256 * k + 256), a("r32"), -16.0 * k, col(R_), A_.add, A_.not_equal)
+        ts(a("ru2", 256 * k, 256 * k + 256), a("r32"), 0.0, 64.0, A_.is_equal, A_.mult)
+    aff(a("dg"), a("ndg", 0, 64), -1048576.0, 1048576.0)
     ts(a("lf"), a("colf", 0, 16), col(R16), None, A_.add)
     ts(a("lp"), a("qp"), col(R8), col(R_), A_.add, A_.add)
-    ts(a("ct"), a("colf", 0, 16), -16.0, col(R255), A_.mult, A_.add)
+    aff(a("ct"), a("colf", 0, 16), -16.0, col(R255))
     ts(a("oh"), a("colf", 0, 16), col(K2), None, A_.is_equal)
-    ts(col(TA), col(R_), -4.0, 64.0, A_.mult, A_.add)
-    ts(a("rslot"), a("colf", 0, 4), -1.0, col(TA), A_.mult, A_.add)
+    aff(a("rslot"), a("colf", 0, 4), -1.0, col(T6))
     for e, c in enumerate((DN0, DN1 if CFG["pair"] else DN0)):
         ts(a("sp16", e, 16, 2), a("colf", 0, 8), 0.0, col(c), A_.mult, A_.add)
-    act(a("idg"), a("idp"), AF.Identity, 0.0, -1.0)
-    ts(a("idn"), a("idp"), -1.0, None, A_.mult)
-    ts(col(TA), col(IS0), 32.0, None, A_.mult)
-    ts(a("e0"), a("idp"), 0.0, col(TA), A_.mult, A_.add)
+    aff(a("idg"), a("idp"), -1.0)
+    aff(a("idn"), a("idp"), -1.0, eng=CFG["ce"][4])
+    aff(a("id16"), a("idp"), -256.0, eng=CFG["ce"][4])
+    aff(a("e0"), a("idp"), 0.0, col(T7), CFG["ce"][4])
     ts(a("g8"), a("hi16"), col(P16), None, A_.is_equal)
     fill(a("ones"), 1.0)
     fill(a("tab", L, L + MIR + 32), 0.0)
     for b in (0, 2064):
         fill(a("vm", b, b + 16), 0.0)
     for o in (a("mg", 0, 16), a("mg", 2064, 2080), a("mgr", 0, 16)):
-        ts(o, a("rr", 0, 16), 0.0, col(DEAD), A_.mult, A_.add)
+        aff(o, a("rr", 0, 16), 0.0, col(DEAD))
     for t in range(NS):
         fill(a("snd%d" % t, 0, 80), 0.0)
     asel(a("bt"), a("bn"), [[-1, 128]], A_.is_ge, 0.0, 0, 1)
@@ -270,8 +282,9 @@ def rank_program(g, core, T, topo):
     cp(a("bnh"), a("bn"))
     for r in range(16):
         asel(a("nsel", 128 * r, 128 * r + 128), a("bnh"), [[-16, 8], [0, 16]], A_.is_equal, 0.0, -r, 1)
-    cp(a("tab", 0, L), a("oci"))
-    cp(a("dlc"), a("dli"))
+    for b in range(0, L, 128):
+        cp(a("tab", b, b + 128), a("oci", b, b + 128))
+    ts(a("dlc"), a("dli"), -2048.0, None, A_.add)
     dma("Y", a("dl8", p=p8), a("dlc"), 32)
     cp(a("thf", p=p8), a("thi", p=p8))
     mm(a("prk", 48, 49), a("g8", p=p8), a("thf", p=p8), True)
@@ -311,8 +324,13 @@ def rank_program(g, core, T, topo):
     def ycols(t):
         return a("x", W - 256 * (t + 1), W - 256 * t)
 
-    def names(dst, tab, lst, t):
-        ts(dst, ind(tab, lst), (11 - t) / 16.0, -15.0 / 32, A_.mult, A_.add)
+    def names(dst, tab, lst, t, eng="V"):
+        if eng == "V":
+            ts(dst, ind(tab, lst), (11 - t) / 16.0, -15.0 / 32, A_.mult, A_.add)
+        else:
+            f = dst[1][0]
+            aff(a("cz", f[1], f[2]), ind(tab, lst), (11 - t) / 16.0, -15.0 / 32, "S")
+            cp(dst, a("cz", f[1], f[2]))
 
     def at16(j):
         return 16 + j + 16 * (j >= 2048)
@@ -324,32 +342,63 @@ def rank_program(g, core, T, topo):
 
     marks = a("win", PAD, PAD + W)
 
-    def main(c, yr, hop, fch, mch):
+    def main(c, yr, hop, fch, mch, sch=()):
         u = 0
+        for n, w in enumerate(sch):
+            raw, bank = a("raw", 128 * u, 128 * (u + w)), a(("pz", "pb", "prk")[n % 3], 0, 128 * w)
+            act(raw, ind(a("x"), a(c, 8 * u, 8 * (u + w))))
+            mm(bank, a("idp"), a(yr, 128 * u, 128 * (u + w)), True)
+            mm(bank, a("idn"), raw)
+            act(a("vm", 16 + 128 * u, 16 + 128 * (u + w)), bank, AF.Relu)
+            u += w
+        skip = u
         for w in fch:
-            o = at16(256 * u)
-            tt(a("vm", o, o + 256 * w), ind(a("x"), a(c, 16 * u, 16 * (u + w))), a(yr, 256 * u, 256 * (u + w)), A_.min)
+            if skip >= w:
+                skip -= w
+                continue
+            w, skip = w - skip, 0
+            o = at16(128 * u)
+            tt(a("vm", o, o + 128 * w), ind(a("x"), a(c, 8 * u, 8 * (u + w))), a(yr, 128 * u, 128 * (u + w)), A_.min)
             u += w
         u = 0
         for w in mch:
-            o = at16(256 * u)
-            o, i = a("mg", o, o + 256 * abs(w)), ind(marks, a(c, 16 * u, 16 * (u + abs(w))))
+            o = at16(128 * u)
+            o, i = a("mg", o, o + 128 * abs(w)), ind(marks, a(c, 8 * u, 8 * (u + abs(w))))
             act(o, i) if w > 0 else cp(o, i)
             u += abs(w)
         for h, bank in enumerate(("pk",) if hop else ("pr", "pk")):
             n = 256 if hop else 128
             opened(bank, n)
+            if hop:
+                mm(a(bank, 0, n, 16), a("idn"), a("lvw"))
             for u in range(16):
-                mm(a(bank, 0, n, 16), sel("zl", u), a("lvn", u, 256, 16) if hop else a("lvn", 16 * u + 8 * h, 16 * u + 8 * h + 8))
+                if not hop:
+                    mm(a(bank, 0, n, 16), sel("zl", u), a("lvn", 16 * u + 8 * h, 16 * u + 8 * h + 8))
                 for buf, fam in (("vm", "zf"), ("mg", "zm")):
                     o = at16(2048 * h + n * u)
+                    if buf == "vm" and 16 * h + u < sum(sch):
+                        mm(a(bank, 0, n), sel(fam, u), a(yr, n * u, n * u + n))
+                        fam = "zn"
                     mm(a(bank, 0, n), sel(fam, u), a(buf, o, o + n))
 
-    def distinct(bank, dig, n, dummy, at=0):
+    def distinct(bank, dig, n, dummy, at=0, wide=None):
         q, e = n // 16, at // 16
-        mm(a(bank, 0, 256 + n), a("idp"), a("ndg", 0, 256 + n), True)
+        if wide:
+            flat = (wide, 0) if n == 256 else (bank, 256)
+            mm(a(bank, 0, 2 * n), a("idp"), a("nd2", 256 - n, 256 + n), True)
+            for k in range(2):
+                mm(a(bank, k * n, k * n + n), a("bd"), a(dig, at, at + n))
+            for k in range(2):
+                mm(a(flat[0], flat[1] + k * n, flat[1] + k * n + n), a("bd"), a(dig, at, at + n), True)
+            scan(a("prop", 0, 2 * n), a("ru2", 0, 2 * n), a(bank, 0, 2 * n), A_.add, A_.min)
+            tt(a("eqa", 0, 2 * n), a("prop", 0, 2 * n), a(flat[0], flat[1], flat[1] + 2 * n), A_.is_equal)
+            scan(a("cna", 0, 2 * n), a("eqa", 0, 2 * n), a(bank, 0, 2 * n), A_.add, A_.min)
+            for k in range(2):
+                ts(a("offa", 2 * e + k, 2 * e + q, 2), a("cna", k * n + 31, k * n + n, 32), 4096.0, col(dummy + k), A_.mult, A_.min)
+            return
+        mm(a(bank, 0, n), a("idp"), a("ndg", 0, n), True)
         mm(a(bank, 0, n), a("bd"), a(dig, at, at + n))
-        mm(a(bank, 256, 256 + n), a("bd"), a(dig, at, at + n))
+        mm(a(bank, 256, 256 + n), a("bd"), a(dig, at, at + n), True)
         scan(a("prop", 0, n), a("rup", 0, n), a(bank, 0, n), A_.add, A_.min)
         tt(a("eqa", 0, n), a("prop", 0, n), a(bank, 256, 256 + n), A_.is_equal)
         scan(a("cna", 0, n), a("eqa", 0, n), a(bank, 0, n), A_.add, A_.min)
@@ -371,12 +420,14 @@ def rank_program(g, core, T, topo):
         ts(a("li", b, n), a("zz", b, n), 5, 1023, A_.arith_shift_right, A_.bitwise_and)
         cp(a(dst, b, n), a("li", b, n))
 
-    def mark(src, lst, bank, n, at=0, names_=("ad", "adf")):
+    def mark(src, lst, bank, n, at=0, names_=("ad", "adf"), wide=None):
         ad, adf = names_
         act(a(ad, at, at + n), ind(src, lst))
         act(a(adf, at, at + n), a(ad, at, at + n), AF.Identity, col(BI), col(SC))
-        distinct(bank, ad, n, DM, at)
-        for q in range(at // 16, (at + n) // 16):
+        distinct(bank, ad, n, DM, at, wide)
+        for q in range(n // 32 if wide else 0):
+            act(ind(a("win"), a("offa", at // 8 + 2 * q, at // 8 + 2 * q + 2)), a(adf, at + 32 * q, at + 32 * q + 32), AF.Silu)
+        for q in range(at // 16, at // 16 if wide else (at + n) // 16):
             act(ind(a("win"), a("offa", 2 * q, 2 * q + 1)), a(adf, 16 * q, 16 * q + 16), AF.Silu)
 
     def ya_out(t, h):
@@ -387,8 +438,7 @@ def rank_program(g, core, T, topo):
         act(a("yab", 256 * (2 * t + h), 256 * (2 * t + h + 1)), a("pz", 0, 256), AF.Identity, -float(PAD), 4096.0)
 
     def name_offsets():
-        for r in range(16):
-            mm(a("psm", 0, 16), sel("zv", r), a("lvn", r, 256, 16), r == 0)
+        mm(a("psm", 0, 16), a("id16"), a("lvw"), True)
         mm(a("psm", 0, 16), a("idh"), a("sp16"))
         tt(a("lw"), a("li", 16, 32), a("psm", 0, 16), A_.max)
         n = 384 if CFG["pair"] else 256
@@ -400,7 +450,11 @@ def rank_program(g, core, T, topo):
             if CFG["pair"]:
                 mm(a("pb", 256 + r, 384, 16), a("idh"), a("lw", 1, 16, 2))
                 mm(a("pb", 256 + r, 384, 16), ns, a("lw", 0, 16, 2))
-        ts(a("eqn", 0, n), a("pb", 0, n), 0.0, 2048.0, A_.is_equal, A_.mult)
+        if CFG["cs"][4] == "V":
+            ts(a("eqn", 0, n), a("pb", 0, n), 0.0, 2048.0, A_.is_equal, A_.mult)
+        else:
+            act(a("eqm", 0, n), a("pb", 0, n), AF.Abs)
+            act(a("eqn", 0, n), a("eqm", 0, n), AF.Relu, 2048.0, -2048.0)
         mm(a("psm", 0, 16), a("idh"), a("lw"), True)
         for r in range(16):
             mm(a("psm", 0, 16), a("idp"), a("eqn", r, 256, 16))
@@ -423,49 +477,60 @@ def rank_program(g, core, T, topo):
 
     first_y(1)
     fill(a("win", 0, PAD), 0.0)
-    fill(a("win", PAD + W, PAD + W + 16), 0.0)
-    fill(a("ymb", PAD + 2048, PAD + 2064), 0.0)
+    fill(a("win", PAD + W, PAD + W + 32), 0.0)
+    fill(a("ymb", PAD + 2048, PAD + 2080), 0.0)
     fill(a("ymb", 0, PAD), 0.0)
 
     for t in range(NS):
         B = W - 256 * (t + 1)
         table = a("tab", 0, L)
         for h in range(2):
-            names(a("c0", 128 * h, 128 * h + 128), a("tab", 0, L + MIR) if t else a("oci"), a("l0", 8 * h, 8 * h + 8), t)
+            names(a("c0", 128 * h, 128 * h + 128), a("tab", 0, L + MIR) if t else a("oci"), a("l0", 8 * h, 8 * h + 8), t,
+                  CFG["cs"][h] if t else "V")
         asel(a("lvn"), a("win", PAD + B, PAD + B + 256), [[0, 256]], A_.is_ge, 0.0, 0, 0)
+        for r in range(16):
+            mm(a("psm", 0, 16), sel("zl", r), a("lvn", r, 256, 16), r == 0)
+        act(a("lvw"), a("psm", 0, 16), AF.Identity, 0.0, -1.0)
         act(a("y0f"), ind(ycols(t), a("lf")))
-        main("c0", yrbuf[t % 2], 0, CFG["f0"], CFG["m0"] if t else CFG["m00"])
+        sch = CFG["sr"] if t else ()
+        if sch:
+            asel(a("y0f", 0, 128), a("y0f", 0, 128), [[0, 8], [1, 16]], A_.is_ge, 0.0, -sum(sch), 0)
+        main("c0", yrbuf[t % 2], 0, CFG["f0" if t else "f00"], CFG["m0" if t else "m00"], sch)
+        y1 = lambda h: ("y1p", "zp", "zn") if sch and not h else ("y1n", "zw", "zf")
         if t + 2 < NS:
             first_y(t + 2)
         for h, bank in enumerate(("pr", "pk")):
             j, b = a("j16", 8 * h, 8 * h + 8), 128 * h
             best(bank, 128, j, J0)
             tt(a("y1n", b, b + 128), ind(a("vm", 2064 * h, 2064 * h + 2064), j), a("y0f", b, b + 128), A_.subtract)
-            if "G" in CFG["yh"][h]:
-                act(a("y1p", b, b + 128), a("y1n", b, b + 128), AF.Identity, 0.0, -1.0)
-            yrep("yrh", CFG["yh"][h], a("y1n", b, b + 128), True, 128, b, a("y1p", b, b + 128))
-            mark(a("mg", 2064 * h, 2064 * h + 2064), j, ("pa", "pb")[h], 128, b)
+            if "G" in CFG["yh"][h] or sch:
+                act(a("y1p", b, b + 128), a("y1n", b, b + 128), AF.Abs)
+            yrep("yrh", CFG["yh"][h], a(y1(h)[0], b, b + 128), y1(h)[0] == "y1n", 128, b, a("y1p", b, b + 128))
+            mark(a("mg", 2064 * h, 2064 * h + 2064), j, ("pa", "pb")[h], 128, b, wide=CFG["two"][h] == "2")
             for r in range(16):
-                mm(a("pu", 8 * h, 8 * h + 8), sel("zw", r), a("y1n", b + r, b + 128, 16), r == 0)
+                mm(a("pu", 8 * h, 8 * h + 8), sel(y1(h)[1], r), a(y1(h)[0], b + r, b + 128, 16), r == 0)
             if h:
                 for r in range(16):
-                    mm(a("pu", 16, 32), sel("zw", r), a("y1n", 16 * r, 16 * r + 16), r == 0)
+                    mm(a("pu", 16, 32), sel(y1(r // 8)[1], r), a(y1(r // 8)[0], 16 * r, 16 * r + 16), r == 0)
             place(a("pu", 8 * h, 32 if h else 8), 8 * h, 32 if h else 8, "l1", t)
-            names(a("c1", b, b + 128), table, a("l1", 8 * h, 8 * h + 8), t)
+            names(a("c1", b, b + 128), table if t else a("oci"), a("l1", 8 * h, 8 * h + 8), t, CFG["cs"][2 + h] if t else "V")
         ya_out(t, 0)
-        act(a("y1r"), ind(a("y1n"), a("lf")), AF.Identity, 0.0, -1.0)
+        act(a("y1r"), ind(a("y1p" if sch else "y1n"), a("lf")), AF.Identity, 0.0, -1.0 if (CFG["cs"][5] == "V") != bool(sch) else 1.0)
         act(a("nn"), ind(table, a("l1", 16, 32)))
+        mm(a("pr", 0, 256), a("g8", p=p8), a("dl8", 256 * t, 256 * t + 256, p=p8), True)
         for b in range(0, 256, 64):
-            mm(a("pz", 256 + b, 320 + b), a("g8", p=p8), a("dl8", 256 * t + b, 256 * t + b + 64, p=p8), True)
-            mm(a("pz", 256 + b, 320 + b), a("idg"), a("nn", b, b + 64))
-        act(a("t2"), a("pz", 256, 512))
+            mm(a("pr", b, b + 64), a("idg"), a("nn", b, b + 64))
+        act(a("t2"), a("pr", 0, 256), AF.Identity, 2048.0)
         for r in range(16):
-            mm(a("prk", 64, 80), sel("zf", r), a("y1n", 16 * r, 16 * r + 16), r == 0)
+            mm(a("prk", 64, 80), sel(y1(r // 8)[2], r), a(y1(r // 8)[0], 16 * r, 16 * r + 16), r == 0)
         act(a("thr"), a("prk", 64, 80), AF.Identity, a("thc"))
         main("c1", "yrh", 1, CFG["f1"], CFG["m1"])
         name_offsets()
         best("pk", 256, a("j16"), J1)
-        tt(a("y2n"), ind(a("vm"), a("j16")), a("y1r"), A_.subtract)
+        if CFG["cs"][5] == "V":
+            tt(a("y2n"), ind(a("vm"), a("j16")), a("y1r"), A_.subtract)
+        else:
+            act(a("y2n"), ind(a("vm"), a("j16")))
         tt(a("dd"), a("rs", 15, 256, 16), a("thr"), A_.add)
         ts(a("jm"), a("ji"), 1, None, A_.bitwise_and)
         tt(a("rdy"), a("jm"), a("dd"), A_.is_gt)
@@ -479,19 +544,22 @@ def rank_program(g, core, T, topo):
         snd, land = "snd%d" % t, "land%d" % t
         ts(a("slot"), a("prk", 0, 16), 255.0, None, A_.add)
         act(a(snd, 0, 1), a("pu", 64, 65), AF.Relu, 64.0, -1.0)
-        cp(ind(a(snd, 16, 528), a("slot")), a("y2n"))
+        if CFG["cs"][5] == "V":
+            cp(ind(a(snd, 16, 528), a("slot")), a("y2n"))
+        else:
+            tt(ind(a(snd, 16, 528), a("slot")), a("y2n"), a("y1r"), A_.add)
         dst = T.cores[(rank + 1 + t % (nrank - 1)) % nrank]
         rid, pid = topo.addr(dst, core)
         mask = sum(1 << e for e in topo.engines(core, dst)[:NENG])
         rec("G", lambda t=t, rid=rid, pid=pid, mask=mask: g.remote_dma(
             a("land%d" % t)[0], a("snd%d" % t, 0, 80)[0], T.sem["arr%d" % t], T.sem.sent, pid, rid, mask),
             [], [a(snd, 0, 80)], ("n", 300), "r")
-        ops.append(["A", None, [], [(land, 0, 80, 1)], ("a", t, len(ops) - 1), ("n", 0), ("r", 0)])
+        sent = len(ops) - 1
         scan(a("rm"), a("rw"), a("pk", 0, 256), A_.add, A_.min)
         ts(a("ki"), a("rm", 15, 256, 16), 1 / U18, 1.0, A_.mult, A_.add)
         ts(a("ka"), a("ki"), 1, 15, A_.arith_shift_right, A_.bitwise_and)
         cp(a("k16"), a("ka"))
-        mark(a("mg"), a("j16"), "pa", 256)
+        mark(a("mg"), a("j16"), "pa", 256, wide="pb" if CFG["two"][2] == "2" else None)
         ya_out(t, 1)
         if t == NS - 1:
             dma("Y", ext(T.ya[:]), a("yab", p=g16), 64)
@@ -503,6 +571,7 @@ def rank_program(g, core, T, topo):
             dma("Y", ext(T.yo[:]), table, 512)
         else:
             act(a("tab", L, L + MIR), a("tab", 0, MIR))
+        ops.append(["A", None, [], [(land, 0, 80, 1)], ("a", t, sent), ("n", 0), ("r", 0)])
         if CFG["uscan"]:
             mm(a("pu", 0, 64), a("idp"), a("dg"), True)
             mm(a("pu", 0, 64), a("bw"), a(land, 16, 80))
@@ -536,25 +605,27 @@ def rank_program(g, core, T, topo):
             u += w
         best("pr", 64, a("jr"), JR)
         if t + 1 < NS:
-            mark(a("mgr"), a("jr"), "pa", 64, 0, ("adr", "adfr"))
+            mark(a("mgr"), a("jr"), "pa", 64, 0, ("adr", "adfr"), CFG["two"][3] == "2")
         if t == NS - 2:
-            dma("G", ext(T.ym[:, 2048:W]), a("win", PAD + 2048, PAD + W, p=g16), 16)
+            for b in range(0, W - 2048, 256):
+                act(a("ymh", b, b + 256), a("win", PAD + 2048 + b, PAD + 2304 + b))
+            dma("Y", ext(T.ym[:, 2048:W]), a("ymh", p=g16), 16)
         if t == NS - 1:
             for b in range(PAD, PAD + 2048, 256):
                 act(a("ymb", b, b + 256), a("win", b, b + 256))
             act(a("adr"), ind(a("mgr"), a("jr")))
-            distinct("pa", "adr", 64, DY)
-            for q in range(4):
-                cp(ind(a("ymb"), a("offa", 2 * q, 2 * q + 1)), a("ones"))
+            distinct("pa", "adr", 64, DY, 0, True)
+            for q in range(2):
+                cp(ind(a("ymb"), a("offa", 2 * q, 2 * q + 2)), a("ones"))
             dma("Y", ext(T.ym[:, 0:2048]), a("ymb", PAD, PAD + 2048, p=g16), 32)
 
     emit(g, T, ops, QO)
 
 
 def price(c, m):
-    cyc, gather, scatter, fused, pe, wake, dma, remote = m
+    cyc, gather, scatter, fused, pe, wake, dma, remote, extra = m
     k, n = c
-    return {"c": n * cyc, "g": 55 + n * gather * cyc, "f": 55 + n * max(gather, fused) * cyc, "s": 55 + n * scatter * cyc,
+    return {"c": n * cyc, "a": extra + n * cyc, "g": 55 + n * gather * cyc, "f": 55 + n * max(gather, fused) * cyc, "s": 55 + n * scatter * cyc,
             "p": n * pe, "n": n, "d": dma + 7 * n, "r": remote}[k]
 
 
@@ -621,7 +692,7 @@ def emit(g, T, ops, QO):
         deps.append(need)
         soft.append(order - need)
     if "seq" not in CFG:
-        CFG["seq"] = arrange(ops, deps, soft, list(QO) + ["A"])
+        CFG["seq"] = arrange(ops, deps, named(ops, soft), list(QO) + ["A"])
     seq = CFG["seq"]
     wanted = set()
     for d in deps:
@@ -663,6 +734,34 @@ def emit(g, T, ops, QO):
             g.wait_ge(T.sem[s], v)
 
 
+def tile(o):
+    return "send" if o[4] == "r" else o[3][0][0].rstrip("0123") if o[3][0][0][:2] in ("sn", "yr") else o[3][0][0]
+
+
+def named(ops, soft):
+    soft = [set(s) for s in soft]
+    calls, stage = {}, 0
+    for i, o in enumerate(ops):
+        if o[3] or o[4] == "r":
+            calls.setdefault((o[0], stage, tile(o)), []).append(i)
+        stage += o[0] == "A"
+    for q, lists in CFG["order"].items():
+        last = None
+        for stage in range(NS + 1):
+            names = []
+            for name in lists[min(stage, len(lists) - 1)].split():
+                name, times = (name + "*1").split("*")[:2]
+                names += [name] * int(times)
+            for k, name in enumerate(names):
+                mine = calls.get((q, stage - name.count("-") + name.count("+"), name.strip("-+")))
+                if mine:
+                    i = mine.pop(max(0, len(mine) - names[k:].count(name)) if "-" in name else 0)
+                    if last is not None:
+                        soft[i].add(last)
+                    last = i
+    return soft
+
+
 def arrange(ops, deps, soft, queues):
     n = len(ops)
     models = CFG["models"]
@@ -680,8 +779,16 @@ def arrange(ops, deps, soft, queues):
     for i in range(n):
         for d, w in prv[i]:
             nxt[d].append((i, w))
+    left = [len(p) for p in prv]
+    flow = [i for i in range(n) if not left[i]]
+    for i in flow:
+        for j, w in nxt[i]:
+            left[j] -= 1
+            if not left[j]:
+                flow.append(j)
+    assert len(flow) == n, [ops[i][0] + str(ops[i][3][:1]) for i in range(n) if left[i]][:12]
     rank_ = [0.0] * n
-    for i in range(n - 1, -1, -1):
+    for i in reversed(flow):
         rank_[i] = cost[i] + max([lat[i]] + [w + rank_[j] for j, w in nxt[i]])
     each = [tables(m) for m in models]
 
@@ -700,7 +807,17 @@ def arrange(ops, deps, soft, queues):
             total.append(top)
         return total
 
-    def schedule(prio, prv=prv, nxt=nxt, end=None):
+    label = [o[0] + ":" + "<".join(f[0].rstrip("0123") for f in o[3][:1] + o[2][:1]) for o in ops]
+    bias = [CFG["bias"].get(s, 0.0) for s in label]
+    if CFG["early"]:
+        for i in range(label.index("V:ui<pu")):
+            if qof[i] in "VS" and ops[i][4] == "c":
+                bias[i] = max(bias[i], rank_[label.index("V:ui<pu")] - CFG["early"] - rank_[i])
+    look = [CFG["wait"].get(s, CFG["look"]) for s in label]
+
+    def schedule(prio, prv=prv, nxt=nxt, end=None, fore=True):
+        if fore:
+            prio = [p + b for p, b in zip(prio, bias)]
         left = [len(p) for p in prv]
         ready = [0.0] * n
         pool = {q: [] for q in queues}
@@ -708,24 +825,30 @@ def arrange(ops, deps, soft, queues):
             if not left[i]:
                 pool[qof[i]].append(i)
         free = {q: 0.0 for q in pool}
+        when = {q: 0.0 if pool[q] else 1e30 for q in pool}
         seq = []
         while len(seq) < n:
-            now, q = min((max(free[q], min(ready[i] for i in pool[q])), q) for q in pool if pool[q])
-            i = max((i for i in pool[q] if ready[i] <= now), key=lambda i: (prio[i], -i))
-            soon = [j for j in pool[q] if now < ready[j] <= now + CFG["look"] * cost[i] and prio[j] > prio[i]]
+            q = min(when, key=when.get)
+            now, mine = when[q], pool[q]
+            i = max([i for i in mine if ready[i] <= now], key=lambda j: prio[j])
+            soon = [j for j in mine if now < ready[j] <= now + look[i] * cost[i] and prio[j] > prio[i]]
             if soon:
                 i = max(soon, key=lambda j: prio[j])
                 now = ready[i]
-            pool[q].remove(i)
+            mine.remove(i)
             seq.append(i)
-            free[q] = now + cost[i]
+            now = free[q] = now + cost[i]
             if end is not None:
-                end[i] = free[q]
+                end[i] = now
+            when[q] = max(now, min([ready[j] for j in mine])) if mine else 1e30
             for j, w in nxt[i]:
-                ready[j] = max(ready[j], free[q] + w)
+                if now + w > ready[j]:
+                    ready[j] = now + w
                 left[j] -= 1
                 if not left[j]:
-                    pool[qof[j]].append(j)
+                    k = qof[j]
+                    pool[k].append(j)
+                    when[k] = min(when[k], max(free[k], ready[j]))
         return seq
 
     seq = schedule(rank_)
@@ -736,17 +859,186 @@ def arrange(ops, deps, soft, queues):
     for _ in range(CFG["turns"]):
         fwd, bwd = [0.0] * n, [0.0] * n
         schedule(back, end=fwd)
-        schedule(fwd, nxt, prv, bwd)
+        schedule(fwd, nxt, prv, bwd, False)
         back = [CFG["mix"] * b + (1 - CFG["mix"]) * o for b, o in zip(bwd, back)]
         s2 = schedule(back)
         l2 = length(s2)
         if sum(l2) < sum(span):
             seq, span, prio = s2, l2, np.array(back)
+    kinds, seen, stage = {}, {}, 0
+    kind = []
+    for o in ops:
+        key = (o[0], stage > 0) + tuple(f[0].rstrip("0123") for f in o[3][:1] + o[2][:1])
+        seen[key] = seen.get(key, 0) + 1
+        kind.append(kinds.setdefault(key + (seen[key] // (CFG["pg"] if o[0] == "P" else 1),), len(kinds)))
+        if o[0] == "A":
+            seen, stage = {}, stage + 1
+    kind = np.array(kind)
+    shift = np.zeros(len(kinds))
     for _ in range(CFG["passes"]):
-        trial = prio + rng.normal(0.0, CFG["shift"], n) * (rng.rand(n) < CFG["share"])
-        s2 = schedule(trial.tolist())
+        trial = shift + rng.normal(0.0, CFG["shift"], len(kinds)) * (rng.rand(len(kinds)) < CFG["share"])
+        s2 = schedule((prio + trial[kind]).tolist())
         l2 = length(s2)
         if sum(l2) < sum(span):
-            seq, span, prio = s2, l2, trial
-    CFG["span"], CFG["path"] = span, max(rank_)
+            seq, span, shift = s2, l2, trial
+    seq = settle(seq, qof, kind.tolist(), [tables(m) for m in CFG["settle"]] or [(cost, lat, prv)], rng)
+    seq = polish(seq, qof, cost, lat, prv, nxt, rng)
+    CFG["span"], CFG["path"] = length(seq), max(rank_)
+    return seq
+
+
+def settle(seq, qof, kind, each, rng):
+    n = len(seq)
+    if not CFG["tries"]:
+        return seq
+    before = [[d for d, w in p] for p in each[0][2]]
+
+    def run(seq, tab):
+        cost, lat, prv = tab
+        end, why, free, last = [0.0] * n, [0] * n, {}, {}
+        for i in seq:
+            q = qof[i]
+            s, y = free.get(q, 0.0), ~last.get(q, n)
+            for d, w in prv[i]:
+                if end[d] + w > s:
+                    s, y = end[d] + w, d
+            end[i] = free[q] = s + cost[i]
+            why[i] = y
+            last[q] = i
+        i = max(seq[-40:], key=lambda i: end[i] + lat[i])
+        return end[i] + lat[i], i, end, why
+
+    def order(place):
+        key = [0.0] * n
+        for i in range(n):
+            k = base[i] + place[kind[i]]
+            for d in before[i]:
+                if key[d] >= k:
+                    k = key[d] + 0.001
+            key[i] = k
+        return sorted(range(n), key=lambda i: key[i]), key
+
+    def judge(seq):
+        total, pairs = 0.0, []
+        for tab in each:
+            top, i, end, why = run(seq, tab)
+            total += top
+            while i != n:
+                y = why[i]
+                if y < 0:
+                    y = ~y
+                    if y != n:
+                        pairs.append((y, i))
+                i = y
+        return total / len(each), pairs
+
+    top, i, end, why = run(seq, each[0])
+    base, place, at, stage = [0.0] * n, {}, 0.0, 0
+    for i in range(n):
+        base[i] = at
+        if stage <= CFG["model"] or kind[i] not in place:
+            place[kind[i]] = end[i] - each[0][0][i] - at
+        if qof[i] == "A":
+            at, stage = end[i], stage + 1
+    first = judge(seq)[0]
+    now, key = order(place)
+    top, pairs = judge(now)
+    best = (top, now)
+    dbg = top
+    for step in range(CFG["tries"]):
+        p, i = pairs[rng.randint(len(pairs))]
+        trial = dict(place)
+        far = CFG["far"] * rng.rand() ** 2
+        if rng.rand() < 0.5:
+            goal, todo = key[p] - far - 0.01, [i]
+            while todo:
+                j = todo.pop()
+                trial[kind[j]] = min(trial[kind[j]], goal - base[j])
+                todo += [d for d in before[j] if key[d] > goal and base[d] + trial[kind[d]] > goal]
+        else:
+            trial[kind[p]] = key[i] + far + 0.01 - base[p]
+        s2, k2 = order(trial)
+        t2, p2 = judge(s2)
+        if t2 <= top + CFG["warm"] * (1 - step / CFG["tries"]) * rng.rand() ** 2:
+            place, key, top, pairs = trial, k2, t2, p2
+            if t2 < best[0]:
+                best = (t2, s2)
+    CFG["dbg"] = (first, dbg, best[0], top)
+    return best[1] if best[0] < first else seq
+
+
+def polish(seq, qof, cost, lat, prv, nxt, rng):
+    n = len(seq)
+
+    def run(seq, at, end, why):
+        free, last = {}, {}
+        for i in seq[:at]:
+            last[qof[i]] = i
+        for q, i in last.items():
+            free[q] = end[i]
+        for i in seq[at:]:
+            q = qof[i]
+            s, y = free.get(q, 0.0), ~last.get(q, n)
+            for d, w in prv[i]:
+                if end[d] + w > s:
+                    s, y = end[d] + w, d
+            end[i] = free[q] = s + cost[i]
+            why[i] = y
+            last[q] = i
+        i = max(seq[-40:], key=lambda i: end[i] + lat[i])
+        return end[i] + lat[i], i
+
+    def chain(i, why):
+        pairs = []
+        while i != n:
+            y = why[i]
+            if y < 0:
+                y = ~y
+                if y != n:
+                    pairs.append((y, i))
+            i = y
+        return pairs
+
+    end, why = [0.0] * n, [0] * n
+    top, tail = run(seq, 0, end, why)
+    pairs = chain(tail, why)
+    for step in range(CFG["moves"]):
+        p, i = pairs[rng.randint(len(pairs))]
+        pos = {x: k for k, x in enumerate(seq)}
+        a, b = pos[p], pos[i]
+        if rng.rand() < 0.5:
+            more = rng.randint(4)
+            while more and a > 0:
+                a -= 1
+                more -= qof[seq[a]] == qof[i]
+            move, todo = {i}, [i]
+            while todo:
+                for d, w in prv[todo.pop()]:
+                    if pos[d] >= a and d not in move:
+                        move.add(d)
+                        todo.append(d)
+            if p in move:
+                continue
+            part = seq[a:b + 1]
+            new = seq[:a] + [x for x in part if x in move] + [x for x in part if x not in move] + seq[b + 1:]
+        else:
+            more = rng.randint(4)
+            while more and b < n - 1:
+                b += 1
+                more -= qof[seq[b]] == qof[i]
+            move, todo = {p}, [p]
+            while todo:
+                for d, w in nxt[todo.pop()]:
+                    if pos[d] <= b and d not in move:
+                        move.add(d)
+                        todo.append(d)
+            if i in move:
+                continue
+            part = seq[a:b + 1]
+            new = seq[:a] + [x for x in part if x not in move] + [x for x in part if x in move] + seq[b + 1:]
+        e2, w2 = end[:], why[:]
+        t2, l2 = run(new, a, e2, w2)
+        if t2 <= top + CFG["heat"] * (1 - step / CFG["moves"]) * rng.rand() ** 3:
+            seq, end, why, top = new, e2, w2, t2
+            pairs = chain(l2, why)
     return seq

import numpy as np
from concourse.mybir import AluOpType, ActivationFunctionType

W, L, NS = 3072, 1024, 4
PAD = 128
MIR = 64
BF, F32, I32, U16, F16 = "bfloat16", "float32", "int32", "uint16", "float16"
_SB = {
    "x": (W, BF), "oci": (L, I32), "tab": (L + MIR + 32, F32), "win": (PAD + W + 32, F32),
    "vm": (4128, BF), "mg": (4128, BF), "yr0": (4096, BF), "yr1": (4096, BF), "yrh": (4096, BF),
    "vmr": (1040, BF), "mgr": (1040, BF), "yrr": (1024, BF),
    "c0": (256, U16), "c1": (256, U16), "cr": (64, U16),
    "pi": (2, I32), "pj": (2, I32), "cols": (48, F32), "wti": (1, I32), "thi": (1, I32), "thf": (1, F16), "thc": (1, F32),
    "colf": (256, F32), "rr": (256, BF), "hi4": (64, BF), "lo64": (64, BF), "hi16": (128, F32),
    "mkb": (W, BF), "m8": (128, BF), "m8a": (128, BF), "ymb": (PAD + 2080, BF), "ymh": (W - 2048, BF), "ones": (32, BF),
    "rslot": (4, F32),
    "z1": (144, BF), "zf": (144, BF), "zm": (144, BF), "zw": (144, BF), "zl": (144, BF), "zn": (144, BF), "zp": (144, BF), "raw": (2048, BF),
    "bo": (128, BF), "bd": (128, BF), "bw": (128, BF), "bn": (128, BF), "bt": (128, BF),
    "tri": (128, BF), "idn": (128, BF), "idp": (128, BF), "e0": (128, BF), "g8": (128, F16), "idg": (128, F32),
    "c17": (128, BF), "cq": (128, BF), "c256": (256, BF), "kseg": (256, BF), "rb": (256, BF), "rw": (256, BF),
    "dm": (384, BF), "nsel": (2048, F16), "dg": (64, BF), "sp16": (16, F16),
    "lp": (16, U16), "qp": (16, F32), "y0p": (256, BF), "lf": (16, U16), "ct": (16, BF), "oh": (16, F32),
    "dli": (64, I32), "dlc": (64, F16), "dl8": (L, F16),
    "base": (64, I32), "ui": (64, I32), "uu": (64, I32), "sq": (64, I32), "t32": (64, I32), "zz": (64, I32), "li": (64, I32),
    "l0": (16, U16), "l1": (32, U16), "lv": (4, U16), "ai": (1, I32), "ac": (4, F32), "us": (64, F32),
    "rs": (256, F32), "ji": (16, I32), "ja": (16, I32), "jm": (16, I32), "j16": (16, U16), "jr": (4, U16),
    "thr": (16, F32), "dd": (16, I32), "idh": (128, F16), "bnh": (128, F16),
    "rm": (256, F32), "ki": (16, I32), "ka": (16, I32), "k16": (16, U16),
    "y0f": (256, BF), "y1n": (256, BF), "y1p": (256, BF), "y1r": (256, BF), "y2n": (256, BF), "lvn": (256, BF), "inv": (4, BF),
    "ad": (256, BF), "adf": (256, F32), "nn": (256, F32), "t1": (256, F32), "t2": (256, F32),
    "adr": (64, BF), "adfr": (64, F32),
    "prop": (512, F32), "eqa": (512, BF), "cna": (512, F32), "nd2": (512, BF), "ru2": (512, BF), "r32": (256, BF), "ndg": (256, BF), "lvw": (16, BF), "id16": (128, BF), "rup": (256, BF), "offa": (32, U16),
    "lw": (16, F16), "eqn": (384, BF), "eqm": (384, BF), "cz": (256, F32), "offn": (32, U16),
    "yab": (2048, F32),
    "rdy": (16, BF), "pre": (16, BF), "rp": (16, BF), "slot": (16, U16),
    "snd0": (528, BF), "snd1": (528, BF), "snd2": (528, BF), "snd3": (528, BF),
    "land0": (80, BF), "land1": (80, BF), "land2": (80, BF), "land3": (80, BF),
}
_PS = ["pk", "pr", "pa", "pb", "pu", "psm", "prk", "pz"]
_AT, _END = {}, {}
for _k, (_n, _d) in _SB.items():
    _b = "pool_" + _d if _n <= 144 else _k
    _AT[_k] = (_b, _END.get(_b, (0, _d))[0])
    _END[_b] = (_AT[_k][1] + -(-_n // 16) * 16, _d)
for _k in ("mk8", "mk9"):
    _SB[_k], _AT[_k] = _SB["mkb"], _AT["mkb"]
SCRATCH = {k: ("sbuf", [128, v[0]], v[1]) for k, v in _END.items()}
SCRATCH.update({k: ("psum", [128, 512], F32) for k in _PS})
NDMA = 20
SEMAPHORES = ["sV", "sS", "sP", "sG", "sent"] + ["arr%d" % t for t in range(NS)] + ["d%d" % i for i in range(NDMA)]

SILU_ONE = 1.2784645427610738
NENG = 8
U18 = 2.0 ** -18
CFG = dict(
    f0=(2, 2, 3, 1, 4, 4, 4, 8, 2, 2), f00=(4, 4, 4, 4, 7, 5, 2, 2), m0=(12, 4, 8, 2, -6), m00=(4, 2, 2, 4, 4, 4, 4, 2, 6),
    f1=(1, 3, 8, 1, 1, 2, 7, 7, 2), m1=(12, 4, 8, 2, 2, 2, -2), rch=(8, 6, 2),
    bias={"V:c<cz": 2300, "P:pu<zw": 2000, "V:l<li": 2000, "V:rs<kseg": 2000, "V:lw<li": 3000, "P:pz<idn": -2000,
          "P:pk<cq": -300, "S:vm<pb": 300, "S:cz<tab": -300, "S:yrr<land": 800, "V:vm<x": -800},
    wait={"S:yab<pz": 1.2, "V:vmr<x": 0.5, "S:nn<tab": 0.5},
    yh=("GGGGGGGGVVVVVVVV", "GGGGGGGGGGSVVVVV"), yrr="SSSSSSSSVVVVVVVV", y00=("VVVVVVVVVVVVVVVV", "GGGGGGVVVVVVSSSS"),
    two="2222", sr=(1, 1, 2, 2), we="SSSSSV", ce="SSVVVSSS", early=0.0, cs="SSSVSS", pair=True, uscan=True, look=0.35,
    order={"G": ("pi hi4 lo64 rr qp hi16 yr*6 lvn r32 bt tri nsel*16 yrh*16 yr*11 send yr*5", "yr-*9 y0f lvn yr-*7 yrh*16 send"),
           "S": ("oci x", "")},
    pg=16, settle=(), tries=0, model=2, far=400.0, warm=200.0, moves=0, heat=0.0, turns=2, mix=0.05, passes=800, seed=1, shift=300.0, share=0.03,
    models=((0.9, 1.56, 3.8, 0.0, 0.42, 215.0, 2000.0, 2800.0, 0.0), (0.85, 1.35, 3.2, 0.0, 0.45, 190.0, 2000.0, 3500.0, 30.0),
            (1.05, 1.7, 4.2, 0.0, 0.5, 230.0, 2000.0, 3200.0, 0.0), (1.0, 1.56, 3.8, 0.0, 0.47, 150.0, 2000.0, 3000.0, 20.0)),
)


def rank_program(g, core, T, topo):
    rank = T.rank_of(core)
    if rank is None:
        return
    A_ = AluOpType
    AF = ActivationFunctionType
    nrank = len(T.cores)
    ops = []

    def a(name, c0=0, c1=None, st=1, p=None):
        n = 512 if name in _PS else _SB[name][0]
        c1 = n if c1 is None else c1
        ps = slice(0, 128) if p is None else p
        b, o = (name, 0) if name in _PS else _AT[name]
        ap = T[b][ps, o + c0:o + c1] if st == 1 else T[b][ps, o + c0:o + c1:st]
        return (ap, [(name, c0, c1, st)])

    def ind(w, o):
        return (w[0].indirect(o[0]), w[1], o[1])

    def val(s):
        return s[0] if isinstance(s, tuple) else s

    def num(s):
        f = s[-1][0]
        return len(range(f[1], f[2], f[3])) * (16 if len(s) == 3 else 1)

    def narrow(*aps):
        return all(s[1][0][0] not in _PS and _SB[s[1][0][0]][1] in (BF, U16, F16) for s in aps)

    def span(o, i, per, fused=False):
        if len(o) == 3:
            return ("s", num(o))
        if len(i) == 3:
            return ("f" if fused else "g", num(i))
        return ("c", max(64, num(o) * per))

    def rec(q, fn, outs, ins, cost, kind="c", lat=("n", 0.0)):
        rd, wr = [], []
        for o in outs:
            wr += o[1]
            if len(o) == 3:
                rd += o[2]
        for s in ins:
            if isinstance(s, tuple):
                rd += s[1]
                if len(s) == 3:
                    rd += s[2]
        ops.append([q, fn, rd, wr, kind, ("a", cost[1]) if q == "S" and cost[0] == "c" else cost, lat])

    def ts(o, i, s1, s2, o0, o1=None):
        c = span(o, i, 0.5 if narrow(o, i) else 1)
        if o1 is None:
            rec("V", lambda: g.vector.tensor_scalar(o[0], i[0], val(s1), None, o0), [o], [i, s1], c)
        else:
            rec("V", lambda: g.vector.tensor_scalar(o[0], i[0], val(s1), val(s2), o0, o1), [o], [i, s1, s2], c)

    def tt(o, i0, i1, op):
        c = span(o, i0, 1 if i0[1][0][0] in _PS or i1[1][0][0] in _PS else 2, True)
        rec("V", lambda: g.vector.tensor_tensor(o[0], i0[0], i1[0], op), [o], [i0, i1], c)

    def cp(o, i):
        rec("V", lambda: g.vector.tensor_copy(o[0], i[0]), [o], [i], span(o, i, 0.5 if narrow(o, i) else 1))

    def scan(o, d0, d1, o0, o1, first=0.0):
        rec("V", lambda: g.vector.tensor_tensor_scan(o[0], d0[0], d1[0], first, o0, o1), [o], [d0, d1],
            span(o, d0, 0.5 if narrow(o, d0, d1) else 1))

    def fill(o, c):
        rec("V", lambda: g.vector.memset(o[0], c), [o], [], span(o, o, 0.5 if narrow(o) else 1))

    def act(o, i, f=AF.Identity, bias=0.0, scale=1.0):
        if f == AF.Silu:
            rec("S", lambda: g.scalar.activation(o[0], i[0], f), [o], [i], span(o, i, 1))
        else:
            rec("S", lambda: g.scalar.activation(o[0], i[0], f, bias=val(bias), scale=val(scale)), [o], [i, bias, scale], span(o, i, 1))

    def aff(o, i, m, b=0.0, eng=None):
        if (eng or CFG["ce"][6]) == "S":
            act(o, i, AF.Identity, b, m)
        else:
            ts(o, i, m, b, A_.mult, A_.add)

    def mm(o, l, r, start=False):
        c = max(64, num(r)) * (4 if _SB[l[1][0][0]][1] == F32 else 1)
        rec("P", lambda last: g.tensor.matmul(o[0], l[0], r[0], start, last), [o], [l, r], ("p", c))
        ops[-1].append(start)

    def iota(o, pat, base=0, cm=0, flag=True):
        if flag:
            rec("G", lambda: g.iota(o[0], pat, base, cm, allow_small_or_imprecise_dtypes=True), [o], [], ("c", 130 + 2 * num(o)))
        else:
            rec("G", lambda: g.iota(o[0], pat, base, cm), [o], [], ("c", 130 + 2 * num(o)))

    def asel(o, i, pat, cmp, fl, base, cm):
        rec("G", lambda: g.affine_select(o[0], i[0], pat, cmp, fl, base, cm), [o], [i], ("c", 170 + 2 * num(o)))

    QO = {"V": g.vector, "S": g.scalar, "P": g.tensor, "G": g, "Y": g.sync}

    def dma(q, o, i, kb):
        rec(q, lambda: QO[q].dma_start(o[0], i[0]), [o], [i], ("n", 1000 if q == "G" else 100), "d", ("d", kb))

    def ext(ap):
        return (ap, [])

    def sel(fam, r):
        return a(fam, 15 - r, 143 - r)

    g16, p1, p8 = slice(0, 128, 16), slice(0, 1), slice(0, 8)
    col = lambda j: a("cols", j, j + 1)
    top = W - 256

    dma("Y", a("x", top, W), ext(T.xc[:, top:W]), 64)
    dma("S", a("oci"), ext(T.oc[:]), 400)
    dma("Y", a("wti"), ext(T.wt[:]), 1)
    dma("Y", a("mkb", p=p8), ext(T.mk[:]), 48)
    dma("S", a("x", 0, top), ext(T.xc[:, 0:top]), 750)
    dma("Y", a("dli"), ext(T.dl[:]), 32)
    dma("Y", a("thi", p=p8), ext(T.th[:]), 1)

    iota(a("pi"), [[2, 2]], 0, 1, False)
    p48 = slice(0, W // 64)
    for row, tile, step in ((8, "hi4", 0), (9, "lo64", 1)):
        iota(a(tile, p=p48), [[step, 64]], 0, 1 - step)
        dma("Y", a("mk%d" % row, p=slice(row, row + 1)), a(tile, p=p48), 6)
    fill(a("c256"), 1.0)
    scan(a("colf"), a("c256"), a("c256"), A_.mult, A_.add, -1.0)
    iota(a("rr"), [[0, 16], [1, 16]])
    iota(a("hi16"), [[16, 8], [0, 16]])
    iota(a("qp"), [[8, 2], [32, 8]])
    (P_, R_, K2, G_, G15, IS0, IS1, IS2, IS3, IS4, DIG, WN, R16, R255, DM, DM1, DN0, DN1, MW, LW, SC, BI, P16, P3, R8, DY, DY1,
     J0, J1, JR, DEAD, T0, T1, T2, T3, T4, T5, T6, T7, T8, T9) = range(41)
    ts(a("pj"), a("pi"), 15, None, A_.bitwise_and)
    cp(col(P_), a("pi", 0, 1))
    cp(a("cols", R_, R_ + 2), a("pj"))
    ts(a("cols", IS0, IS0 + 5), a("colf", 0, 5), col(R_), None, A_.is_equal)
    for j, m, v in ((R16, 16.0, 0.0), (R255, -1.0, 255.0), (DM, 1.0, PAD + W), (DN0, 1.0, L + MIR), (DN1, 1.0, L + MIR + 16),
                    (DY, 1.0, PAD + 2048), (DY1, 1.0, PAD + 2064), (DM1, 1.0, PAD + W + 16), (J0, 128.0, -240 - (1 << 21)), (JR, 64.0, -240 - (1 << 21))):
        aff(col(j), col(R_), m, float(v), CFG["ce"][5])
    ts(col(G15), col(P_), col(R_), 15.0, A_.subtract, A_.add)
    ts(col(G_), col(P_), col(R_), None, A_.subtract)
    ts(col(WN), a("wti"), -1.0, None, A_.mult)
    ts(col(R8), col(R_), 8.0, 8.0, A_.is_ge, A_.mult)
    for j, i, m, v in ((P16, P_, 16.0, 0.0), (P3, P_, 16.0, 1.5), (LW, IS0, -16.0, 0.0),
                       (MW, IS3, -U18, col(IS0)), (T0, IS0, 1.0, col(IS3)), (BI, T0, SILU_ONE, 0.0), (SC, T0, -1.0, 1.0),
                       (T1, IS1, 64.0, col(IS2)), (T2, IS4, -64.0, col(T1)), (DIG, T2, 1.0 / 4096, 0.0),
                       (T3, R8, 2.0, -240.0 - (1 << 21)), (J1, R_, 256.0, col(T3)), (T4, IS4, 128.0, 0.0),
                       (T5, IS1, 128.0, col(T4)), (DEAD, IS2, 127.0, col(T5)), (T6, R_, -4.0, 64.0), (T7, IS0, 32.0, 0.0),
                       (T9, IS2, 128.0, col(T5))):
        aff(col(j), col(i), m, v, CFG["ce"][7])
    act(a("m8a"), a("colf", 0, 128), AF.Abs, col(P3), -1.0)
    ts(a("m8"), a("m8a"), 1.5, None, A_.is_equal)
    ts(col(T8), col(P_), 8.0, 64.0, A_.is_lt, A_.mult)
    ts(a("m8a"), a("rr", 0, 128), col(T8), 7.0, A_.add, A_.add)
    ts(a("m8a"), a("m8a"), col(P_), None, A_.is_equal)
    tt(a("m8"), a("m8"), a("m8a"), A_.add)
    ts(a("idp"), a("colf", 0, 128), col(P_), None, A_.is_equal)
    p10 = slice(0, 10)
    for b, eng in zip(range(5, -1, -1), CFG["we"]):
        o = a(("pa", "pb", "pz", "psm", "pk", "pr")[b], 0, 512)
        rows = a("mkb", 512 * b, 512 * b + 512, p=p10)
        mm(o, a("m8", p=p10), (rows[0], rows[1] + a("mk8")[1] + a("mk9")[1]), True)
        aff(a("win", PAD + 512 * b, PAD + 512 * b + 512), o, 1.0, col(T9), eng)
    ts(a("zw"), a("colf", 0, 144), col(G15), col(WN), A_.is_equal, A_.mult)
    ts(a("z1"), a("colf", 0, 144), col(G15), None, A_.is_equal)
    for fam, w in (("zf", 1.0 / 256), ("zm", col(MW)), ("zl", col(LW))):
        aff(a(fam), a("z1"), w, eng=CFG["ce"][0])
    if CFG["sr"]:
        aff(a("zn"), a("zf"), -1.0)
        aff(a("zp"), a("zw"), -1.0)
    ts(a("bo"), a("hi16"), col(G_), None, A_.is_equal)
    for fam, w in (("bd", col(DIG)), ("bw", col(WN)), ("bn", -1.0)):
        aff(a(fam), a("bo"), w, eng=CFG["ce"][1])
    fill(a("c17"), 2 * U18)
    fill(a("cq"), -0.25)
    aff(a("c256"), a("colf"), -1.0, 256.0)
    ts(a("kseg"), a("rr"), 0.0, None, A_.not_equal)
    aff(a("rb"), a("kseg"), 64.0, -64.0, CFG["ce"][2])
    aff(a("rw"), a("rb"), -1.0, -4 * U18, CFG["ce"][3])
    aff(a("rup"), a("rb"), -1.0, 0.0, CFG["ce"][3])
    ts(a("dm", 0, 256), a("rr"), col(R_), 2048.0, A_.is_ge, A_.mult)
    fill(a("dm", 256, 384), 0.0)
    ts(a("ndg"), a("rr"), col(R_), None, A_.not_equal)
    iota(a("r32"), [[0, 8], [1, 32]])
    for k in range(2):
        ts(a("nd2", 256 * k, 256 * k + 256), a("r32"), -16.0 * k, col(R_), A_.add, A_.not_equal)
        ts(a("ru2", 256 * k, 256 * k + 256), a("r32"), 0.0, 64.0, A_.is_equal, A_.mult)
    aff(a("dg"), a("ndg", 0, 64), -1048576.0, 1048576.0)
    ts(a("lf"), a("colf", 0, 16), col(R16), None, A_.add)
    ts(a("lp"), a("qp"), col(R8), col(R_), A_.add, A_.add)
    aff(a("ct"), a("colf", 0, 16), -16.0, col(R255))
    ts(a("oh"), a("colf", 0, 16), col(K2), None, A_.is_equal)
    aff(a("rslot"), a("colf", 0, 4), -1.0, col(T6))
    for e, c in enumerate((DN0, DN1 if CFG["pair"] else DN0)):
        ts(a("sp16", e, 16, 2), a("colf", 0, 8), 0.0, col(c), A_.mult, A_.add)
    aff(a("idg"), a("idp"), -1.0)
    aff(a("idn"), a("idp"), -1.0, eng=CFG["ce"][4])
    aff(a("id16"), a("idp"), -256.0, eng=CFG["ce"][4])
    aff(a("e0"), a("idp"), 0.0, col(T7), CFG["ce"][4])
    ts(a("g8"), a("hi16"), col(P16), None, A_.is_equal)
    fill(a("ones"), 1.0)
    fill(a("tab", L, L + MIR + 32), 0.0)
    for b in (0, 2064):
        fill(a("vm", b, b + 16), 0.0)
    for o in (a("mg", 0, 16), a("mg", 2064, 2080), a("mgr", 0, 16)):
        aff(o, a("rr", 0, 16), 0.0, col(DEAD))
    for t in range(NS):
        fill(a("snd%d" % t, 0, 80), 0.0)
    asel(a("bt"), a("bn"), [[-1, 128]], A_.is_ge, 0.0, 0, 1)
    asel(a("tri"), a("bt"), [[1, 128]], A_.not_equal, -256.0, 0, -1)
    cp(a("idh"), a("idp"))
    cp(a("bnh"), a("bn"))
    for r in range(16):
        asel(a("nsel", 128 * r, 128 * r + 128), a("bnh"), [[-16, 8], [0, 16]], A_.is_equal, 0.0, -r, 1)
    for b in range(0, L, 128):
        cp(a("tab", b, b + 128), a("oci", b, b + 128))
    ts(a("dlc"), a("dli"), -2048.0, None, A_.add)
    dma("Y", a("dl8", p=p8), a("dlc"), 32)
    cp(a("thf", p=p8), a("thi", p=p8))
    mm(a("prk", 48, 49), a("g8", p=p8), a("thf", p=p8), True)
    act(a("thc"), a("prk", 48, 49), AF.Identity, -129.0 / 256, 1.0 / 256)

    def first_places(n, x0, x1, at):
        for h in range(2):
            for r in range(16):
                mm(a("pu", n * h, n * h + n), sel("zw", r), a("x", x0 + 8 * h + r + 8 * (r >> 3), x1, 32), r == 0)
        n *= 2
        ts(a("ui", 0, n), a("pu", 0, n), -1.0, None, A_.mult)
        ts(a("uu", 0, n), a("ui", 0, n), 4095, None, A_.bitwise_and)
        tt(a("sq", 0, n), a("uu", 0, n), a("uu", 0, n), A_.mult)
        ts(a("t32", 0, n), a("uu", 0, n), 1184.0, None, A_.mult)
        tt(a("zz", 0, n), a("sq", 0, n), a("t32", 0, n), A_.add)
        if at:
            ts(a("base", at, at + n), a("zz", 0, n), 32736, None, A_.bitwise_and)
        else:
            ts(a("li", 0, n), a("zz", 0, n), 5, 1023, A_.arith_shift_right, A_.bitwise_and)
            cp(a("l0"), a("li", 0, n))

    first_places(8, top, W, 0)
    first_places(24, 2048, top, 16)

    def yrep(dst, who, src, neg, n=256, at=0, pos=None):
        for k, eng in enumerate(who):
            o = a(dst, 16 * at + k, 16 * (at + n), 16)
            if eng == "V" and neg:
                ts(o, src, -1.0, None, A_.mult)
            elif eng == "V":
                cp(o, src)
            elif eng == "S":
                act(o, src, AF.Identity, 0.0, -1.0 if neg else 1.0)
            else:
                asel(o, pos or src, [[0, n]], A_.is_ge, 0.0, 0, 0)

    def ycols(t):
        return a("x", W - 256 * (t + 1), W - 256 * t)

    def names(dst, tab, lst, t, eng="V"):
        if eng == "V":
            ts(dst, ind(tab, lst), (11 - t) / 16.0, -15.0 / 32, A_.mult, A_.add)
        else:
            f = dst[1][0]
            aff(a("cz", f[1], f[2]), ind(tab, lst), (11 - t) / 16.0, -15.0 / 32, "S")
            cp(dst, a("cz", f[1], f[2]))

    def at16(j):
        return 16 + j + 16 * (j >= 2048)

    def opened(bank, n, dead=True):
        mm(a(bank, 0, n), a("c17", p=p1), a("c256", 0, n, p=p1), True)
        if dead:
            mm(a(bank, 0, n), a("cq", p=p1), a("rb", 0, n, p=p1))

    marks = a("win", PAD, PAD + W)

    def main(c, yr, hop, fch, mch, sch=()):
        u = 0
        for n, w in enumerate(sch):
            raw, bank = a("raw", 128 * u, 128 * (u + w)), a(("pz", "pb", "prk")[n % 3], 0, 128 * w)
            act(raw, ind(a("x"), a(c, 8 * u, 8 * (u + w))))
            mm(bank, a("idp"), a(yr, 128 * u, 128 * (u + w)), True)
            mm(bank, a("idn"), raw)
            act(a("vm", 16 + 128 * u, 16 + 128 * (u + w)), bank, AF.Relu)
            u += w
        skip = u
        for w in fch:
            if skip >= w:
                skip -= w
                continue
            w, skip = w - skip, 0
            o = at16(128 * u)
            tt(a("vm", o, o + 128 * w), ind(a("x"), a(c, 8 * u, 8 * (u + w))), a(yr, 128 * u, 128 * (u + w)), A_.min)
            u += w
        u = 0
        for w in mch:
            o = at16(128 * u)
            o, i = a("mg", o, o + 128 * abs(w)), ind(marks, a(c, 8 * u, 8 * (u + abs(w))))
            act(o, i) if w > 0 else cp(o, i)
            u += abs(w)
        for h, bank in enumerate(("pk",) if hop else ("pr", "pk")):
            n = 256 if hop else 128
            opened(bank, n)
            if hop:
                mm(a(bank, 0, n, 16), a("idn"), a("lvw"))
            for u in range(16):
                if not hop:
                    mm(a(bank, 0, n, 16), sel("zl", u), a("lvn", 16 * u + 8 * h, 16 * u + 8 * h + 8))
                for buf, fam in (("vm", "zf"), ("mg", "zm")):
                    o = at16(2048 * h + n * u)
                    if buf == "vm" and 16 * h + u < sum(sch):
                        mm(a(bank, 0, n), sel(fam, u), a(yr, n * u, n * u + n))
                        fam = "zn"
                    mm(a(bank, 0, n), sel(fam, u), a(buf, o, o + n))

    def distinct(bank, dig, n, dummy, at=0, wide=None):
        q, e = n // 16, at // 16
        if wide:
            flat = (wide, 0) if n == 256 else (bank, 256)
            mm(a(bank, 0, 2 * n), a("idp"), a("nd2", 256 - n, 256 + n), True)
            for k in range(2):
                mm(a(bank, k * n, k * n + n), a("bd"), a(dig, at, at + n))
            for k in range(2):
                mm(a(flat[0], flat[1] + k * n, flat[1] + k * n + n), a("bd"), a(dig, at, at + n), True)
            scan(a("prop", 0, 2 * n), a("ru2", 0, 2 * n), a(bank, 0, 2 * n), A_.add, A_.min)
            tt(a("eqa", 0, 2 * n), a("prop", 0, 2 * n), a(flat[0], flat[1], flat[1] + 2 * n), A_.is_equal)
            scan(a("cna", 0, 2 * n), a("eqa", 0, 2 * n), a(bank, 0, 2 * n), A_.add, A_.min)
            for k in range(2):
                ts(a("offa", 2 * e + k, 2 * e + q, 2), a("cna", k * n + 31, k * n + n, 32), 4096.0, col(dummy + k), A_.mult, A_.min)
            return
        mm(a(bank, 0, n), a("idp"), a("ndg", 0, n), True)
        mm(a(bank, 0, n), a("bd"), a(dig, at, at + n))
        mm(a(bank, 256, 256 + n), a("bd"), a(dig, at, at + n), True)
        scan(a("prop", 0, n), a("rup", 0, n), a(bank, 0, n), A_.add, A_.min)
        tt(a("eqa", 0, n), a("prop", 0, n), a(bank, 256, 256 + n), A_.is_equal)
        scan(a("cna", 0, n), a("eqa", 0, n), a(bank, 0, n), A_.add, A_.min)
        ts(a("offa", 2 * e, 2 * (e + q), 2), a("cna", 15, n, 16), 4096.0, col(dummy), A_.mult, A_.min)

    def best(bank, n, dst, first):
        q = n // 16
        scan(a("rs", 0, n), a("kseg", 0, n), a(bank, 0, n), A_.mult, A_.max)
        ts(a("ji", 0, q), a("rs", 15, n, 16), -1 / U18, None, A_.mult)
        ts(a("ja", 0, q), a("ji", 0, q), 1, 511 + (1 << 21), A_.arith_shift_right, A_.bitwise_and)
        ts(dst, a("ja", 0, q), col(first), 0.0, A_.add, A_.max)

    def place(src, b, n, dst, t):
        cp(a("ui", b, n), src)
        ts(a("uu", b, n), a("ui", b, n), 4095, None, A_.bitwise_and)
        tt(a("sq", b, n), a("uu", b, n), a("uu", b, n), A_.mult)
        ts(a("t32", b, n), a("uu", b, n), 1184.0, a("ac", t, t + 1) if t else 0.0, A_.mult, A_.add)
        tt(a("zz", b, n), a("sq", b, n), a("t32", b, n), A_.add)
        ts(a("li", b, n), a("zz", b, n), 5, 1023, A_.arith_shift_right, A_.bitwise_and)
        cp(a(dst, b, n), a("li", b, n))

    def mark(src, lst, bank, n, at=0, names_=("ad", "adf"), wide=None):
        ad, adf = names_
        act(a(ad, at, at + n), ind(src, lst))
        act(a(adf, at, at + n), a(ad, at, at + n), AF.Identity, col(BI), col(SC))
        distinct(bank, ad, n, DM, at, wide)
        for q in range(n // 32 if wide else 0):
            act(ind(a("win"), a("offa", at // 8 + 2 * q, at // 8 + 2 * q + 2)), a(adf, at + 32 * q, at + 32 * q + 32), AF.Silu)
        for q in range(at // 16, at // 16 if wide else (at + n) // 16):
            act(ind(a("win"), a("offa", 2 * q, 2 * q + 1)), a(adf, 16 * q, 16 * q + 16), AF.Silu)

    def ya_out(t, h):
        if h:
            mm(a("pz", 0, 256), a("bd"), a("ad"), True)
        for r in range(0 if h else 16):
            mm(a("pz", r, 256, 16), a("bd"), a("ad", 16 * r, 16 * r + 16), True)
        act(a("yab", 256 * (2 * t + h), 256 * (2 * t + h + 1)), a("pz", 0, 256), AF.Identity, -float(PAD), 4096.0)

    def name_offsets():
        mm(a("psm", 0, 16), a("id16"), a("lvw"), True)
        mm(a("psm", 0, 16), a("idh"), a("sp16"))
        tt(a("lw"), a("li", 16, 32), a("psm", 0, 16), A_.max)
        n = 384 if CFG["pair"] else 256
        mm(a("pb", 0, n), a("idp"), a("dm", 0, n), True)
        for r in range(16):
            ns = a("nsel", 128 * r, 128 * r + 128)
            mm(a("pb", r, 256, 16), a("idh"), a("lw"))
            mm(a("pb", r, 256, 16), ns, a("lw"))
            if CFG["pair"]:
                mm(a("pb", 256 + r, 384, 16), a("idh"), a("lw", 1, 16, 2))
                mm(a("pb", 256 + r, 384, 16), ns, a("lw", 0, 16, 2))
        if CFG["cs"][4] == "V":
            ts(a("eqn", 0, n), a("pb", 0, n), 0.0, 2048.0, A_.is_equal, A_.mult)
        else:
            act(a("eqm", 0, n), a("pb", 0, n), AF.Abs)
            act(a("eqn", 0, n), a("eqm", 0, n), AF.Relu, 2048.0, -2048.0)
        mm(a("psm", 0, 16), a("idh"), a("lw"), True)
        for r in range(16):
            mm(a("psm", 0, 16), a("idp"), a("eqn", r, 256, 16))
            if CFG["pair"]:
                mm(a("psm", 1, 16, 2), a("idp"), a("eqn", 256 + r, 384, 16))
        if CFG["pair"]:
            for e, c in enumerate((DN0, DN1)):
                ts(a("offn", e, 16, 2), a("psm", e, 16, 2), col(c), None, A_.min)
        else:
            ts(a("offn", 0, 32, 2), a("psm", 0, 16), col(DN0), None, A_.min)

    yrbuf = ["yr0", "yr1"]
    act(a("y0p"), ind(ycols(0), a("lp")))
    for h in range(2):
        yrep("yr0", CFG["y00"][h], a("y0p", 128 * h, 128 * h + 128), False, 128, 128 * h)

    def first_y(t):
        act(a("y0p"), ind(ycols(t), a("lp")))
        yrep(yrbuf[t % 2], "G" * 16, a("y0p"), False)

    first_y(1)
    fill(a("win", 0, PAD), 0.0)
    fill(a("win", PAD + W, PAD + W + 32), 0.0)
    fill(a("ymb", PAD + 2048, PAD + 2080), 0.0)
    fill(a("ymb", 0, PAD), 0.0)

    for t in range(NS):
        B = W - 256 * (t + 1)
        table = a("tab", 0, L)
        for h in range(2):
            names(a("c0", 128 * h, 128 * h + 128), a("tab", 0, L + MIR) if t else a("oci"), a("l0", 8 * h, 8 * h + 8), t,
                  CFG["cs"][h] if t else "V")
        asel(a("lvn"), a("win", PAD + B, PAD + B + 256), [[0, 256]], A_.is_ge, 0.0, 0, 0)
        for r in range(16):
            mm(a("psm", 0, 16), sel("zl", r), a("lvn", r, 256, 16), r == 0)
        act(a("lvw"), a("psm", 0, 16), AF.Identity, 0.0, -1.0)
        act(a("y0f"), ind(ycols(t), a("lf")))
        sch = CFG["sr"] if t else ()
        if sch:
            asel(a("y0f", 0, 128), a("y0f", 0, 128), [[0, 8], [1, 16]], A_.is_ge, 0.0, -sum(sch), 0)
        main("c0", yrbuf[t % 2], 0, CFG["f0" if t else "f00"], CFG["m0" if t else "m00"], sch)
        y1 = lambda h: ("y1p", "zp", "zn") if sch and not h else ("y1n", "zw", "zf")
        if t + 2 < NS:
            first_y(t + 2)
        for h, bank in enumerate(("pr", "pk")):
            j, b = a("j16", 8 * h, 8 * h + 8), 128 * h
            best(bank, 128, j, J0)
            tt(a("y1n", b, b + 128), ind(a("vm", 2064 * h, 2064 * h + 2064), j), a("y0f", b, b + 128), A_.subtract)
            if "G" in CFG["yh"][h] or sch:
                act(a("y1p", b, b + 128), a("y1n", b, b + 128), AF.Abs)
            yrep("yrh", CFG["yh"][h], a(y1(h)[0], b, b + 128), y1(h)[0] == "y1n", 128, b, a("y1p", b, b + 128))
            mark(a("mg", 2064 * h, 2064 * h + 2064), j, ("pa", "pb")[h], 128, b, wide=CFG["two"][h] == "2")
            for r in range(16):
                mm(a("pu", 8 * h, 8 * h + 8), sel(y1(h)[1], r), a(y1(h)[0], b + r, b + 128, 16), r == 0)
            if h:
                for r in range(16):
                    mm(a("pu", 16, 32), sel(y1(r // 8)[1], r), a(y1(r // 8)[0], 16 * r, 16 * r + 16), r == 0)
            place(a("pu", 8 * h, 32 if h else 8), 8 * h, 32 if h else 8, "l1", t)
            names(a("c1", b, b + 128), table if t else a("oci"), a("l1", 8 * h, 8 * h + 8), t, CFG["cs"][2 + h] if t else "V")
        ya_out(t, 0)
        act(a("y1r"), ind(a("y1p" if sch else "y1n"), a("lf")), AF.Identity, 0.0, -1.0 if (CFG["cs"][5] == "V") != bool(sch) else 1.0)
        act(a("nn"), ind(table, a("l1", 16, 32)))
        mm(a("pr", 0, 256), a("g8", p=p8), a("dl8", 256 * t, 256 * t + 256, p=p8), True)
        for b in range(0, 256, 64):
            mm(a("pr", b, b + 64), a("idg"), a("nn", b, b + 64))
        act(a("t2"), a("pr", 0, 256), AF.Identity, 2048.0)
        for r in range(16):
            mm(a("prk", 64, 80), sel(y1(r // 8)[2], r), a(y1(r // 8)[0], 16 * r, 16 * r + 16), r == 0)
        act(a("thr"), a("prk", 64, 80), AF.Identity, a("thc"))
        main("c1", "yrh", 1, CFG["f1"], CFG["m1"])
        name_offsets()
        best("pk", 256, a("j16"), J1)
        if CFG["cs"][5] == "V":
            tt(a("y2n"), ind(a("vm"), a("j16")), a("y1r"), A_.subtract)
        else:
            act(a("y2n"), ind(a("vm"), a("j16")))
        tt(a("dd"), a("rs", 15, 256, 16), a("thr"), A_.add)
        ts(a("jm"), a("ji"), 1, None, A_.bitwise_and)
        tt(a("rdy"), a("jm"), a("dd"), A_.is_gt)
        scan(a("pre"), a("kseg", 0, 16), a("rdy"), A_.mult, A_.add)
        tt(a("rp"), a("rdy"), a("ct"), A_.mult)
        mm(a("prk", 0, 16), a("idp"), a("ct"), True)
        mm(a("prk", 0, 16), a("tri"), a("rdy"))
        mm(a("prk", 0, 16), a("bo"), a("pre"))
        mm(a("prk", 0, 16), a("idn"), a("rp"))
        mm(a("pu", 64, 65), a("bo"), a("pre", 15, 16), True)
        snd, land = "snd%d" % t, "land%d" % t
        ts(a("slot"), a("prk", 0, 16), 255.0, None, A_.add)
        act(a(snd, 0, 1), a("pu", 64, 65), AF.Relu, 64.0, -1.0)
        if CFG["cs"][5] == "V":
            cp(ind(a(snd, 16, 528), a("slot")), a("y2n"))
        else:
            tt(ind(a(snd, 16, 528), a("slot")), a("y2n"), a("y1r"), A_.add)
        dst = T.cores[(rank + 1 + t % (nrank - 1)) % nrank]
        rid, pid = topo.addr(dst, core)
        mask = sum(1 << e for e in topo.engines(core, dst)[:NENG])
        rec("G", lambda t=t, rid=rid, pid=pid, mask=mask: g.remote_dma(
            a("land%d" % t)[0], a("snd%d" % t, 0, 80)[0], T.sem["arr%d" % t], T.sem.sent, pid, rid, mask),
            [], [a(snd, 0, 80)], ("n", 300), "r")
        sent = len(ops) - 1
        scan(a("rm"), a("rw"), a("pk", 0, 256), A_.add, A_.min)
        ts(a("ki"), a("rm", 15, 256, 16), 1 / U18, 1.0, A_.mult, A_.add)
        ts(a("ka"), a("ki"), 1, 15, A_.arith_shift_right, A_.bitwise_and)
        cp(a("k16"), a("ka"))
        mark(a("mg"), a("j16"), "pa", 256, wide="pb" if CFG["two"][2] == "2" else None)
        ya_out(t, 1)
        if t == NS - 1:
            dma("Y", ext(T.ya[:]), a("yab", p=g16), 64)
        tt(a("t1"), ind(a("oh"), a("k16")), a("t2"), A_.mult)
        step = 32 if CFG["pair"] else 16
        for q in range(256 // step - 1, -1, -1):
            tt(ind(a("tab"), a("offn", 2 * q, 2 * q + step // 16)), a("t1", step * q, step * q + step), a("nn", step * q, step * q + step), A_.add)
        if t == NS - 1:
            dma("Y", ext(T.yo[:]), table, 512)
        else:
            act(a("tab", L, L + MIR), a("tab", 0, MIR))
        ops.append(["A", None, [], [(land, 0, 80, 1)], ("a", t, sent), ("n", 0), ("r", 0)])
        if CFG["uscan"]:
            mm(a("pu", 0, 64), a("idp"), a("dg"), True)
            mm(a("pu", 0, 64), a("bw"), a(land, 16, 80))
            scan(a("us"), a("kseg", 0, 64), a("pu", 0, 64), A_.mult, A_.max)
            place(a("us", 15, 64, 16), 0, 4, "lv", t)
        else:
            for r in range(16):
                mm(a("pu", 0, 4), sel("zw", r), a(land, 16 + r, 80, 16), r == 0)
            place(a("pu", 0, 4), 0, 4, "lv", t)
        yrep("yrr", CFG["yrr"], a(land, 16, 80), True, 64)
        ts(a("inv"), a("rslot"), a(land, 0, 1), 16.0, A_.is_le, A_.mult)
        names(a("cr"), table, a("lv"), t)
        if t + 1 < NS:
            u = t + 1
            mm(a("prk", 32, 33), a("e0"), a(land, 0, 1), True)
            ts(a("ai"), a("prk", 32, 33), -1.0 / 2048, -31.5 / 64, A_.mult, A_.add)
            ts(a("ac", u, u + 1), a("ai"), -2048.0, a("prk", 32, 33), A_.mult, A_.subtract)
            for h in range(2):
                b = 16 + 24 * h + 8 * (3 - u)
                ts(a("l0", 8 * h, 8 * h + 8), a("base", b, b + 8), a("ac", u, u + 1), 1.0 / 32, A_.add, A_.mult)
        opened("pr", 64, False)
        mm(a("pr", 0, 64, 16), a("idp"), a("inv"))
        u = 0
        for w in CFG["rch"]:
            c = a("cr", 4 * u, 4 * (u + w))
            tt(a("vmr", 16 + 64 * u, 16 + 64 * (u + w)), ind(a("x"), c), a("yrr", 64 * u, 64 * (u + w)), A_.min)
            act(a("mgr", 16 + 64 * u, 16 + 64 * (u + w)), ind(marks, c))
            for r in range(u, u + w):
                mm(a("pr", 0, 64), sel("zf", r), a("vmr", 16 + 64 * r, 80 + 64 * r))
                mm(a("pr", 0, 64), sel("zm", r), a("mgr", 16 + 64 * r, 80 + 64 * r))
            u += w
        best("pr", 64, a("jr"), JR)
        if t + 1 < NS:
            mark(a("mgr"), a("jr"), "pa", 64, 0, ("adr", "adfr"), CFG["two"][3] == "2")
        if t == NS - 2:
            for b in range(0, W - 2048, 256):
                act(a("ymh", b, b + 256), a("win", PAD + 2048 + b, PAD + 2304 + b))
            dma("Y", ext(T.ym[:, 2048:W]), a("ymh", p=g16), 16)
        if t == NS - 1:
            for b in range(PAD, PAD + 2048, 256):
                act(a("ymb", b, b + 256), a("win", b, b + 256))
            act(a("adr"), ind(a("mgr"), a("jr")))
            distinct("pa", "adr", 64, DY, 0, True)
            for q in range(2):
                cp(ind(a("ymb"), a("offa", 2 * q, 2 * q + 2)), a("ones"))
            dma("Y", ext(T.ym[:, 0:2048]), a("ymb", PAD, PAD + 2048, p=g16), 32)

    emit(g, T, ops, QO)


def price(c, m):
    cyc, gather, scatter, fused, pe, wake, dma, remote, extra = m
    k, n = c
    return {"c": n * cyc, "a": extra + n * cyc, "g": 55 + n * gather * cyc, "f": 55 + n * max(gather, fused) * cyc, "s": 55 + n * scatter * cyc,
            "p": n * pe, "n": n, "d": dma + 7 * n, "r": remote}[k]


def emit(g, T, ops, QO):
    n = len(ops)
    width = {k: v[0] for k, v in _SB.items()}
    width.update({k: 1 for k in _PS})
    writer = {k: np.full(w, -1) for k, w in width.items()}
    reader = {k: [] for k in width}
    semof, deps, soft, nd = [], [], [], 0

    def cols(f):
        return slice(0, 1) if f[0] in _PS else slice(f[1], f[2], f[3])

    member = {k: [] for k in _PS}
    opener = {}
    group, last = {}, {}
    for i, (q, fn, rd, wr, kind, cost, lat) in enumerate(o[:7] for o in ops):
        if kind == "d":
            semof.append("d%d" % nd)
            nd += 1
        else:
            semof.append("sent" if kind == "r" else "s" + q if kind == "c" else "arr%d" % kind[1])
        me = semof[i]
        need, order = set(), set()
        for f in rd:
            need.update(int(w) for w in np.unique(writer[f[0]][cols(f)]) if w >= 0)
            if f[0] in _PS:
                need.update(r for r, m in reader[f[0]] if semof[r] != me)
                need.update(member[f[0]])
        for f in wr:
            if q == "P":
                if ops[i][7]:
                    order.update(member[f[0]])
                    member[f[0]] = []
                    opener[f[0]] = i
                member[f[0]].append(i)
                group[i] = opener[f[0]]
                order.add(group[i])
                order.discard(i)
            else:
                need.update(int(w) for w in np.unique(writer[f[0]][cols(f)]) if w >= 0)
            keep = []
            for r, m in reader[f[0]]:
                if m[cols(f)].any():
                    need.add(r)
                    m[cols(f)] = False
                if m.any():
                    keep.append((r, m))
            reader[f[0]] = keep
        for f in wr:
            writer[f[0]][cols(f)] = i
        for f in rd:
            m = np.zeros(width[f[0]], bool)
            m[cols(f)] = True
            reader[f[0]].append((i, m))
        need.discard(i)
        if fn is None:
            order.add(kind[2])
        if wr and wr[0][0] in ("vm", "mg", "vmr", "mgr") and cost[0] in "fg":
            if (q, wr[0][0]) in last:
                order.add(last[q, wr[0][0]])
            last[q, wr[0][0]] = i
        deps.append(need)
        soft.append(order - need)
    if "seq" not in CFG:
        CFG["seq"] = arrange(ops, deps, named(ops, soft), list(QO) + ["A"])
    seq = CFG["seq"]
    wanted = set()
    for d in deps:
        wanted |= d
    count, value = {}, {}
    for i in seq:
        kind = ops[i][4]
        step = 16 if kind == "d" else (1 if i in wanted else 0) if kind == "c" else NENG
        count[semof[i]] = count.get(semof[i], 0) + step
        value[i] = count[semof[i]]
    final = {group[i]: i for i in seq if i in group}
    known = {q: {} for q in QO}
    after = {}
    for i in seq:
        q, fn, kind = ops[i][0], ops[i][1], ops[i][4]
        if fn is None:
            after[i] = {semof[i]: value[i]}
            continue
        kn = known[q]
        top = {}
        for d in deps[i]:
            if semof[d] not in top or value[d] > value[top[semof[d]]]:
                top[semof[d]] = d
        for d in sorted(top.values(), key=lambda d: -len(after[d])):
            if kn.get(semof[d], 0) < value[d]:
                QO[q].wait_ge(T.sem[semof[d]], value[d])
                for s, v in after[d].items():
                    kn[s] = max(kn.get(s, 0), v)
        ins = fn(final[group[i]] == i) if q == "P" else fn()
        if kind == "d":
            ins.then_inc(T.sem[semof[i]], 16)
        elif kind == "c" and i in wanted:
            ins.then_inc(T.sem[semof[i]], 1)
        done = dict(kn)
        done[semof[i]] = max(done.get(semof[i], 0), value[i])
        after[i] = done
    for s, v in count.items():
        if v and known["G"].get(s, 0) < v:
            g.wait_ge(T.sem[s], v)


def tile(o):
    return "send" if o[4] == "r" else o[3][0][0].rstrip("0123") if o[3][0][0][:2] in ("sn", "yr") else o[3][0][0]


def named(ops, soft):
    soft = [set(s) for s in soft]
    calls, stage = {}, 0
    for i, o in enumerate(ops):
        if o[3] or o[4] == "r":
            calls.setdefault((o[0], stage, tile(o)), []).append(i)
        stage += o[0] == "A"
    for q, lists in CFG["order"].items():
        last = None
        for stage in range(NS + 1):
            names = []
            for name in lists[min(stage, len(lists) - 1)].split():
                name, times = (name + "*1").split("*")[:2]
                names += [name] * int(times)
            for k, name in enumerate(names):
                mine = calls.get((q, stage - name.count("-") + name.count("+"), name.strip("-+")))
                if mine:
                    i = mine.pop(max(0, len(mine) - names[k:].count(name)) if "-" in name else 0)
                    if last is not None:
                        soft[i].add(last)
                    last = i
    return soft


def arrange(ops, deps, soft, queues):
    n = len(ops)
    models = CFG["models"]
    mean = [sum(m[k] for m in models) / len(models) for k in range(len(models[0]))]
    qof = [o[0] for o in ops]

    def tables(m):
        cost = [price(o[5], m) for o in ops]
        lat = [price(o[6], m) for o in ops]
        prv = [[(d, m[5] + lat[d]) for d in deps[i]] + [(d, 0.0) for d in soft[i]] for i in range(n)]
        return cost, lat, prv

    cost, lat, prv = tables(mean)
    nxt = [[] for _ in range(n)]
    for i in range(n):
        for d, w in prv[i]:
            nxt[d].append((i, w))
    left = [len(p) for p in prv]
    flow = [i for i in range(n) if not left[i]]
    for i in flow:
        for j, w in nxt[i]:
            left[j] -= 1
            if not left[j]:
                flow.append(j)
    assert len(flow) == n, [ops[i][0] + str(ops[i][3][:1]) for i in range(n) if left[i]][:12]
    rank_ = [0.0] * n
    for i in reversed(flow):
        rank_[i] = cost[i] + max([lat[i]] + [w + rank_[j] for j, w in nxt[i]])
    each = [tables(m) for m in models]

    def length(seq):
        total = []
        for c, la, pv in each:
            end, free, top = [0.0] * n, {q: 0.0 for q in queues}, 0.0
            for i in seq:
                s = free[qof[i]]
                for d, w in pv[i]:
                    if end[d] + w > s:
                        s = end[d] + w
                end[i] = free[qof[i]] = s + c[i]
                if end[i] + la[i] > top:
                    top = end[i] + la[i]
            total.append(top)
        return total

    label = [o[0] + ":" + "<".join(f[0].rstrip("0123") for f in o[3][:1] + o[2][:1]) for o in ops]
    bias = [CFG["bias"].get(s, 0.0) for s in label]
    if CFG["early"]:
        for i in range(label.index("V:ui<pu")):
            if qof[i] in "VS" and ops[i][4] == "c":
                bias[i] = max(bias[i], rank_[label.index("V:ui<pu")] - CFG["early"] - rank_[i])
    look = [CFG["wait"].get(s, CFG["look"]) for s in label]

    def schedule(prio, prv=prv, nxt=nxt, end=None, fore=True):
        if fore:
            prio = [p + b for p, b in zip(prio, bias)]
        left = [len(p) for p in prv]
        ready = [0.0] * n
        pool = {q: [] for q in queues}
        for i in range(n):
            if not left[i]:
                pool[qof[i]].append(i)
        free = {q: 0.0 for q in pool}
        when = {q: 0.0 if pool[q] else 1e30 for q in pool}
        seq = []
        while len(seq) < n:
            q = min(when, key=when.get)
            now, mine = when[q], pool[q]
            i = max([i for i in mine if ready[i] <= now], key=lambda j: prio[j])
            soon = [j for j in mine if now < ready[j] <= now + look[i] * cost[i] and prio[j] > prio[i]]
            if soon:
                i = max(soon, key=lambda j: prio[j])
                now = ready[i]
            mine.remove(i)
            seq.append(i)
            now = free[q] = now + cost[i]
            if end is not None:
                end[i] = now
            when[q] = max(now, min([ready[j] for j in mine])) if mine else 1e30
            for j, w in nxt[i]:
                if now + w > ready[j]:
                    ready[j] = now + w
                left[j] -= 1
                if not left[j]:
                    k = qof[j]
                    pool[k].append(j)
                    when[k] = min(when[k], max(free[k], ready[j]))
        return seq

    seq = schedule(rank_)
    span = length(seq)
    rng = np.random.RandomState(CFG["seed"])
    prio = np.array(rank_)
    back = rank_
    for _ in range(CFG["turns"]):
        fwd, bwd = [0.0] * n, [0.0] * n
        schedule(back, end=fwd)
        schedule(fwd, nxt, prv, bwd, False)
        back = [CFG["mix"] * b + (1 - CFG["mix"]) * o for b, o in zip(bwd, back)]
        s2 = schedule(back)
        l2 = length(s2)
        if sum(l2) < sum(span):
            seq, span, prio = s2, l2, np.array(back)
    kinds, seen, stage = {}, {}, 0
    kind = []
    for o in ops:
        key = (o[0], stage > 0) + tuple(f[0].rstrip("0123") for f in o[3][:1] + o[2][:1])
        seen[key] = seen.get(key, 0) + 1
        kind.append(kinds.setdefault(key + (seen[key] // (CFG["pg"] if o[0] == "P" else 1),), len(kinds)))
        if o[0] == "A":
            seen, stage = {}, stage + 1
    kind = np.array(kind)
    shift = np.zeros(len(kinds))
    for _ in range(CFG["passes"]):
        trial = shift + rng.normal(0.0, CFG["shift"], len(kinds)) * (rng.rand(len(kinds)) < CFG["share"])
        s2 = schedule((prio + trial[kind]).tolist())
        l2 = length(s2)
        if sum(l2) < sum(span):
            seq, span, shift = s2, l2, trial
    seq = settle(seq, qof, kind.tolist(), [tables(m) for m in CFG["settle"]] or [(cost, lat, prv)], rng)
    seq = polish(seq, qof, cost, lat, prv, nxt, rng)
    CFG["span"], CFG["path"] = length(seq), max(rank_)
    return seq


def settle(seq, qof, kind, each, rng):
    n = len(seq)
    if not CFG["tries"]:
        return seq
    before = [[d for d, w in p] for p in each[0][2]]

    def run(seq, tab):
        cost, lat, prv = tab
        end, why, free, last = [0.0] * n, [0] * n, {}, {}
        for i in seq:
            q = qof[i]
            s, y = free.get(q, 0.0), ~last.get(q, n)
            for d, w in prv[i]:
                if end[d] + w > s:
                    s, y = end[d] + w, d
            end[i] = free[q] = s + cost[i]
            why[i] = y
            last[q] = i
        i = max(seq[-40:], key=lambda i: end[i] + lat[i])
        return end[i] + lat[i], i, end, why

    def order(place):
        key = [0.0] * n
        for i in range(n):
            k = base[i] + place[kind[i]]
            for d in before[i]:
                if key[d] >= k:
                    k = key[d] + 0.001
            key[i] = k
        return sorted(range(n), key=lambda i: key[i]), key

    def judge(seq):
        total, pairs = 0.0, []
        for tab in each:
            top, i, end, why = run(seq, tab)
            total += top
            while i != n:
                y = why[i]
                if y < 0:
                    y = ~y
                    if y != n:
                        pairs.append((y, i))
                i = y
        return total / len(each), pairs

    top, i, end, why = run(seq, each[0])
    base, place, at, stage = [0.0] * n, {}, 0.0, 0
    for i in range(n):
        base[i] = at
        if stage <= CFG["model"] or kind[i] not in place:
            place[kind[i]] = end[i] - each[0][0][i] - at
        if qof[i] == "A":
            at, stage = end[i], stage + 1
    first = judge(seq)[0]
    now, key = order(place)
    top, pairs = judge(now)
    best = (top, now)
    dbg = top
    for step in range(CFG["tries"]):
        p, i = pairs[rng.randint(len(pairs))]
        trial = dict(place)
        far = CFG["far"] * rng.rand() ** 2
        if rng.rand() < 0.5:
            goal, todo = key[p] - far - 0.01, [i]
            while todo:
                j = todo.pop()
                trial[kind[j]] = min(trial[kind[j]], goal - base[j])
                todo += [d for d in before[j] if key[d] > goal and base[d] + trial[kind[d]] > goal]
        else:
            trial[kind[p]] = key[i] + far + 0.01 - base[p]
        s2, k2 = order(trial)
        t2, p2 = judge(s2)
        if t2 <= top + CFG["warm"] * (1 - step / CFG["tries"]) * rng.rand() ** 2:
            place, key, top, pairs = trial, k2, t2, p2
            if t2 < best[0]:
                best = (t2, s2)
    CFG["dbg"] = (first, dbg, best[0], top)
    return best[1] if best[0] < first else seq


def polish(seq, qof, cost, lat, prv, nxt, rng):
    n = len(seq)

    def run(seq, at, end, why):
        free, last = {}, {}
        for i in seq[:at]:
            last[qof[i]] = i
        for q, i in last.items():
            free[q] = end[i]
        for i in seq[at:]:
            q = qof[i]
            s, y = free.get(q, 0.0), ~last.get(q, n)
            for d, w in prv[i]:
                if end[d] + w > s:
                    s, y = end[d] + w, d
            end[i] = free[q] = s + cost[i]
            why[i] = y
            last[q] = i
        i = max(seq[-40:], key=lambda i: end[i] + lat[i])
        return end[i] + lat[i], i

    def chain(i, why):
        pairs = []
        while i != n:
            y = why[i]
            if y < 0:
                y = ~y
                if y != n:
                    pairs.append((y, i))
            i = y
        return pairs

    end, why = [0.0] * n, [0] * n
    top, tail = run(seq, 0, end, why)
    pairs = chain(tail, why)
    for step in range(CFG["moves"]):
        p, i = pairs[rng.randint(len(pairs))]
        pos = {x: k for k, x in enumerate(seq)}
        a, b = pos[p], pos[i]
        if rng.rand() < 0.5:
            more = rng.randint(4)
            while more and a > 0:
                a -= 1
                more -= qof[seq[a]] == qof[i]
            move, todo = {i}, [i]
            while todo:
                for d, w in prv[todo.pop()]:
                    if pos[d] >= a and d not in move:
                        move.add(d)
                        todo.append(d)
            if p in move:
                continue
            part = seq[a:b + 1]
            new = seq[:a] + [x for x in part if x in move] + [x for x in part if x not in move] + seq[b + 1:]
        else:
            more = rng.randint(4)
            while more and b < n - 1:
                b += 1
                more -= qof[seq[b]] == qof[i]
            move, todo = {p}, [p]
            while todo:
                for d, w in nxt[todo.pop()]:
                    if pos[d] <= b and d not in move:
                        move.add(d)
                        todo.append(d)
            if i in move:
                continue
            part = seq[a:b + 1]
            new = seq[:a] + [x for x in part if x not in move] + [x for x in part if x in move] + seq[b + 1:]
        e2, w2 = end[:], why[:]
        t2, l2 = run(new, a, e2, w2)
        if t2 <= top + CFG["heat"] * (1 - step / CFG["moves"]) * rng.rand() ** 3:
            seq, end, why, top = new, e2, w2, t2
            pairs = chain(l2, why)
    return seq
